import numpy as np, ml_dtypes
CORES = [10,34,74,98]
N = 4
import mx_ref
BF = ml_dtypes.bfloat16
def gcols(t, e):
    v = np.concatenate([t.reshape(8, 16, -1, 4), np.zeros((8, 16, 1, 4), BF)], axis=2)
    return np.ascontiguousarray(np.stack([v[g][:, e[g]] for g in range(8)])).reshape(128, -1)
def tile(rs):
    return np.stack(rs, axis=2).reshape(128, -1).astype(BF)
def cut(t, i, w=512):
    return t[:, w * i:w * i + w]
def pick(q, e):
    c = np.concatenate([q[0].reshape(128, -1, 4), np.zeros((128, 1, 4), np.uint8)], axis=1); s = np.concatenate([q[1], np.ones((16, 1), np.uint8)], axis=1)
    return (np.ascontiguousarray(c[:, e].reshape(128, -1)), np.ascontiguousarray(s[:, e]))
def join(*qs):
    return (np.concatenate([q[0] for q in qs], axis=1), np.concatenate([q[1] for q in qs], axis=1))
def put(q, e, v):
    c, s = q[0].reshape(128, -1, 4).copy(), q[1].copy(); c[:, e] = v[0].reshape(128, -1, 4); s[:, e] = v[1]
    return (c.reshape(128, -1), s)
def pk(c, s):
    return (np.ascontiguousarray(c), mx_ref.live(s))
def emit(q):
    return q[0], q[1]
def packed(v, rng):
    q = [mx_ref.quantize(np.ascontiguousarray(v[r])) for r in range(N)]
    return np.stack([a for a, b in q]), np.stack([mx_ref.plane(b, rng) for a, b in q])
def values_of_codes():
    e, c = np.zeros((128, 128, 4), np.float32), np.zeros((128, 2, 4), np.uint8)
    e[np.arange(128), np.arange(128), 0] = 1
    c[:127, :, 0] = np.arange(256).reshape(2, 128).T[:127]
    return mx_ref.matmul(mx_ref.quantize(e.reshape(128, 512).astype(BF)), (c.reshape(128, 8), np.full((16, 2), 127, np.uint8))).T.reshape(-1).astype(np.float64)
CODE_VALUE, SCALE_VALUE = values_of_codes(), 2.0 ** (np.arange(256) - 127.0)
def decode(q):
    return (CODE_VALUE[q[0]].reshape(16, 8, -1, 4) * SCALE_VALUE[q[1]][:, None, :, None] + 0.0).reshape(128, -1).astype(np.float32)
def f(rng, *shape):
    return mx_ref.flush((rng.standard_normal(shape, dtype=np.float32) * np.exp2(rng.integers(-2, 3, shape[:-1] + (1,)))).astype(BF))
def wide(rng, *shape, cols=0):
    v = rng.standard_normal(shape, dtype=np.float32) * np.exp2(rng.integers(-12, 13, shape)).astype(np.float32)
    if cols: v *= np.repeat(np.exp2(rng.integers(-cols, cols + 1, shape[:-2] + (1, shape[-1] // 4))) * (rng.random(shape[:-2] + (1, shape[-1] // 4)) > 0.0625), 4, axis=-1).astype(np.float32)
    return mx_ref.flush(v.astype(BF))
C, K, A, P, L, R = 512, 7, 128, 224, 96, 3
DECIDE = (16 * np.arange(8)[:, None] + np.arange(8)).reshape(-1)
def address(s):
    a = np.zeros((8, s.shape[1]), np.int64)
    for i in range(K): a |= (s[i::16] > 0).astype(np.int64) << i
    return a
def match(ad):
    e = np.argsort(ad, kind="stable")
    e = e[ad[e] >= 0]
    s = ad[e]
    k = (np.arange(len(e)) - np.searchsorted(s, s)) % 2
    two = np.flatnonzero(k)
    two = two[np.argsort(e[two])][:P]
    pair, wait = np.full((2, P), -1), np.full(A, -1)
    pair[0, :len(two)] = e[two - 1]
    pair[1, :len(two)] = e[two]
    last = np.flatnonzero((k == 0) & (np.append(s, -1)[1:] != s))
    wait[s[last]] = e[last]
    return pair, wait
def big(v):
    v = v.astype(np.float32)
    v[np.abs(v) < np.float32(2.0 ** -16)] = 0
    return v.astype(BF)
def numbers_of(rng):
    return {"x": big(f(rng, N, 128, 4 * C)), "u": np.array(f(rng, N, 128, 512)), "v": np.array(f(rng, N, 128, 512))}
def weights(rng, w):
    c, p = packed(w, rng)
    return {"wc": c, "ws": p}
def setup_inputs(rng):
    return {**numbers_of(rng), **weights(rng, big(f(rng, N, 128, 2048)))}
def setup_inputs_one(rng):
    d = numbers_of(rng)
    e = rng.permutation(N) % 4
    x = d["x"].reshape(N, 8, 16, C, 4)
    for r in range(N):
        k = rng.permutation(C) % 3
        if e[r] == 0: k = np.zeros(C, int)
        if e[r] == 1: k = np.full(C, 2)
        a = x[r][:, :8, :3].copy()
        a[:, :, 2] = 0
        x[r][:, :8] = a[:, :, k]
    u = d["u"].reshape(N, 8, 16, 128, 4)
    u[:, :, 8:, DECIDE] = 0
    w = big(f(rng, N, 128, 2048)).reshape(N, 8, 16, 4, 8, 16, 4)
    w[:, :, 8:, :, :, :8] = 0
    return {"x": x.reshape(N, 128, 4 * C), "u": u.reshape(N, 128, 512), "v": d["v"], **weights(rng, w.reshape(N, 128, 2048))}
def some(rng, k):
    return np.bincount(rng.integers(0, A, k), minlength=A)
def setup_inputs_caps(rng):
    d = numbers_of(rng)
    x = d["x"].reshape(N, 8, 16, C, 4)
    u = d["u"].reshape(N, 128, 128, 4)
    z = rng.permutation(N) % 4
    size = np.exp2(np.array([-28.0, -12.0, 0.0, 28.0])[z])
    one = np.exp2(np.array([-30.0, 0.0, 0.0, 30.0])[z]).astype(np.float32)
    u[:, :, DECIDE] = 0
    u[:, DECIDE, DECIDE, 0] = one.astype(BF)[:, None]
    u[:, DECIDE, DECIDE, 1] = (-one).astype(BF)[:, None]
    lead = np.array([[[0, 0], [1, -1], [-2, 1]], [[1, 1], [2, -1], [-1, 2]]])
    o = rng.permutation(8)
    g1, g2 = int(o[6]), int(o[7])
    turn = int(rng.integers(4))
    few = (C - A) // 2
    come = np.bincount(rng.permutation(A)[np.arange(L) % A], minlength=A)
    own = (come + 1) % 2
    own = own + 2 * some(rng, (few - np.sum(own)) // 2)
    made = (come + 1) % 2
    made[rng.permutation(A)[:((few + L) // 2 - np.sum(made)) // 2]] += 2
    early = np.bincount(rng.permutation(np.repeat(np.flatnonzero(made), 2))[:L], minlength=A)
    none, half = 0 * come, come // 2
    plan = {g1: [(own, none), (come + some(rng, P - L), come)] * 2,
            g2: [(2 * made - early, none), (early + some(rng, P - L), early), (come + 2 * some(rng, (few - L) // 2), none), (half + some(rng, P - np.sum(half)), half)]}
    for r in range(N):
        a, b = np.zeros(8, int), np.zeros(8, int)
        a[o[:6]] = rng.permutation(6) % 5
        b[o[:6]] = rng.permutation(6) % 5
        part = (r ^ turn) & 3
        for g in range(8):
            if g in plan:
                i = np.repeat(np.arange(A), plan[g][part][0])
                i = i // 2 + i % 2 * (A // 2)
                odd = C - 2 * len(i)
            else:
                odd = [C - 2 * P, C - 2 * P - 2, C - 2 * P + 2, 0, A][a[g]]
                i = rng.integers(0, A, (C - odd) // 2)
            e = rng.permutation(np.concatenate([rng.permutation(A)[:odd], i, i]))
            pair, wait = match(e)
            pair = pair[:, pair[0] >= 0]
            n = pair.shape[1]
            if g in plan:
                to = 2 * e[pair[0]] % A + 2 * e[pair[0]] // A
                j = rng.permutation(n)
                j = j[np.argsort(to[j], kind="stable")]
                go = np.zeros(n, bool)
                go[j] = np.arange(n) - np.searchsorted(to[j], to[j]) < plan[g][part][1][to[j]]
            else:
                go = rng.permutation(n) < [L, L + 1, L - 1, 0, n][b[g]]
            h = lead[go.astype(int), rng.integers(0, 3, n)]
            mark = np.zeros((8, C))
            mark[:K] = ((e >> np.arange(K)[:, None]) & 1) * 2 - 1
            if z[r] == 0 and g != g2: mark[:K] *= 0.25
            mark[7, pair[0]] = h[:, 0]
            mark[7, pair[1]] = h[:, 1]
            if g == g2:
                mark[7] = -8 if part == 0 else -1
                mark[7, pair[:, go]] = 4
                if part == 2: mark[7, wait[come > 0]] = 4
            m = np.stack([np.maximum(mark, 0), np.maximum(-mark, 0) + 0.0, 0 * mark + 0.0, 0 * mark + 0.0], axis=2)
            x[r, g, :8] = (np.abs(m) * (1.0 if g == g2 else size[r])).astype(np.float32).astype(BF)
    w = big(f(rng, N, 128, 2048)).reshape(N, 128, 4, 128, 4)
    w[:, DECIDE] = 0
    w[:, :, :, DECIDE] = 0
    to = DECIDE - DECIDE % 16 + np.where(DECIDE % 16 < K, (DECIDE % 16 + 1) % K, DECIDE % 16)
    less = (z == 0)[:, None] & ((DECIDE % 16 == 7) & (DECIDE // 16 != g2))[None, :]
    for b in range(4): w[:, DECIDE, b, to, b] = np.where(less, 0.0625, 32.0).astype(np.float32).astype(BF)
    return {"x": x.reshape(N, 128, 4 * C), "u": u.reshape(N, 128, 512), "v": d["v"], **weights(rng, w.reshape(N, 128, 2048))}
def setup_inputs_huge(rng):
    d = numbers_of(rng)
    o = rng.permutation(N)
    x = 2.0 ** 30 * (0.5 + 0.5 * rng.random((N, 128, 4 * C))) * (rng.random((N, 128, 4 * C)) < 0.5)
    q = int(rng.integers(8))
    x[o % 2 == 1, 16 * q:16 * q + 16] = 0
    c = np.argsort(rng.random((N, 512, 64)), axis=1) % 2 * 2.0 - 1.0
    c = c.reshape(N, 128, 4, 64).transpose(0, 1, 3, 2).copy()
    for r in range(N):
        s = rng.permutation(8) % 2 * 2.0 - 1.0
        if o[r] < 2: s = np.full(8, 2.0 * o[r] - 1.0)
        c[r][:, 7::8] = s[None, :, None]
        k = 8 * np.arange(8) + rng.integers(0, K, 8)
        c[r][:, k] = (rng.permutation(8) % 2 * 2.0 - 1.0)[None, :, None]
    u = d["u"].reshape(N, 128, 128, 4)
    u[:, :, DECIDE] = (2.0 ** 30 * (0.75 + 0.25 * rng.random((N, 128, 64, 4))) * c).astype(np.float32).astype(BF)
    w = np.zeros((N, 128, 4, 128, 4), np.float32)
    i = np.arange(128)
    for b in range(4): w[:, i, b, i, b] = 32
    return {"x": x.astype(np.float32).astype(BF), "u": u.reshape(N, 128, 512), "v": d["v"], **weights(rng, w.reshape(N, 128, 2048).astype(BF))}
def setup_inputs_spread(rng):
    d = setup_inputs(rng)
    d["x"] = big(wide(rng, N, 128, 4 * C, cols=6))
    return d
def check_inputs(d):
    b = []
    for k in ("x", "u", "v"):
        a = np.abs(d[k].astype(np.float32))
        if not (np.isfinite(a).all() and ((a == 0) | (a >= 2.0 ** -30) & (a <= 2.0 ** 30)).all()): b.append("a value of " + k)
    return b
def reference(x, u, v, wc, ws):
    qu = [mx_ref.quantize(u[r]) for r in range(N)]
    lay = [pk(wc[r], ws[r]) for r in range(N)]
    pool = [np.concatenate([np.zeros((128, 4 * A), BF), x[r]], axis=1) for r in range(N)]
    ad = [np.concatenate([np.full((8, A), -1), address(mx_ref.matmul(qu[r], mx_ref.quantize(x[r])))], axis=1) for r in range(N)]
    y, occ = np.zeros((N, 128, A + P), np.float32), np.zeros((N, 8, A + P), np.float32)
    oc, osc = np.zeros((N, 128, 4 * (A + P)), np.uint8), np.zeros((N, 16, A + P), np.uint8)
    for t in range(R):
        kept, slots, sent, dest = [], [], [], []
        for r in range(N):
            found = [match(a) for a in ad[r]]
            pair, wait = np.stack([e[0] for e in found]), np.stack([e[1] for e in found])
            have = pair[:, 0] >= 0
            one, two = gcols(pool[r], pair[:, 0]), gcols(pool[r], pair[:, 1])
            q = mx_ref.quantize(((one.astype(np.float32) + two.astype(np.float32)) * np.float32(0.5)).astype(BF))
            h = tile([np.maximum(mx_ref.matmul(pick(lay[r], np.arange(128 * b, 128 * b + 128)), q), np.float32(0.0)) * np.float32(0.03125) for b in range(4)])
            store = gcols(pool[r], wait)
            if t == R - 1:
                q = mx_ref.quantize(np.concatenate([store, gcols(h, np.where(have, np.arange(P), -1))], axis=1))
                y[r] = mx_ref.matmul(mx_ref.quantize(v[r]), q)
                occ[r] = np.concatenate([wait >= 0, have], axis=1)
                oc[r], osc[r] = emit(q)
                continue
            s = mx_ref.matmul(qu[r], mx_ref.quantize(h))
            to = np.where(have, address(s), -1)
            go, at = np.full((8, L), -1), np.full((8, L), -1)
            for g in range(8):
                i = np.flatnonzero(have[g] & (s[16 * g + 7] > 0))[:L]
                go[g, :len(i)] = i
                at[g, :len(i)] = to[g, i]
                to[g, i] = -1
            sent.append(mx_ref.quantize(gcols(h, go)))
            dest.append(at)
            kept.append(np.concatenate([store, h], axis=1))
            slots.append(np.concatenate([np.where(wait >= 0, np.arange(A), -1), to], axis=1))
        if t < R - 1:
            came = decode(join(*sent)).astype(BF)
            for r in range(N):
                e = r ^ (1 << t)
                pool[r] = np.concatenate([kept[r], cut(came, e, 4 * L)], axis=1)
                ad[r] = np.concatenate([slots[r], dest[e]], axis=1)
    return {"y": y, "occ": occ, "oc": oc, "osc": osc}

@@ -1,0 +1,409 @@
+import math
+from concourse.mybir import dt, AluOpType as OP, ActivationFunctionType as AF
+
+C, A, P, L, R = 512, 128, 224, 96, 3
+NT = [C, 2 * P, 2 * P]
+Q0 = [0, C, C + 2 * P]
+Z0 = 1
+NQ = C + 4 * P
+ZE = Z0 + NQ
+PW = ZE + 15
+BIG = 16777216
+FIRST, OWN, FAR = (0, 7), (0, 7), ()
+GAP0, GAP1 = -3, 2
+H16 = "float16"
+CD, U8, BF, F32, I32, U16 = "float8_e4m3fn_x4", "uint8", "bfloat16", "float32", "int32", "uint16"
+
+SCRATCH = {}
+
+
+def _sb(name, cols, dtype):
+    SCRATCH[name] = ("sbuf", [128, cols], dtype)
+
+
+for _n, _c, _d in [
+    ("xin", 4 * C, BF), ("qx", C, CD), ("sx", C, U8), ("uin", 512, BF), ("qu", 128, CD), ("su", 128, U8),
+    ("vin", 512, BF), ("qv", 128, CD), ("sv", 128, U8), ("qw", 512, CD), ("sw", 512, U8),
+    ("pool", 4 * PW, BF), ("gb", C + 16, H16), ("vv", C + 32, H16),
+    ("pcol", 1, I32), ("ci", 4, I32), ("cf", 4, F32), ("cx", 8, F32), ("wexp", 2, BF),
+    ("d64", 64, BF), ("pat", 192, BF), ("i16", 16, F32), ("gm", 16, F32), ("c4", 128, BF), ("raw", 32, F32),
+    ("cb", 512, BF), ("ca", 512, BF), ("gro", 512, BF), ("qc", 256, CD), ("sc", 256, U8),
+    ("eb", 516, BF), ("et", 2048, BF), ("qe", 512, CD), ("se", 512, U8),
+    ("msk", 128, BF), ("c64", 128, BF), ("r64", 128, F32), ("sgt", 624, BF), ("st", 8 * NQ, F32), ("sg16", 16, BF),
+    ("tab8", 32, I32), ("dump", 32, F32), ("tw0", 16, F32), ("smr", 544, BF), ("sm", 544, BF),
+    ("rmp", NQ, F32), ("tbx", NQ, F32), ("t01", 16, F32),
+    ("tt", 4 * (A + P), BF), ("qt", A + P, CD), ("sct", A + P, U8), ("ysb", A + P, F32), ("ocb", A + P, F32),
+    ("hm", 4 * P, F32), ("wa", 8, F32), ("wo", 16, U16), ("hf", 16, U16),
+]:
+    _sb(_n, _c, _d)
+WID = {"bt": (512, BF), "qb": (128, CD), "sb": (128, U8), "ii": (128, F32), "vl": (128, F32), "sl": (128, F32),
+       "wi": (160, I32), "au": (64, U16), "sig": (8 * C, BF), "xx": (C, F32),
+       "ga": (C, H16), "tr": (1088, H16), "ss": (1088, H16),
+       "vk": (80, F32), "de": (32, U16), "xs": (848, F32), "tx": (480, F32), "sx2": (480, F32),
+       "vi": (64, I32), "ofs": (28, U16), "tmp": (4 * P, BF), "bb": (4 * P, BF), "qbb": (P, CD), "sbb": (P, U8),
+       "tw": (32, F32)}
+for _n, (_c, _d) in WID.items():
+    _sb(_n, R * _c, _d)
+for _t in range(2):
+    for _n, _c, _d in [("hh", 4 * P, BF), ("qh", P, CD), ("sh", P, U8), ("lq", P, CD), ("ls", P, U8),
+                       ("msg", 28, U16), ("ll", 28, U16)]:
+        _sb("%s%d" % (_n, _t), _c, _d)
+for _n, _c in [("ps", 512), ("pa", 512), ("pb", 512), ("pw", 2048), ("py", 512)]:
+    SCRATCH[_n] = ("psum", [128, _c], F32)
+
+SEMAPHORES = ["cv", "cs", "cp", "cg", "du", "dxa", "dxb", "dw", "dv", "do", "sent", "ac0", "ac1", "al0", "al1"]
+
+
+def rank_program(g, core, T, topo):
+    rank = T.rank_of(core)
+    if rank is None:
+        return
+    que = {"v": g.vector, "s": g.scalar, "p": g.tensor, "g": g, "y": g.sync}
+    cnt = {}
+    seen = {}
+
+    def wait(q, deps):
+        need = {}
+        for d in deps:
+            if d is not None and d[1] > need.get(d[0], 0):
+                need[d[0]] = d[1]
+        for s, n in need.items():
+            if n > seen.get((q, s), 0):
+                que[q].wait_ge(T.sem[s], n)
+                seen[(q, s)] = n
+
+    def done(ins, s, n):
+        ins.then_inc(T.sem[s], n)
+        cnt[s] = cnt.get(s, 0) + n
+        return (s, cnt[s])
+
+    def ts(out, in0, s1, s2, o0, o1, deps):
+        wait("v", deps)
+        if o1 is None:
+            return done(g.vector.tensor_scalar(out, in0, s1, None, o0), "cv", 1)
+        return done(g.vector.tensor_scalar(out, in0, s1, s2, o0, o1), "cv", 1)
+
+    def tt(out, a, b, o, deps):
+        wait("v", deps)
+        return done(g.vector.tensor_tensor(out, a, b, o), "cv", 1)
+
+    def cp(out, a, deps):
+        wait("v", deps)
+        return done(g.vector.tensor_copy(out, a), "cv", 1)
+
+    def ms(out, c):
+        return done(g.vector.memset(out, c), "cv", 1)
+
+    def scan(out, d0, d1, init, o0, o1, deps):
+        wait("v", deps)
+        return done(g.vector.tensor_tensor_scan(out, d0, d1, init, o0, o1), "cv", 1)
+
+    def trp(out, a, deps):
+        wait("v", deps)
+        return done(g.vector.transpose(out, a), "cv", 1)
+
+    def qz(q, s, a, deps):
+        wait("v", deps)
+        return done(g.vector.quantize_mx(q, s, a), "cv", 1)
+
+    def act(out, a, f, deps, **kw):
+        wait("s", deps)
+        return done(g.scalar.activation(out, a, f, **kw), "cs", 1)
+
+    def mm(out, q1, s1, q2, s2, deps):
+        wait("p", deps)
+        return done(g.tensor.matmul_mx(out, q1, s1, q2, s2, True, True), "cp", 1)
+
+    def iota(out, pat, base, ch, flag=True):
+        if flag:
+            return done(g.iota(out, pat, base, ch, allow_small_or_imprecise_dtypes=True), "cg", 1)
+        return done(g.iota(out, pat, base, ch), "cg", 1)
+
+    def dma(q, out, a, s, deps):
+        wait(q, deps)
+        return done(que[q].dma_start(out, a), s, 16)
+
+    def V(name, t, a, b, step=1):
+        w = 8 * Q0[t] if name == "st" else WID[name][0] * t
+        return T[name][:, w + a:w + b:step] if step != 1 else T[name][:, w + a:w + b]
+
+    def plane(e, a, b):
+        return T.pool[:, PW * e + a:PW * e + b]
+
+    du = dma("y", T.uin[:], T.u[:], "du", [])
+    dxa = dma("y", T.xin[:, 0:2 * C], T.x[:, 0:2 * C], "dxa", [])
+    dxb = dma("s", T.xin[:, 2 * C:4 * C], T.x[:, 2 * C:4 * C], "dxb", [])
+    dma("y", T.qw[:].bitcast(dt.uint8), T.wc[:], "dw", [dxa, dxb])
+    dw = dma("y", T.sw[:], T.ws[:], "dw", [])
+    dv = dma("y", T.vin[:], T.v[:], "dv", [])
+
+    g_p = iota(T.pcol[:], [[0, 1]], 0, 1, False)
+    g_d = iota(T.d64[:], [[0, 4], [-1, 4], [1, 4]], 0, 0)
+    g_i = iota(T.i16[:], [[1, 16]], 0, 0)
+    g_c = iota(T.c4[:], [[0, 32], [1, 4]], 0, 0)
+    g_r = iota(T.raw[:], [[16, 32]], 0, 0)
+    g_r0 = iota(T.rmp[:, 0:C], [[8192, C]], 8192 * Z0 - BIG, 0)
+    g_sm = iota(T.smr[:], [[0, 17], [1, 2], [0, 16]], 0, 0)
+    g_x0 = iota(T.tbx[:, 0:C], [[8191, C]], 8191 * Z0 - BIG, 0)
+    g_g = iota(T.gro[:], [[1, 8], [0, 64]], 0, 0)
+    g_e = iota(T.eb[:], [[0, 516]], 1, 0)
+    wait("g", [g_e])
+    g_e = done(g.affine_select(T.eb[:], T.eb[:], [[1, 516]], OP.is_equal, 0.0, -3, -4), "cg", 1)
+    g_r1 = iota(T.rmp[:, C:NQ], [[8192, NQ - C]], 8192 * (Z0 + C) - BIG, 0)
+    g_x1 = iota(T.tbx[:, C:NQ], [[8191, NQ - C]], 8191 * (Z0 + C) - BIG, 0)
+
+    k_sg = ms(T.sgt[:], 1.0)
+    k_c = ms(T.c64[:], 65536.0)
+    ts(T.ci[:, 0:1], T.pcol[:], 15, None, OP.bitwise_and, None, [g_p])
+    ts(T.ci[:, 1:2], T.pcol[:], 4, 1, OP.arith_shift_right, OP.bitwise_and, [])
+    ts(T.ci[:, 2:3], T.pcol[:], 4, None, OP.arith_shift_right, None, [])
+    k = ts(T.ci[:, 3:4], T.pcol[:], 2, 3, OP.arith_shift_right, OP.bitwise_and, [])
+    k_cf = cp(T.cf[:], T.ci[:], [k])
+    fi, fh, fg, fq = (T.cf[:, j:j + 1] for j in range(4))
+    w0, vp, w1, hb, q1 = (T.cx[:, j:j + 1] for j in range(5))
+    s_w = act(T.wexp[:, 0:1], fi, AF.Exp, [k_cf], scale=math.log(2.0))
+    k_vp = ts(vp, fi, 7.0, 256.0, OP.is_equal, OP.mult, [k_cf])
+    k_gm = ts(T.gm[:], T.i16[:], fg, None, OP.is_equal, None, [g_i])
+    k = ts(T.sg16[:], T.i16[:], fi, 2.0, OP.not_equal, OP.mult, [])
+    k_l = ts(T.pat[:, 64:128], T.d64[:], 0.0, vp, OP.is_gt, OP.mult, [g_d, k_vp])
+    k_sg = ts(T.sgt[:, 240:256], T.sg16[:], -1.0, None, OP.add, None, [k, k_sg])
+    k_m = ts(T.msk[:], T.c4[:], fq, 33554432.0, OP.is_equal, OP.mult, [g_c])
+    k_r = scan(T.r64[:], T.c64[:], T.c64[:], 0.0, OP.add, OP.max, [k_c])
+    k_t8 = ts(T.tab8[:], T.raw[:], fi, 8.0, OP.add, OP.mult, [g_r])
+    k_du = ts(T.dump[:], T.raw[:], fi, 320.0, OP.add, OP.add, [])
+    k_hb = ts(hb, fh, -1.0, None, OP.add, None, [])
+    k = ts(q1, fq, 1.0, 65536.0, OP.add, OP.mult, [])
+    k_z = [ms(T.pool[:, 0:4 * PW:PW], 0.0), ms(T.pool[:, ZE:4 * PW:PW], 0.0)]
+    k_tw = ts(T.tw0[:], T.raw[:, 0:16], 16384.0, q1, OP.mult, OP.add, [k])
+    fills = [ms(T.gb[:, 0:2], 0.0), ms(T.vv[:], 0.0)]
+    k = ts(w0, fi, 7.0, T.wexp[:, 0:1], OP.is_lt, OP.mult, [s_w])
+    k = ts(w1, vp, -128.0, w0, OP.mult, OP.add, [k])
+    k = ts(T.pat[:, 0:64], T.d64[:], 0.0, w1, OP.is_equal, OP.mult, [k])
+    k_pat = tt(T.pat[:, 128:192], T.pat[:, 0:64], T.pat[:, 64:128], OP.subtract, [k, k_l])
+    kb = []
+    for j in range(8):
+        if j % 2:
+            kb.append(act(T.cb[:, 64 * j:64 * j + 64], T.pat[:, 128:192], AF.Copy, [k_pat, k_gm], scale=T.gm[:, j:j + 1]))
+        else:
+            kb.append(ts(T.cb[:, 64 * j:64 * j + 64], T.pat[:, 128:192], T.gm[:, j:j + 1], None, OP.mult, None, [k_pat, k_gm]))
+    k_qu = qz(T.qu[:], T.su[:], T.uin[:], [du])
+    k_qb = qz(T.qc[:, 0:128], T.sc[:, 0:128], T.cb[:], kb)
+
+    def signs_and_scans(t, pos, n, offs, deps, init, ideps, mine, w0):
+        def win(m):
+            return T.sgt[:, w0 - 16 * m:w0 + 384 - 16 * m].indirect(offs)
+
+        def sg(m):
+            return V("sig", t, 8 * pos + m * n, 8 * pos + (m + 1) * n)
+        tok = {}
+        for m in range(8):
+            if m not in mine:
+                tok[m] = act(sg(m), win(m), AF.Copy, deps + [k_sg])
+
+        def one(m):
+            if m not in tok:
+                tok[m] = cp(sg(m), win(m), deps + [k_sg])
+            return scan(V("st", t, 8 * pos + m, 8 * (pos + n), 8), T.rmp[:, Q0[t] + pos:Q0[t] + pos + n], sg(m),
+                        init(m), OP.max, OP.mult, [tok[m]] + ideps)
+        return [(one, m) for m in ((0, 1, 2, 3, 7, 4, 5, 6) if 7 in mine else range(8))]
+
+    def run(jobs, k=99):
+        last = None
+        for _ in range(min(k, len(jobs))):
+            f, a = jobs.pop(0)
+            last = f(a)
+        return last
+
+    def fold(src, tr, ss, out, n, op, deps, gap):
+        trp(tr(0, n), src(16, 16 + n), deps)
+        k = trp(tr(n, 2 * n + 32), src(0, n + 32), [])
+        gap(0)
+        k = scan(ss(0, 2 * n + 32, 1), tr(0, 2 * n + 32), T.sm[:, 0:2 * n + 32], 0.0, op, OP.mult, [k, s_sm])
+        gap(1)
+        tt(out(0, n // 16, 2), ss(15, n, 32), ss(n + 31, 2 * n, 32), OP.add, [k])
+        return tt(out(1, n // 16, 2), ss(n + 47, 2 * n + 32, 32), ss(31, n, 32), OP.add, [])
+
+    def number(t, pos, n, lead, offs, deps, before, jobs, first):
+        def gap(j):
+            if j >= first:
+                run(jobs, 1)
+        k = tt(V("xx", t, pos, pos + n), V("st", t, -lead, 8 * (pos + n)).indirect(offs),
+               T.tbx[:, Q0[t] + pos:Q0[t] + pos + n], OP.subtract, deps)
+        init = 64.0
+        gap(-4)
+        if pos:
+            init = V("vk", t, 64, 65)
+            cp(init, T.vv[:, 15 + pos:16 + pos], [before])
+        k = ts(V("ga", t, pos, pos + n), V("xx", t, pos, pos + n), 0.0, -1024.0, OP.is_lt, OP.mult, [k])
+        gap(-3)
+        k = ts(T.gb[:, pos + 1:pos + n + 1], V("ga", t, pos, pos + n), -1025.0 / 1024.0, None, OP.mult, None, [k] + fills)
+        gap(-2)
+        k = scan(T.vv[:, 16 + pos:16 + pos + n], V("ga", t, pos, pos + n), T.gb[:, pos:pos + n], init, OP.add, OP.add, [k])
+        gap(-1)
+        o, c = (544 if pos else 0), pos // 16
+        k = fold(lambda a, b: T.vv[:, pos + a:pos + b], lambda a, b: V("tr", t, o + a, o + b),
+                 lambda a, b, s: V("ss", t, o + a, o + b, s), lambda a, b, s: V("vk", t, c + a, c + b, s), n, OP.add,
+                 [k], gap)
+        gap(2)
+        d = c + n // 16
+        k = tt(V("vk", t, 32 + c, 32 + d), V("vk", t, c, d), T.dump[:, c:d], OP.min, [k, k_du])
+        gap(3)
+        k = cp(V("de", t, c, d), V("vk", t, 32 + c, 32 + d), [k])
+        gap(4)
+        return cp(V("xs", t, 16, 848).indirect(V("de", t, c, d)), V("xx", t, pos, pos + n), [k, k_xs[t]])
+
+    qz(T.qx[:, 0:C // 2], T.sx[:, 0:C // 2], T.xin[:, 0:2 * C], [dxa])
+    k = qz(T.qx[:, C // 2:C], T.sx[:, C // 2:C], T.xin[:, 2 * C:4 * C], [dxb])
+    s_x = [act(plane(0, Z0, Z0 + C), T.xin[:, 0:4 * C:4], AF.Copy, [dxa, dxb], scale=0.5)]
+    s_sm = act(T.sm[:], T.smr[:], AF.Abs, [g_sm, k_hb], bias=hb)
+    k_xs = [act(V("xs", 0, 0, 256), T.rmp[:, 0:256], AF.Copy, [g_r0], scale=0.0)]
+    p = mm(T.ps[:, 0:C], T.qu[:], T.su[:], T.qx[:], T.sx[:], [k, k_qu])
+    k_bz = [ms(V("bt", t, P, 512), 0.0) for t in (1, 2)]
+    k_bits = ts(V("bt", 0, 0, C), T.ps[:, 0:C], 0.0, None, OP.is_gt, None, [p])
+    k = qz(V("qb", 0, 0, 128), V("sb", 0, 0, 128), V("bt", 0, 0, 512), [k_bits])
+    p = mm(T.pb[:, 0:128], T.qc[:, 0:128], T.sc[:, 0:128], V("qb", 0, 0, 128), V("sb", 0, 0, 128), [k, k_qb])
+    k_pb = tt(V("vl", 0, 0, 128), T.pb[:, 0:128], T.r64[:], OP.add, [p, k_r])
+    k_pa = None
+    k = scan(V("sl", 0, 0, 128), T.msk[:], V("vl", 0, 0, 128), 0.0, OP.max, OP.min, [k_pb, k_m])
+    k = cp(V("wi", 0, 0, 32), V("sl", 0, 3, 128, 4), [k])
+    k1 = ts(V("wi", 0, 32, 64), V("wi", 0, 0, 32), 127, None, OP.bitwise_and, None, [k])
+    k2 = ts(V("wi", 0, 64, 96), V("wi", 0, 0, 32), 4, 7, OP.arith_shift_right, OP.bitwise_and, [])
+    k1 = cp(V("au", 0, 0, 32), V("wi", 0, 32, 64), [k1])
+    k2 = tt(V("wi", 0, 96, 128), V("wi", 0, 64, 96), T.tab8[:], OP.add, [k2, k_t8])
+    hc = C // 2
+    jobs = signs_and_scans(0, 0, hc, V("au", 0, 0, 16), [k1], lambda m: -float(BIG), [g_r0], FIRST, 240)
+    run(jobs, 1)
+    k2 = cp(V("au", 0, 32, 64), V("wi", 0, 96, 128), [k2])
+    k_sc = run(jobs)
+    jobs = signs_and_scans(0, hc, hc, V("au", 0, 16, 32), [k1],
+                           lambda m: V("st", 0, 8 * (hc - 1) + m, 8 * (hc - 1) + m + 1), [k_sc], (), 240)
+    k_num = number(0, 0, hc, 0, V("au", 0, 32, 48), [k_sc, k2, g_x0], None, jobs, GAP0)
+    k_sc = run(jobs) or k_num
+    s_x += [act(plane(e, Z0, Z0 + C), T.xin[:, e:4 * C:4], AF.Copy, [], scale=0.5) for e in range(1, 4)]
+    k_xs += [act(V("xs", t, 0, 256), T.rmp[:, 0:256], AF.Copy, [], scale=0.0) for t in (1, 2)]
+    s_e = [act(T.et[:, 512 * b:512 * b + 512], T.eb[:, 3 - b:515 - b], AF.Copy, [g_e]) for b in range(4)]
+    k_num = number(0, hc, hc, 0, V("au", 0, 48, 64), [k_sc, k_num], k_num, [], 0)
+    pool_deps = k_z + s_x
+    pw_free = []
+    k_qe = []
+    qe_jobs = [(lambda b: k_qe.append(qz(T.qe[:, 128 * b:128 * b + 128], T.se[:, 128 * b:128 * b + 128],
+                                         T.et[:, 512 * b:512 * b + 512], [s_e[b]])), b) for b in range(4)]
+    nsent = 0
+
+    for t in range(R):
+        n = NT[t]
+        end = Z0 + Q0[t] + n
+        k_v = fold(lambda a, b: V("xs", t, a, b), lambda a, b: V("tx", t, a, b), lambda a, b, s: V("sx2", t, a, b, s),
+                   lambda a, b, s: V("vi", t, a, b, s), P, OP.min, [k_num], lambda j: None)
+        k1 = ts(V("vi", t, 46, 60), V("vi", t, 0, 14), 8191, None, OP.bitwise_and, None, [k_v])
+        k2 = ts(V("vi", t, 16, 30), V("vi", t, 0, 14), 13, None, OP.arith_shift_right, None, [])
+        ko = cp(V("ofs", t, 0, 14), V("vi", t, 46, 60), [k1])
+        k = tt(V("vi", t, 32, 46), V("vi", t, 16, 30), V("vi", t, 46, 60), OP.add, [k2])
+        s1 = [act(V("tmp", t, P * e, P * e + P), plane(e, 0, end).indirect(V("ofs", t, 0, 14)), AF.Copy,
+                  [ko] + pool_deps) for e in range(4)]
+        if t < R - 1:
+            k3 = ts(V("tw", t, 0, 14), V("vi", t, 0, 14), 0.0, 32896.0, OP.is_equal, OP.mult, [])
+            kj = cp(V("ofs", t, 14, 28), V("vi", t, 32, 46), [k])
+            k_w = tt(V("tw", t, 16, 30), T.tw0[:, 0:14], V("tw", t, 0, 14), OP.subtract, [k3, k_tw])
+        else:
+            k3 = ts(T.hf[:, 0:14], V("vi", t, 0, 14), 0.0, None, OP.is_lt, None, [])
+            kj = cp(V("ofs", t, 14, 28), V("vi", t, 32, 46), [k])
+            s_have = act(T.ocb[:, A:A + P], T.t01[:].indirect(T.hf[:, 0:14]), AF.Copy, [k3, k_01])
+            dma("y", T.occ[:], T.ocb[0:128:16, :], "do", [s_have, s_occ])
+            k = qz(T.qt[:, 0:A], T.sct[:, 0:A], T.tt[:, 0:4 * A], s_t)
+            dma("y", T.oc[:, 0:4 * A], T.qt[:, 0:A].bitcast(dt.uint8), "do", [k])
+            p_y = mm(T.py[:, 0:A], T.qv[:], T.sv[:], T.qt[:, 0:A], T.sct[:, 0:A], [k, k_qv])
+        run(qe_jobs, 2)
+        for e in range(4):
+            k = tt(V("bb", t, e, 4 * P, 4), plane(e, 0, end).indirect(V("ofs", t, 14, 28)),
+                   V("tmp", t, P * e, P * e + P), OP.add, [s1[e], kj] + pool_deps)
+        k = qz(V("qbb", t, 0, P), V("sbb", t, 0, P), V("bb", t, 0, 4 * P), [k])
+        pw = [mm(T.pw[:, 512 * b:512 * b + P], T.qw[:, 128 * b:128 * b + 128], T.sw[:, 128 * b:128 * b + 128],
+                 V("qbb", t, 0, P), V("sbb", t, 0, P), [k, dw] + pw_free) for b in range(4)]
+        if t == R - 1:
+            break
+        if t == 0:
+            k = ts(T.ca[:], T.gro[:], fg, vp, OP.is_equal, OP.mult, [g_g])
+            k_qa = qz(T.qc[:, 128:256], T.sc[:, 128:256], T.ca[:], [k])
+        else:
+            k_qv = qz(T.qv[:], T.sv[:], T.vin[:], [dv])
+            ms(T.t01[:, 0:1], 0.0)
+            k_01 = ms(T.t01[:, 1:16], 1.0)
+        hh, qh, sh = T["hh%d" % t], T["qh%d" % t], T["sh%d" % t]
+        ev = []
+        for b in range(4):
+            if b % 2:
+                ev.append(ts(hh[:, b:4 * P:4], T.pw[:, 512 * b:512 * b + P], 0.0, 0.03125, OP.max, OP.mult, [pw[b]]))
+            else:
+                ev.append(act(hh[:, b:4 * P:4], T.pw[:, 512 * b:512 * b + P], AF.Relu, [pw[b]], scale=0.03125))
+        k_qh = qz(qh[:], sh[:], hh[:], ev)
+        s_h = [act(plane(e, end, end + P), hh[:, e:4 * P:4], AF.Copy, ev, scale=0.5) for e in range(4)]
+        mate = T.cores[rank ^ (1 << t)]
+        rid, pid, _ = topo.addr(mate)
+        em, ne = topo.mask(core, mate), len(topo.engines(core, mate))
+        wait("g", [k_qh])
+        g.remote_dma(T["lq%d" % t][:].bitcast(dt.uint8), qh[:].bitcast(dt.uint8), T.sem["ac%d" % t], T.sem.sent, pid, rid, em)
+        u = t + 1
+        p = mm(T.ps[:, 0:P], T.qu[:], T.su[:], qh[:], sh[:], [k_qh, k_bits])
+        run(qe_jobs, 1)
+        k_bits = ts(V("bt", u, 0, P), T.ps[:, 0:P], 0.0, None, OP.is_gt, None, [p])
+        k = qz(V("qb", u, 0, 128), V("sb", u, 0, 128), V("bt", u, 0, 512), [k_bits] + k_bz)
+        pa = mm(T.pa[:, 0:128], T.qc[:, 128:256], T.sc[:, 128:256], V("qb", u, 0, 128), V("sb", u, 0, 128), [k, k_qa, k_pa])
+        pb = mm(T.pb[:, 0:128], T.qc[:, 0:128], T.sc[:, 0:128], V("qb", u, 0, 128), V("sb", u, 0, 128), [k, k_pb])
+        run(qe_jobs, 1)
+        k_pa = scan(V("ii", u, 0, 56), T.pa[:, 0:56], T.c64[:, 0:56], 32768.0, OP.add, OP.add, [pa])
+        k_pb = tt(V("vl", u, 0, 56), T.pb[:, 0:56], V("ii", u, 0, 56), OP.add, [pb, k_pa])
+        k = scan(V("sl", u, 0, 56), T.msk[:, 0:56], V("vl", u, 0, 56), 0.0, OP.max, OP.min, [k_pb])
+        k = tt(V("wi", u, 0, 14), V("sl", u, 3, 56, 4), V("tw", t, 16, 30), OP.subtract, [k, k_w])
+        ts(V("wi", u, 16, 30), V("wi", u, 0, 14), 255, None, OP.bitwise_and, None, [k])
+        k1 = ts(V("wi", u, 32, 46), V("wi", u, 0, 14), 256.0 * (L + 1), 128.0, OP.is_ge, OP.mult, [])
+        k2 = ts(V("wi", u, 48, 62), V("wi", u, 0, 14), 4, 7, OP.arith_shift_right, OP.bitwise_and, [])
+        tt(V("wi", u, 64, 78), V("wi", u, 16, 30), V("wi", u, 32, 46), OP.add, [k1])
+        k2 = tt(V("wi", u, 78, 92), V("wi", u, 48, 62), T.tab8[:, 14:28], OP.add, [k2])
+        msg, ll = T["msg%d" % t], T["ll%d" % t]
+        k_msg = cp(msg[:], V("wi", u, 64, 92), [k2])
+        wait("g", [k_msg])
+        g.remote_dma(ll[:], msg[:], T.sem["al%d" % t], T.sem.sent, pid, rid, em)
+        g.remote_dma(T["ls%d" % t][:], sh[:], T.sem["ac%d" % t], T.sem.sent, pid, rid, em)
+        nsent += 3 * ne
+        k_sc = run(signs_and_scans(u, 0, P, msg[:, 0:14], [k_msg],
+                                   lambda m: V("st", t, 8 * (n - 1) + m, 8 * (n - 1) + m + 1), [k_sc, g_r1], OWN, 112))
+        al, ac = ("al%d" % t, ne), ("ac%d" % t, 2 * ne)
+        jobs = signs_and_scans(u, P, P, ll[:, 0:14], [al],
+                               lambda m: V("st", u, 8 * (P - 1) + m, 8 * (P - 1) + m + 1), [k_sc], FAR, 240)
+        k_own = number(u, 0, P, 8 * P, msg[:, 14:28], [k_sc, g_x1], None, jobs, GAP1)
+        k_sc = run(jobs) or k_own
+        pd = [mm(T.pw[:, 512 * b:512 * b + P], T.qe[:, 128 * b:128 * b + 128], T.se[:, 128 * b:128 * b + 128],
+                 T["lq%d" % t][:], T["ls%d" % t][:], [ac] + k_qe + ev) for b in range(4)]
+        pw_free = [act(plane(b, end + P, end + 2 * P), T.pw[:, 512 * b:512 * b + P], AF.Copy,
+                       [pd[b]], scale=0.5) for b in range(4)]
+        pool_deps = pw_free + s_h
+        if u == R - 1:
+            fin = V("st", u, 8 * (2 * P - 1), 16 * P)
+            tok = {}
+            jobs = [(lambda j: tok.update(a=ts(T.wa[:], fin, -1.0 / 8192.0, 2048.0, OP.mult, OP.add, [k_sc]),
+                                          f=ts(T.wo[:, 8:16], fin, 0.0, None, OP.is_gt, None, [])), 0),
+                    (lambda j: tok.update(w=ts(T.wo[:, 0:8], T.wa[:], float(ZE), None, OP.min, None, [tok["a"]])), 1)]
+        k_num = number(u, P, P, 0, ll[:, 14:28], [k_sc, k_own, al], k_own, jobs, -4)
+        if u == R - 1:
+            s_t = [act(T.tt[:, e:4 * A:4], plane(e, 0, ZE + 1).indirect(T.wo[:, 0:8]), AF.Copy,
+                       [tok["w"]] + pool_deps, scale=2.0) for e in range(4)]
+            s_occ = act(T.ocb[:, 0:A], T.t01[:].indirect(T.wo[:, 8:16]), AF.Copy, [tok["f"], k_01])
+
+    s_y = act(T.ysb[:, 0:A], T.py[:, 0:A], AF.Copy, [p_y])
+    dma("y", T.y[:, 0:A], T.ysb[:, 0:A], "do", [s_y])
+    ev = []
+    for b in range(4):
+        k = tt(T.hm[:, P * b:P * b + P], T.pw[:, 512 * b:512 * b + P], T.ocb[:, A:A + P], OP.mult, [pw[b], s_have])
+        if b < 3:
+            ev.append(act(T.tt[:, 4 * A + b:4 * (A + P):4], T.hm[:, P * b:P * b + P], AF.Relu, [k], scale=0.03125))
+        else:
+            ev.append(ts(T.tt[:, 4 * A + b:4 * (A + P):4], T.hm[:, P * b:P * b + P], 0.0, 0.03125, OP.max, OP.mult, [k]))
+    k = qz(T.qt[:, A:A + P], T.sct[:, A:A + P], T.tt[:, 4 * A:4 * (A + P)], ev)
+    p = mm(T.ps[:, 0:P], T.qv[:], T.sv[:], T.qt[:, A:A + P], T.sct[:, A:A + P], [k, k_bits])
+    dma("y", T.oc[:, 4 * A:4 * (A + P)], T.qt[:, A:A + P].bitcast(dt.uint8), "do", [k])
+    for j in range(4):
+        dma("s" if j < 2 else "y", T.osc[4 * j:4 * j + 4, :], T.sct[32 * j:32 * j + 4, :], "do", [k])
+    k = cp(T.ysb[:, A:A + P], T.ps[:, 0:P], [p])
+    dma("s", T.y[:, A:A + P], T.ysb[:, A:A + P], "do", [k])
+    wait("g", [(s, c) for s, c in cnt.items()] + [("sent", nsent)])

@@ -1,4 +1,3 @@
-import math
 from concourse.mybir import dt, AluOpType as OP, ActivationFunctionType as AF
 
 C, A, P, L, R = 512, 128, 224, 96, 3
@@ -8,9 +7,12 @@ Z0 = 1
 NQ = C + 4 * P
 ZE = Z0 + NQ
 PW = ZE + 15
-BIG = 16777216
-FIRST, OWN, FAR = (0, 7), (0, 7), ()
-GAP0, GAP1 = -3, 2
+LAM, TOP = 48.0, 14.7
+BIG = 2.0 ** 30
+STEP = 2.0 ** 18
+AW = 512.0
+W0, W1, TW = 224, 192, 272
+DUMP = P + L
 H16 = "float16"
 CD, U8, BF, F32, I32, U16 = "float8_e4m3fn_x4", "uint8", "bfloat16", "float32", "int32", "uint16"
 
@@ -25,25 +27,26 @@ for _n, _c, _d in [
     ("xin", 4 * C, BF), ("qx", C, CD), ("sx", C, U8), ("uin", 512, BF), ("qu", 128, CD), ("su", 128, U8),
     ("vin", 512, BF), ("qv", 128, CD), ("sv", 128, U8), ("qw", 512, CD), ("sw", 512, U8),
     ("pool", 4 * PW, BF), ("gb", C + 16, H16), ("vv", C + 32, H16),
-    ("pcol", 1, I32), ("ci", 4, I32), ("cf", 4, F32), ("cx", 8, F32), ("wexp", 2, BF),
-    ("d64", 64, BF), ("pat", 192, BF), ("i16", 16, F32), ("gm", 16, F32), ("c4", 128, BF), ("raw", 32, F32),
+    ("pcol", 1, I32), ("ci", 4, I32), ("cf", 4, F32), ("cx", 12, F32), ("lt", 8, F32), ("pw2", 8, F32),
+    ("d64", 64, BF), ("pat", 192, BF), ("i16", 16, F32), ("gm", 16, F32), ("c4", 128, BF), ("raw", 34, F32),
     ("cb", 512, BF), ("ca", 512, BF), ("gro", 512, BF), ("qc", 256, CD), ("sc", 256, U8),
-    ("eb", 516, BF), ("et", 2048, BF), ("qe", 512, CD), ("se", 512, U8),
-    ("msk", 128, BF), ("c64", 128, BF), ("r64", 128, F32), ("sgt", 624, BF), ("st", 8 * NQ, F32), ("sg16", 16, BF),
-    ("tab8", 32, I32), ("dump", 32, F32), ("tw0", 16, F32), ("smr", 544, BF), ("sm", 544, BF),
-    ("rmp", NQ, F32), ("tbx", NQ, F32), ("t01", 16, F32),
+    ("eb", 516, BF), ("qe", 512, CD), ("se", 512, U8),
+    ("msk", 128, BF), ("c64", 64, BF), ("r64", 128, F32), ("st", 8 * NQ, BF), ("sg16", 16, BF),
+    ("one", W0 + TW, BF), ("two", W1 + TW, BF), ("tw0", 32, F32), ("smr", 544, BF), ("sm", 544, BF),
+    ("cap", 544, H16), ("dmp", 34, F32), ("rin", PW, F32), ("nam", PW, BF), ("t01", 16, F32), ("ln0", 1, F32),
     ("tt", 4 * (A + P), BF), ("qt", A + P, CD), ("sct", A + P, U8), ("ysb", A + P, F32), ("ocb", A + P, F32),
-    ("hm", 4 * P, F32), ("wa", 8, F32), ("wo", 16, U16), ("hf", 16, U16),
+    ("hm", 4 * P, F32), ("wa", 8, F32), ("wl", 8, F32), ("wo", 16, U16), ("hf", 16, U16),
 ]:
     _sb(_n, _c, _d)
-WID = {"bt": (512, BF), "qb": (128, CD), "sb": (128, U8), "ii": (128, F32), "vl": (128, F32), "sl": (128, F32),
-       "wi": (160, I32), "au": (64, U16), "sig": (8 * C, BF), "xx": (C, F32),
+WID = {"bt": (512, BF), "qb": (128, CD), "sb": (128, U8), "ii": (64, F32), "vl": (128, F32), "sl": (128, F32),
+       "pk": (32, F32), "ee": (4 * 256, BF), "sig": (8 * C, BF), "zz": (C, BF),
        "ga": (C, H16), "tr": (1088, H16), "ss": (1088, H16),
-       "vk": (80, F32), "de": (32, U16), "xs": (848, F32), "tx": (480, F32), "sx2": (480, F32),
-       "vi": (64, I32), "ofs": (28, U16), "tmp": (4 * P, BF), "bb": (4 * P, BF), "qbb": (P, CD), "sbb": (P, U8),
-       "tw": (32, F32)}
+       "vk": (48, F32), "de": (32, U16), "xs": (896, BF), "tx": (480, BF), "lo": (480, BF), "hi": (480, BF),
+       "fv": (32, F32), "lg": (32, F32), "ofs": (28, U16), "tmp": (4 * P, BF), "bb": (4 * P, BF), "qbb": (P, CD),
+       "sbb": (P, U8), "tw": (32, F32)}
 for _n, (_c, _d) in WID.items():
     _sb(_n, R * _c, _d)
+_sb("au", 64, U16)
 for _t in range(2):
     for _n, _c, _d in [("hh", 4 * P, BF), ("qh", P, CD), ("sh", P, U8), ("lq", P, CD), ("ls", P, U8),
                        ("msg", 28, U16), ("ll", 28, U16)]:
@@ -130,6 +133,15 @@ def rank_program(g, core, T, topo):
     def plane(e, a, b):
         return T.pool[:, PW * e + a:PW * e + b]
 
+    def names(t, pos, n):
+        return T.nam[:, Z0 + Q0[t] + pos:Z0 + Q0[t] + pos + n]
+
+    def run(jobs, k=99):
+        last = None
+        for _ in range(min(k, len(jobs))):
+            last = jobs.pop(0)()
+        return last
+
     du = dma("y", T.uin[:], T.u[:], "du", [])
     dxa = dma("y", T.xin[:, 0:2 * C], T.x[:, 0:2 * C], "dxa", [])
     dxb = dma("s", T.xin[:, 2 * C:4 * C], T.x[:, 2 * C:4 * C], "dxb", [])
@@ -138,176 +150,182 @@ def rank_program(g, core, T, topo):
     dv = dma("y", T.vin[:], T.v[:], "dv", [])
 
     g_p = iota(T.pcol[:], [[0, 1]], 0, 1, False)
-    g_d = iota(T.d64[:], [[0, 4], [-1, 4], [1, 4]], 0, 0)
     g_i = iota(T.i16[:], [[1, 16]], 0, 0)
+    g_d = iota(T.d64[:], [[0, 4], [-1, 4], [1, 4]], 0, 0)
+    g_r0 = iota(T.rin[:, 0:C + Z0], [[1, C + Z0]], 0, 0)
     g_c = iota(T.c4[:], [[0, 32], [1, 4]], 0, 0)
-    g_r = iota(T.raw[:], [[16, 32]], 0, 0)
-    g_r0 = iota(T.rmp[:, 0:C], [[8192, C]], 8192 * Z0 - BIG, 0)
+    g_r = iota(T.raw[:], [[16, 34]], DUMP, 0)
     g_sm = iota(T.smr[:], [[0, 17], [1, 2], [0, 16]], 0, 0)
-    g_x0 = iota(T.tbx[:, 0:C], [[8191, C]], 8191 * Z0 - BIG, 0)
+    g_r1 = iota(T.rin[:, C + Z0:PW], [[1, PW - C - Z0]], C + Z0, 0)
     g_g = iota(T.gro[:], [[1, 8], [0, 64]], 0, 0)
     g_e = iota(T.eb[:], [[0, 516]], 1, 0)
     wait("g", [g_e])
     g_e = done(g.affine_select(T.eb[:], T.eb[:], [[1, 516]], OP.is_equal, 0.0, -3, -4), "cg", 1)
-    g_r1 = iota(T.rmp[:, C:NQ], [[8192, NQ - C]], 8192 * (Z0 + C) - BIG, 0)
-    g_x1 = iota(T.tbx[:, C:NQ], [[8191, NQ - C]], 8191 * (Z0 + C) - BIG, 0)
 
-    k_sg = ms(T.sgt[:], 1.0)
-    k_c = ms(T.c64[:], 65536.0)
+    k_two = ms(T.two[:], -1.0)
     ts(T.ci[:, 0:1], T.pcol[:], 15, None, OP.bitwise_and, None, [g_p])
     ts(T.ci[:, 1:2], T.pcol[:], 4, 1, OP.arith_shift_right, OP.bitwise_and, [])
     ts(T.ci[:, 2:3], T.pcol[:], 4, None, OP.arith_shift_right, None, [])
     k = ts(T.ci[:, 3:4], T.pcol[:], 2, 3, OP.arith_shift_right, OP.bitwise_and, [])
+    k_c = ms(T.c64[:], STEP)
     k_cf = cp(T.cf[:], T.ci[:], [k])
     fi, fh, fg, fq = (T.cf[:, j:j + 1] for j in range(4))
-    w0, vp, w1, hb, q1 = (T.cx[:, j:j + 1] for j in range(5))
-    s_w = act(T.wexp[:, 0:1], fi, AF.Exp, [k_cf], scale=math.log(2.0))
-    k_vp = ts(vp, fi, 7.0, 256.0, OP.is_equal, OP.mult, [k_cf])
-    k_gm = ts(T.gm[:], T.i16[:], fg, None, OP.is_equal, None, [g_i])
-    k = ts(T.sg16[:], T.i16[:], fi, 2.0, OP.not_equal, OP.mult, [])
+    w0, vp, w1, hb, q1, q2, c2 = (T.cx[:, j:j + 1] for j in range(7))
+    scan(T.r64[:, 0:64], T.c64[:], T.c64[:], 456.0, OP.add, OP.max, [k_c])
+    k = ts(T.lt[:], T.i16[:, 0:8], fi, 1.0, OP.is_lt, OP.add, [k_cf, g_i])
+    k_vp = ts(vp, fi, 7.0, None, OP.is_equal, None, [])
+    k_gm = ts(T.gm[:], T.i16[:], fg, None, OP.is_equal, None, [])
+    k = scan(T.pw2[:], T.lt[:], T.lt[:], AW, OP.mult, OP.max, [k])
     k_l = ts(T.pat[:, 64:128], T.d64[:], 0.0, vp, OP.is_gt, OP.mult, [g_d, k_vp])
-    k_sg = ts(T.sgt[:, 240:256], T.sg16[:], -1.0, None, OP.add, None, [k, k_sg])
-    k_m = ts(T.msk[:], T.c4[:], fq, 33554432.0, OP.is_equal, OP.mult, [g_c])
-    k_r = scan(T.r64[:], T.c64[:], T.c64[:], 0.0, OP.add, OP.max, [k_c])
-    k_t8 = ts(T.tab8[:], T.raw[:], fi, 8.0, OP.add, OP.mult, [g_r])
-    k_du = ts(T.dump[:], T.raw[:], fi, 320.0, OP.add, OP.add, [])
-    k_hb = ts(hb, fh, -1.0, None, OP.add, None, [])
-    k = ts(q1, fq, 1.0, 65536.0, OP.add, OP.mult, [])
-    k_z = [ms(T.pool[:, 0:4 * PW:PW], 0.0), ms(T.pool[:, ZE:4 * PW:PW], 0.0)]
-    k_tw = ts(T.tw0[:], T.raw[:, 0:16], 16384.0, q1, OP.mult, OP.add, [k])
-    fills = [ms(T.gb[:, 0:2], 0.0), ms(T.vv[:], 0.0)]
-    k = ts(w0, fi, 7.0, T.wexp[:, 0:1], OP.is_lt, OP.mult, [s_w])
+    k_16 = ts(T.sg16[:], T.i16[:], fi, 2.0, OP.not_equal, OP.mult, [])
+    k = ts(w0, fi, 7.0, T.pw2[:, 7:8], OP.is_lt, OP.mult, [k])
+    k_r = scan(T.r64[:, 64:128], T.c64[:], T.c64[:], 64 * STEP + 200.0, OP.add, OP.max, [])
+    k_hb = ts(hb, fh, -1.0, BIG, OP.add, OP.mult, [])
     k = ts(w1, vp, -128.0, w0, OP.mult, OP.add, [k])
+    ts(T.two[:, W1 + 3:W1 + 35:2], T.sg16[:], -3.0, None, OP.add, None, [k_16, k_two])
+    k_two = ts(T.two[:, W1 + 35:W1 + 67:2], T.sg16[:], -1.0, 1.0, OP.mult, OP.add, [])
     k = ts(T.pat[:, 0:64], T.d64[:], 0.0, w1, OP.is_equal, OP.mult, [k])
+    ts(q1, fq, STEP, STEP - AW - DUMP * STEP / 4, OP.mult, OP.add, [])
+    k_q = ts(q2, fq, -32.0, -32.504, OP.mult, OP.add, [])
     k_pat = tt(T.pat[:, 128:192], T.pat[:, 0:64], T.pat[:, 64:128], OP.subtract, [k, k_l])
-    kb = []
-    for j in range(8):
-        if j % 2:
-            kb.append(act(T.cb[:, 64 * j:64 * j + 64], T.pat[:, 128:192], AF.Copy, [k_pat, k_gm], scale=T.gm[:, j:j + 1]))
-        else:
-            kb.append(ts(T.cb[:, 64 * j:64 * j + 64], T.pat[:, 128:192], T.gm[:, j:j + 1], None, OP.mult, None, [k_pat, k_gm]))
+    k_c2 = ts(c2, fi, 8.0, q2, OP.mult, OP.add, [k_q])
+    s_n0 = act(T.nam[:, 0:C + Z0], T.rin[:, 0:C + Z0], AF.Exp, [g_r0], scale=-1.0 / LAM, bias=TOP)
+    kb = [ts(T.cb[:, 64 * j:64 * j + 64], T.pat[:, 128:192], T.gm[:, j:j + 1], None, OP.mult, None, [k_pat, k_gm])
+          for j in range(8)]
     k_qu = qz(T.qu[:], T.su[:], T.uin[:], [du])
-    k_qb = qz(T.qc[:, 0:128], T.sc[:, 0:128], T.cb[:], kb)
 
-    def signs_and_scans(t, pos, n, offs, deps, init, ideps, mine, w0):
-        def win(m):
-            return T.sgt[:, w0 - 16 * m:w0 + 384 - 16 * m].indirect(offs)
+    def sg(t, pos, n, m):
+        return V("sig", t, 8 * pos + m * n, 8 * pos + (m + 1) * n)
 
-        def sg(m):
-            return V("sig", t, 8 * pos + m * n, 8 * pos + (m + 1) * n)
-        tok = {}
-        for m in range(8):
-            if m not in mine:
-                tok[m] = act(sg(m), win(m), AF.Copy, deps + [k_sg])
+    def follow(t, pos, n, m, init, deps):
+        return scan(V("st", t, 8 * pos + m, 8 * (pos + n), 8), names(t, pos, n), sg(t, pos, n, m), init(m),
+                    OP.min, OP.mult, deps)
 
-        def one(m):
-            if m not in tok:
-                tok[m] = cp(sg(m), win(m), deps + [k_sg])
-            return scan(V("st", t, 8 * pos + m, 8 * (pos + n), 8), T.rmp[:, Q0[t] + pos:Q0[t] + pos + n], sg(m),
-                        init(m), OP.max, OP.mult, [tok[m]] + ideps)
-        return [(one, m) for m in ((0, 1, 2, 3, 7, 4, 5, 6) if 7 in mine else range(8))]
+    def scans_by_twos(t, n, offs, deps, init, ideps):
+        def win(q):
+            return T.two[:, W1 - 64 * q:W1 - 64 * q + TW].indirect(offs)
+        e = [act(V("ee", t, 256 * q, 256 * q + n), win(q), AF.Copy, deps + [k_two]) for q in range(3 if t else 4)]
+        for q in range(4):
+            if q == 0 and t:
+                e.append(cp(V("ee", t, 768, 768 + n), win(3), deps + [k_two]))
+            ka = ts(sg(t, 0, n, 2 * q), V("ee", t, 256 * q, 256 * q + n), -1.0, 2.0, OP.min, OP.add, [e[q]])
+            kc = ts(sg(t, 0, n, 2 * q + 1), V("ee", t, 256 * q, 256 * q + n), -1.0, -1.0, OP.max, OP.mult, [])
+            follow(t, 0, n, 2 * q, init, [ka] + ideps)
+            k = follow(t, 0, n, 2 * q + 1, init, [kc])
+        return k
 
-    def run(jobs, k=99):
-        last = None
-        for _ in range(min(k, len(jobs))):
-            f, a = jobs.pop(0)
-            last = f(a)
-        return last
+    def scans_by_ones(t, pos, n, offs, deps, ideps):
+        tok = [act(sg(t, pos, n, m), T.one[:, W0 - 32 * m:W0 - 32 * m + TW].indirect(offs), AF.Copy, deps)
+               for m in range(8)]
 
-    def fold(src, tr, ss, out, n, op, deps, gap):
+        def job(m):
+            return lambda: follow(t, pos, n, m, lambda j: V("st", t, 8 * (pos - 1) + j, 8 * (pos - 1) + j + 1),
+                                  [tok[m]] + ideps)
+        return [job(m) for m in range(8)]
+
+    def turn(src, tr, n, deps):
         trp(tr(0, n), src(16, 16 + n), deps)
-        k = trp(tr(n, 2 * n + 32), src(0, n + 32), [])
-        gap(0)
-        k = scan(ss(0, 2 * n + 32, 1), tr(0, 2 * n + 32), T.sm[:, 0:2 * n + 32], 0.0, op, OP.mult, [k, s_sm])
-        gap(1)
-        tt(out(0, n // 16, 2), ss(15, n, 32), ss(n + 31, 2 * n, 32), OP.add, [k])
-        return tt(out(1, n // 16, 2), ss(n + 47, 2 * n + 32, 32), ss(31, n, 32), OP.add, [])
+        return trp(tr(n, 2 * n + 32), src(0, n + 32), [])
 
-    def number(t, pos, n, lead, offs, deps, before, jobs, first):
+    def number(t, pos, n, offs, deps, before, jobs, gaps):
         def gap(j):
-            if j >= first:
-                run(jobs, 1)
-        k = tt(V("xx", t, pos, pos + n), V("st", t, -lead, 8 * (pos + n)).indirect(offs),
-               T.tbx[:, Q0[t] + pos:Q0[t] + pos + n], OP.subtract, deps)
-        init = 64.0
-        gap(-4)
+            run(jobs, gaps[j])
+        z = V("zz", t, pos, pos + n)
+        kz = tt(z, V("st", t, 8 * pos if t else 0, 8 * (pos + n)).indirect(offs), names(t, pos, n), OP.max, deps)
+        init = 1.0 / 16
+        gap(0)
         if pos:
-            init = V("vk", t, 64, 65)
+            init = V("vk", t, 40, 41)
             cp(init, T.vv[:, 15 + pos:16 + pos], [before])
-        k = ts(V("ga", t, pos, pos + n), V("xx", t, pos, pos + n), 0.0, -1024.0, OP.is_lt, OP.mult, [k])
-        gap(-3)
-        k = ts(T.gb[:, pos + 1:pos + n + 1], V("ga", t, pos, pos + n), -1025.0 / 1024.0, None, OP.mult, None, [k] + fills)
-        gap(-2)
-        k = scan(T.vv[:, 16 + pos:16 + pos + n], V("ga", t, pos, pos + n), T.gb[:, pos:pos + n], init, OP.add, OP.add, [k])
-        gap(-1)
-        o, c = (544 if pos else 0), pos // 16
-        k = fold(lambda a, b: T.vv[:, pos + a:pos + b], lambda a, b: V("tr", t, o + a, o + b),
-                 lambda a, b, s: V("ss", t, o + a, o + b, s), lambda a, b, s: V("vk", t, c + a, c + b, s), n, OP.add,
-                 [k], gap)
+        k = tt(V("ga", t, pos, pos + n), z, names(t, pos, n), OP.is_gt, [kz])
+        gap(1)
+        k = ts(T.gb[:, pos + 1:pos + n + 1], V("ga", t, pos, pos + n), 1025.0 / 1024.0, None, OP.mult, None, [k] + fills)
         gap(2)
-        d = c + n // 16
-        k = tt(V("vk", t, 32 + c, 32 + d), V("vk", t, c, d), T.dump[:, c:d], OP.min, [k, k_du])
+        k = scan(T.vv[:, 16 + pos:16 + pos + n], T.gb[:, pos:pos + n], V("ga", t, pos, pos + n), init, OP.add, OP.subtract, [k])
         gap(3)
-        k = cp(V("de", t, c, d), V("vk", t, 32 + c, 32 + d), [k])
+        o, c = (544 if pos else 0), pos // 16
+        d = c + n // 16
+        k = turn(lambda a, b: T.vv[:, pos + a:pos + b], lambda a, b: V("tr", t, o + a, o + b), n, [k])
         gap(4)
-        return cp(V("xs", t, 16, 848).indirect(V("de", t, c, d)), V("xx", t, pos, pos + n), [k, k_xs[t]])
+        k = scan(V("ss", t, o, o + 2 * n + 32), V("tr", t, o, o + 2 * n + 32), T.cap[:, 0:2 * n + 32], 0.0, OP.add, OP.min,
+                 [k] + k_cap)
+        gap(5)
+        k = tt(V("vk", t, c, d), V("ss", t, o + 15, o + n, 16), V("ss", t, o + n + 31, o + 2 * n + 16, 16), OP.add, [k])
+        gap(6)
+        k = ts(V("de", t, c, d), V("vk", t, c, d), 1024.0, None, OP.mult, None, [k])
+        gap(7)
+        return cp(V("xs", t, 16, 896).indirect(V("de", t, c, d)), z, [k, k_xs[t]])
 
     qz(T.qx[:, 0:C // 2], T.sx[:, 0:C // 2], T.xin[:, 0:2 * C], [dxa])
     k = qz(T.qx[:, C // 2:C], T.sx[:, C // 2:C], T.xin[:, 2 * C:4 * C], [dxb])
-    s_x = [act(plane(0, Z0, Z0 + C), T.xin[:, 0:4 * C:4], AF.Copy, [dxa, dxb], scale=0.5)]
-    s_sm = act(T.sm[:], T.smr[:], AF.Abs, [g_sm, k_hb], bias=hb)
-    k_xs = [act(V("xs", 0, 0, 256), T.rmp[:, 0:256], AF.Copy, [g_r0], scale=0.0)]
+    s_sm = act(T.sm[:], T.smr[:], AF.Abs, [g_sm, k_hb], bias=hb, scale=BIG)
+    s_x = [act(plane(e, Z0, Z0 + C), T.xin[:, e:4 * C:4], AF.Copy, [dxa, dxb], scale=0.5) for e in range(2)]
     p = mm(T.ps[:, 0:C], T.qu[:], T.su[:], T.qx[:], T.sx[:], [k, k_qu])
-    k_bz = [ms(V("bt", t, P, 512), 0.0) for t in (1, 2)]
+    k_qb = qz(T.qc[:, 0:128], T.sc[:, 0:128], T.cb[:], kb)
+    k_m = ts(T.msk[:], T.c4[:], fq, 2.0 ** 26, OP.is_equal, OP.mult, [g_c])
+    k_tw = ts(T.tw0[:], T.raw[:, 0:32], STEP / 4, q1, OP.mult, OP.add, [g_r, k_q])
     k_bits = ts(V("bt", 0, 0, C), T.ps[:, 0:C], 0.0, None, OP.is_gt, None, [p])
+    k_du = ts(T.dmp[:], T.raw[:], fi, 1.0 / 1024, OP.add, OP.mult, [])
     k = qz(V("qb", 0, 0, 128), V("sb", 0, 0, 128), V("bt", 0, 0, 512), [k_bits])
     p = mm(T.pb[:, 0:128], T.qc[:, 0:128], T.sc[:, 0:128], V("qb", 0, 0, 128), V("sb", 0, 0, 128), [k, k_qb])
+    k_one = ms(T.one[:], 1.0)
     k_pb = tt(V("vl", 0, 0, 128), T.pb[:, 0:128], T.r64[:], OP.add, [p, k_r])
     k_pa = None
+    k_one = ts(T.one[:, W0 + 2:W0 + 34:2], T.sg16[:], -1.0, None, OP.add, None, [k_one])
     k = scan(V("sl", 0, 0, 128), T.msk[:], V("vl", 0, 0, 128), 0.0, OP.max, OP.min, [k_pb, k_m])
-    k = cp(V("wi", 0, 0, 32), V("sl", 0, 3, 128, 4), [k])
-    k1 = ts(V("wi", 0, 32, 64), V("wi", 0, 0, 32), 127, None, OP.bitwise_and, None, [k])
-    k2 = ts(V("wi", 0, 64, 96), V("wi", 0, 0, 32), 4, 7, OP.arith_shift_right, OP.bitwise_and, [])
-    k1 = cp(V("au", 0, 0, 32), V("wi", 0, 32, 64), [k1])
-    k2 = tt(V("wi", 0, 96, 128), V("wi", 0, 64, 96), T.tab8[:], OP.add, [k2, k_t8])
+    fills = [ms(T.gb[:, 0:2], 0.0), ms(T.vv[:, 0:16], 0.0)]
+    k1 = tt(V("pk", 0, 0, 32), V("sl", 0, 3, 128, 4), T.tw0[:], OP.subtract, [k, k_tw])
+    k2 = ts(T.au[:, 32:64], V("sl", 0, 3, 128, 4), 1.0 / (16 * AW), c2, OP.mult, OP.add, [k_c2])
+    k1 = ts(T.au[:, 0:32], V("pk", 0, 0, 32), 1.0 / 256, -0.498, OP.mult, OP.add, [k1])
     hc = C // 2
-    jobs = signs_and_scans(0, 0, hc, V("au", 0, 0, 16), [k1], lambda m: -float(BIG), [g_r0], FIRST, 240)
-    run(jobs, 1)
-    k2 = cp(V("au", 0, 32, 64), V("wi", 0, 96, 128), [k2])
-    k_sc = run(jobs)
-    jobs = signs_and_scans(0, hc, hc, V("au", 0, 16, 32), [k1],
-                           lambda m: V("st", 0, 8 * (hc - 1) + m, 8 * (hc - 1) + m + 1), [k_sc], (), 240)
-    k_num = number(0, 0, hc, 0, V("au", 0, 32, 48), [k_sc, k2, g_x0], None, jobs, GAP0)
+    fills += [ms(T.vv[:, 16 + hc:32 + hc], 0.0), ms(T.vv[:, 16 + C:32 + C], 0.0)]
+    k_cap = [ms(T.cap[:], 60000.0)]
+    k_sc = scans_by_twos(0, hc, T.au[:, 0:16], [k1], lambda m: BIG, [s_n0])
+    k_cap = [tt(T.cap[:, 15:544:16], T.dmp[:], T.sm[:, 15:544:16], OP.min, k_cap + [k_du, s_sm])]
+    k_xs = [act(V("xs", 0, 0, 256), T.rin[:, 0:256], AF.Identity, [s_n0], scale=0.0, bias=T.nam[:, 0:1])]
+    jobs = scans_by_ones(0, hc, hc, T.au[:, 16:32], [k1, k_one], [k_sc])
+    k_num = number(0, 0, hc, T.au[:, 32:48], [k_sc, k2], None, jobs, [1, 1, 1, 1, 1, 1, 0, 1])
     k_sc = run(jobs) or k_num
-    s_x += [act(plane(e, Z0, Z0 + C), T.xin[:, e:4 * C:4], AF.Copy, [], scale=0.5) for e in range(1, 4)]
-    k_xs += [act(V("xs", t, 0, 256), T.rmp[:, 0:256], AF.Copy, [], scale=0.0) for t in (1, 2)]
-    s_e = [act(T.et[:, 512 * b:512 * b + 512], T.eb[:, 3 - b:515 - b], AF.Copy, [g_e]) for b in range(4)]
-    k_num = number(0, hc, hc, 0, V("au", 0, 48, 64), [k_sc, k_num], k_num, [], 0)
+    s_n1 = act(T.nam[:, C + Z0:PW], T.rin[:, C + Z0:PW], AF.Exp, [g_r1], scale=-1.0 / LAM, bias=TOP)
+    s_ln = act(T.ln0[:], T.nam[:, 0:1], AF.Ln, [])
+    s_x += [act(plane(e, Z0, Z0 + C), T.xin[:, e:4 * C:4], AF.Copy, [], scale=0.5) for e in range(2, 4)]
+    k_z, k_bz = [], []
+    jobs = [lambda: k_z.append(ms(T.pool[:, 0:4 * PW:PW], 0.0)), lambda: k_z.append(ms(T.pool[:, ZE:4 * PW:PW], 0.0)),
+            lambda: k_bz.append(ms(V("bt", 1, P, 512), 0.0)), lambda: k_bz.append(ms(V("bt", 2, P, 512), 0.0))]
+    k_num = number(0, hc, hc, T.au[:, 48:64], [k_sc, k_num], k_num, jobs, [0, 1, 1, 1, 1, 0, 0, 0])
     pool_deps = k_z + s_x
     pw_free = []
     k_qe = []
-    qe_jobs = [(lambda b: k_qe.append(qz(T.qe[:, 128 * b:128 * b + 128], T.se[:, 128 * b:128 * b + 128],
-                                         T.et[:, 512 * b:512 * b + 512], [s_e[b]])), b) for b in range(4)]
+
+    def qe_job(b):
+        return lambda: k_qe.append(qz(T.qe[:, 128 * b:128 * b + 128], T.se[:, 128 * b:128 * b + 128],
+                                      T.eb[:, 3 - b:515 - b], [g_e]))
+    qe_jobs = [qe_job(b) for b in range(4)]
     nsent = 0
 
     for t in range(R):
         n = NT[t]
         end = Z0 + Q0[t] + n
-        k_v = fold(lambda a, b: V("xs", t, a, b), lambda a, b: V("tx", t, a, b), lambda a, b, s: V("sx2", t, a, b, s),
-                   lambda a, b, s: V("vi", t, a, b, s), P, OP.min, [k_num], lambda j: None)
-        k1 = ts(V("vi", t, 46, 60), V("vi", t, 0, 14), 8191, None, OP.bitwise_and, None, [k_v])
-        k2 = ts(V("vi", t, 16, 30), V("vi", t, 0, 14), 13, None, OP.arith_shift_right, None, [])
-        ko = cp(V("ofs", t, 0, 14), V("vi", t, 46, 60), [k1])
-        k = tt(V("vi", t, 32, 46), V("vi", t, 16, 30), V("vi", t, 46, 60), OP.add, [k2])
+        k = turn(lambda a, b: V("xs", t, a, b), lambda a, b: V("tx", t, a, b), P, [k_num])
+        w = 2 * P + 32
+        k_lo = scan(V("lo", t, 0, w), V("tx", t, 0, w), T.sm[:, 16:16 + w], BIG, OP.min, OP.max, [k, s_sm])
+        k_hi = scan(V("hi", t, 0, w), V("tx", t, 0, w), T.sm[:, 0:w], 0.0, OP.max, OP.min, [])
+        k_lo = tt(V("fv", t, 0, 14), V("lo", t, 15, P, 16), V("lo", t, P + 31, w - 16, 16), OP.min, [k_lo])
+        k_hi = tt(V("fv", t, 16, 30), V("hi", t, 15, P, 16), V("hi", t, P + 31, w - 16, 16), OP.max, [k_hi])
+        s_lo = act(V("lg", t, 0, 14), V("fv", t, 0, 14), AF.Ln, [k_lo])
+        s_hi = act(V("lg", t, 16, 30), V("fv", t, 16, 30), AF.Ln, [k_hi])
+        if t < R - 1:
+            k3 = ts(V("tw", t, 0, 14), V("fv", t, 0, 14), T.nam[:, 0:1], 2.0 ** 22, OP.is_ge, OP.mult, [k_lo])
+        else:
+            k3 = ts(T.hf[:, 0:14], V("fv", t, 0, 14), T.nam[:, 0:1], None, OP.is_lt, None, [k_lo])
+        ko = ts(V("ofs", t, 0, 14), V("lg", t, 0, 14), T.ln0[:], -LAM, OP.subtract, OP.mult, [s_lo, s_ln])
+        kj = ts(V("ofs", t, 14, 28), V("lg", t, 16, 30), T.ln0[:], -LAM, OP.subtract, OP.mult, [s_hi])
         s1 = [act(V("tmp", t, P * e, P * e + P), plane(e, 0, end).indirect(V("ofs", t, 0, 14)), AF.Copy,
                   [ko] + pool_deps) for e in range(4)]
         if t < R - 1:
-            k3 = ts(V("tw", t, 0, 14), V("vi", t, 0, 14), 0.0, 32896.0, OP.is_equal, OP.mult, [])
-            kj = cp(V("ofs", t, 14, 28), V("vi", t, 32, 46), [k])
-            k_w = tt(V("tw", t, 16, 30), T.tw0[:, 0:14], V("tw", t, 0, 14), OP.subtract, [k3, k_tw])
+            k_w = tt(V("tw", t, 16, 30), T.tw0[:, 0:14], V("tw", t, 0, 14), OP.add, [k3, k_tw])
+            k_xs.append(act(V("xs", t + 1, 0, 256), T.rin[:, 0:256], AF.Identity, [], scale=0.0, bias=T.nam[:, 0:1]))
         else:
-            k3 = ts(T.hf[:, 0:14], V("vi", t, 0, 14), 0.0, None, OP.is_lt, None, [])
-            kj = cp(V("ofs", t, 14, 28), V("vi", t, 32, 46), [k])
             s_have = act(T.ocb[:, A:A + P], T.t01[:].indirect(T.hf[:, 0:14]), AF.Copy, [k3, k_01])
             dma("y", T.occ[:], T.ocb[0:128:16, :], "do", [s_have, s_occ])
             k = qz(T.qt[:, 0:A], T.sct[:, 0:A], T.tt[:, 0:4 * A], s_t)
@@ -324,7 +342,6 @@ def rank_program(g, core, T, topo):
             break
         if t == 0:
             k = ts(T.ca[:], T.gro[:], fg, vp, OP.is_equal, OP.mult, [g_g])
-            k_qa = qz(T.qc[:, 128:256], T.sc[:, 128:256], T.ca[:], [k])
         else:
             k_qv = qz(T.qv[:], T.sv[:], T.vin[:], [dv])
             ms(T.t01[:, 0:1], 0.0)
@@ -342,49 +359,53 @@ def rank_program(g, core, T, topo):
         rid, pid, _ = topo.addr(mate)
         em, ne = topo.mask(core, mate), len(topo.engines(core, mate))
         wait("g", [k_qh])
-        g.remote_dma(T["lq%d" % t][:].bitcast(dt.uint8), qh[:].bitcast(dt.uint8), T.sem["ac%d" % t], T.sem.sent, pid, rid, em)
+        g.remote_dma(T["ls%d" % t][:], sh[:], T.sem["ac%d" % t], T.sem.sent, pid, rid, em)
         u = t + 1
         p = mm(T.ps[:, 0:P], T.qu[:], T.su[:], qh[:], sh[:], [k_qh, k_bits])
-        run(qe_jobs, 1)
+        if t == 0:
+            k_qa = qz(T.qc[:, 128:256], T.sc[:, 128:256], T.ca[:], [k])
         k_bits = ts(V("bt", u, 0, P), T.ps[:, 0:P], 0.0, None, OP.is_gt, None, [p])
         k = qz(V("qb", u, 0, 128), V("sb", u, 0, 128), V("bt", u, 0, 512), [k_bits] + k_bz)
         pa = mm(T.pa[:, 0:128], T.qc[:, 128:256], T.sc[:, 128:256], V("qb", u, 0, 128), V("sb", u, 0, 128), [k, k_qa, k_pa])
         pb = mm(T.pb[:, 0:128], T.qc[:, 0:128], T.sc[:, 0:128], V("qb", u, 0, 128), V("sb", u, 0, 128), [k, k_pb])
         run(qe_jobs, 1)
-        k_pa = scan(V("ii", u, 0, 56), T.pa[:, 0:56], T.c64[:, 0:56], 32768.0, OP.add, OP.add, [pa])
+        k_pa = scan(V("ii", u, 0, 56), T.pa[:, 0:56], T.c64[:, 0:56], 384.0 - L - 1, OP.add, OP.add, [pa])
         k_pb = tt(V("vl", u, 0, 56), T.pb[:, 0:56], V("ii", u, 0, 56), OP.add, [pb, k_pa])
         k = scan(V("sl", u, 0, 56), T.msk[:, 0:56], V("vl", u, 0, 56), 0.0, OP.max, OP.min, [k_pb])
-        k = tt(V("wi", u, 0, 14), V("sl", u, 3, 56, 4), V("tw", t, 16, 30), OP.subtract, [k, k_w])
-        ts(V("wi", u, 16, 30), V("wi", u, 0, 14), 255, None, OP.bitwise_and, None, [k])
-        k1 = ts(V("wi", u, 32, 46), V("wi", u, 0, 14), 256.0 * (L + 1), 128.0, OP.is_ge, OP.mult, [])
-        k2 = ts(V("wi", u, 48, 62), V("wi", u, 0, 14), 4, 7, OP.arith_shift_right, OP.bitwise_and, [])
-        tt(V("wi", u, 64, 78), V("wi", u, 16, 30), V("wi", u, 32, 46), OP.add, [k1])
-        k2 = tt(V("wi", u, 78, 92), V("wi", u, 48, 62), T.tab8[:, 14:28], OP.add, [k2])
         msg, ll = T["msg%d" % t], T["ll%d" % t]
-        k_msg = cp(msg[:], V("wi", u, 64, 92), [k2])
-        wait("g", [k_msg])
+        k1 = tt(V("pk", u, 0, 14), V("sl", u, 3, 56, 4), V("tw", t, 16, 30), OP.subtract, [k, k_w])
+        k2 = ts(msg[:, 14:28], V("sl", u, 3, 56, 4), 1.0 / (16 * AW), c2, OP.mult, OP.add, [])
+        k1 = ts(msg[:, 0:14], V("pk", u, 0, 14), 1.0 / 256, -0.498, OP.mult, OP.add, [k1])
+        wait("g", [k1])
         g.remote_dma(ll[:], msg[:], T.sem["al%d" % t], T.sem.sent, pid, rid, em)
-        g.remote_dma(T["ls%d" % t][:], sh[:], T.sem["ac%d" % t], T.sem.sent, pid, rid, em)
+        g.remote_dma(T["lq%d" % t][:].bitcast(dt.uint8), qh[:].bitcast(dt.uint8), T.sem["ac%d" % t], T.sem.sent, pid, rid, em)
         nsent += 3 * ne
-        k_sc = run(signs_and_scans(u, 0, P, msg[:, 0:14], [k_msg],
-                                   lambda m: V("st", t, 8 * (n - 1) + m, 8 * (n - 1) + m + 1), [k_sc, g_r1], OWN, 112))
+        run(qe_jobs, 1)
+        k_sc = scans_by_twos(u, P, msg[:, 0:14], [k1], lambda m: V("st", t, 8 * (n - 1) + m, 8 * (n - 1) + m + 1),
+                             [k_sc, s_n1])
         al, ac = ("al%d" % t, ne), ("ac%d" % t, 2 * ne)
-        jobs = signs_and_scans(u, P, P, ll[:, 0:14], [al],
-                               lambda m: V("st", u, 8 * (P - 1) + m, 8 * (P - 1) + m + 1), [k_sc], FAR, 240)
-        k_own = number(u, 0, P, 8 * P, msg[:, 14:28], [k_sc, g_x1], None, jobs, GAP1)
+        jobs = scans_by_ones(u, P, P, ll[:, 0:14], [al], [k_sc])
+        k_own = number(u, 0, P, msg[:, 14:28], [k_sc], None, jobs, [1, 1, 1, 1, 1, 1, 0, 1])
         k_sc = run(jobs) or k_own
         pd = [mm(T.pw[:, 512 * b:512 * b + P], T.qe[:, 128 * b:128 * b + 128], T.se[:, 128 * b:128 * b + 128],
                  T["lq%d" % t][:], T["ls%d" % t][:], [ac] + k_qe + ev) for b in range(4)]
         pw_free = [act(plane(b, end + P, end + 2 * P), T.pw[:, 512 * b:512 * b + P], AF.Copy,
                        [pd[b]], scale=0.5) for b in range(4)]
         pool_deps = pw_free + s_h
+        jobs = []
         if u == R - 1:
             fin = V("st", u, 8 * (2 * P - 1), 16 * P)
             tok = {}
-            jobs = [(lambda j: tok.update(a=ts(T.wa[:], fin, -1.0 / 8192.0, 2048.0, OP.mult, OP.add, [k_sc]),
-                                          f=ts(T.wo[:, 8:16], fin, 0.0, None, OP.is_gt, None, [])), 0),
-                    (lambda j: tok.update(w=ts(T.wo[:, 0:8], T.wa[:], float(ZE), None, OP.min, None, [tok["a"]])), 1)]
-        k_num = number(u, P, P, 0, ll[:, 14:28], [k_sc, k_own, al], k_own, jobs, -4)
+
+            def fin_a():
+                k = ts(T.wa[:], fin, -1.0, T.nam[:, ZE:ZE + 1], OP.mult, OP.max, [k_sc])
+                tok["l"] = act(T.wl[:], T.wa[:], AF.Ln, [k])
+                tok["f"] = ts(T.wo[:, 8:16], fin, 0.0, None, OP.is_lt, None, [])
+
+            def fin_b():
+                tok["w"] = ts(T.wo[:, 0:8], T.wl[:], T.ln0[:], -LAM, OP.subtract, OP.mult, [tok["l"]])
+            jobs = [fin_a, fin_b]
+        k_num = number(u, P, P, ll[:, 14:28], [k_sc, k_own, al], k_own, jobs, [1, 0, 0, 0, 1, 0, 0, 0])
         if u == R - 1:
             s_t = [act(T.tt[:, e:4 * A:4], plane(e, 0, ZE + 1).indirect(T.wo[:, 0:8]), AF.Copy,
                        [tok["w"]] + pool_deps, scale=2.0) for e in range(4)]

@@ -9,10 +9,13 @@ ZE = Z0 + NQ
 PW = ZE + 15
 LAM, TOP = 48.0, 14.7
 BIG = 2.0 ** 30
-STEP = 2.0 ** 18
+NONE = 2 ** 22
+PICK = 2.0 ** 18
+GONE = 2.0 ** 20
 AW = 512.0
 W0, W1, TW = 224, 192, 272
 DUMP = P + L
+RUNS = [(0, 128), (128, P)]
 H16 = "float16"
 CD, U8, BF, F32, I32, U16 = "float8_e4m3fn_x4", "uint8", "bfloat16", "float32", "int32", "uint16"
 
@@ -31,28 +34,27 @@ for _n, _c, _d in [
     ("d64", 64, BF), ("pat", 192, BF), ("i16", 16, F32), ("gm", 16, F32), ("c4", 128, BF), ("raw", 34, F32),
     ("cb", 512, BF), ("ca", 512, BF), ("gro", 512, BF), ("qc", 256, CD), ("sc", 256, U8),
     ("eb", 516, BF), ("qe", 512, CD), ("se", 512, U8),
-    ("msk", 128, BF), ("c64", 64, BF), ("r64", 128, F32), ("st", 8 * NQ, BF), ("sg16", 16, BF),
-    ("one", W0 + TW, BF), ("two", W1 + TW, BF), ("tw0", 32, F32), ("smr", 544, BF), ("sm", 544, BF),
+    ("m01", 128, BF), ("pik", 130, F32), ("st", 8 * NQ, BF), ("sg16", 16, BF),
+    ("one", W0 + TW, BF), ("two", W1 + TW, BF), ("tab", 32, F32), ("smr", 544, BF), ("sm", 544, BF),
     ("cap", 544, H16), ("dmp", 34, F32), ("rin", PW, F32), ("nam", PW, BF), ("t01", 16, F32), ("ln0", 1, F32),
-    ("tt", 4 * (A + P), BF), ("qt", A + P, CD), ("sct", A + P, U8), ("ysb", A + P, F32), ("ocb", A + P, F32),
+    ("tt", 4 * (A + 256), BF), ("qt", A + 256, CD), ("sct", A + 256, U8), ("ysb", A + P, F32), ("ocb", A + P, F32),
     ("hm", 4 * P, F32), ("wa", 8, F32), ("wl", 8, F32), ("wo", 16, U16), ("hf", 16, U16),
+    ("bb", 1024, BF), ("au", 64, U16),
 ]:
     _sb(_n, _c, _d)
 WID = {"bt": (512, BF), "qb": (128, CD), "sb": (128, U8), "ii": (64, F32), "vl": (128, F32), "sl": (128, F32),
-       "pk": (32, F32), "ee": (4 * 256, BF), "sig": (8 * C, BF), "zz": (C, BF),
+       "pk": (32, F32), "ee": (4 * 256, BF), "sig": (8 * C, BF), "zz": (C, BF), "inc": (64, BF),
        "ga": (C, H16), "tr": (1088, H16), "ss": (1088, H16),
-       "vk": (48, F32), "de": (32, U16), "xs": (896, BF), "tx": (480, BF), "lo": (480, BF), "hi": (480, BF),
-       "fv": (32, F32), "lg": (32, F32), "ofs": (28, U16), "tmp": (4 * P, BF), "bb": (4 * P, BF), "qbb": (P, CD),
-       "sbb": (P, U8), "tw": (32, F32)}
+       "vk": (48, F32), "de": (32, U16), "xs": (896, BF), "tx": (480, BF), "lo": (64, BF), "hi": (480, BF),
+       "fv": (32, F32), "lg": (32, F32), "ofs": (28, U16), "tmp": (4 * P, BF), "qbb": (256, CD),
+       "sbb": (256, U8), "tw": (48, F32)}
 for _n, (_c, _d) in WID.items():
     _sb(_n, R * _c, _d)
-_sb("au", 64, U16)
 for _t in range(2):
-    for _n, _c, _d in [("hh", 4 * P, BF), ("qh", P, CD), ("sh", P, U8), ("lq", P, CD), ("ls", P, U8),
+    for _n, _c, _d in [("hh", 1024, BF), ("qh", 256, CD), ("sh", 256, U8), ("lq", P, CD), ("ls", P, U8),
                        ("msg", 28, U16), ("ll", 28, U16)]:
         _sb("%s%d" % (_n, _t), _c, _d)
-for _n, _c in [("ps", 512), ("pa", 512), ("pb", 512), ("pw", 2048), ("py", 512)]:
-    SCRATCH[_n] = ("psum", [128, _c], F32)
+SCRATCH["pm"] = ("psum", [128, 4096], F32)
 
 SEMAPHORES = ["cv", "cs", "cp", "cg", "du", "dxa", "dxb", "dw", "dv", "do", "sent", "ac0", "ac1", "al0", "al1"]
 
@@ -64,6 +66,7 @@ def rank_program(g, core, T, topo):
     que = {"v": g.vector, "s": g.scalar, "p": g.tensor, "g": g, "y": g.sync}
     cnt = {}
     seen = {}
+    users = [[] for _ in range(8)]
 
     def wait(q, deps):
         need = {}
@@ -113,9 +116,17 @@ def rank_program(g, core, T, topo):
         wait("s", deps)
         return done(g.scalar.activation(out, a, f, **kw), "cs", 1)
 
-    def mm(out, q1, s1, q2, s2, deps):
-        wait("p", deps)
-        return done(g.tensor.matmul_mx(out, q1, s1, q2, s2, True, True), "cp", 1)
+    def bank(i, n):
+        return T.pm[:, 512 * i:512 * i + n]
+
+    def mm(i, q1, s1, q2, s2, n, deps):
+        wait("p", deps + users[i])
+        users[i] = []
+        return done(g.tensor.matmul_mx(bank(i, n), q1, s1, q2, s2, True, True), "cp", 1)
+
+    def used(i, k):
+        users[i].append(k)
+        return k
 
     def iota(out, pat, base, ch, flag=True):
         if flag:
@@ -142,9 +153,13 @@ def rank_program(g, core, T, topo):
             last = jobs.pop(0)()
         return last
 
+    def weave(order, lists):
+        for c in order:
+            run(lists[c], 1)
+
     du = dma("y", T.uin[:], T.u[:], "du", [])
-    dxa = dma("y", T.xin[:, 0:2 * C], T.x[:, 0:2 * C], "dxa", [])
-    dxb = dma("s", T.xin[:, 2 * C:4 * C], T.x[:, 2 * C:4 * C], "dxb", [])
+    dxa = dma("s", T.xin[:, 0:2 * C], T.x[:, 0:2 * C], "dxa", [])
+    dxb = dma("y", T.xin[:, 2 * C:4 * C], T.x[:, 2 * C:4 * C], "dxb", [])
     dma("y", T.qw[:].bitcast(dt.uint8), T.wc[:], "dw", [dxa, dxb])
     dw = dma("y", T.sw[:], T.ws[:], "dw", [])
     dv = dma("y", T.vin[:], T.v[:], "dv", [])
@@ -152,26 +167,28 @@ def rank_program(g, core, T, topo):
     g_p = iota(T.pcol[:], [[0, 1]], 0, 1, False)
     g_i = iota(T.i16[:], [[1, 16]], 0, 0)
     g_d = iota(T.d64[:], [[0, 4], [-1, 4], [1, 4]], 0, 0)
-    g_r0 = iota(T.rin[:, 0:C + Z0], [[1, C + Z0]], 0, 0)
+    g_r0 = iota(T.rin[:, 16:C + Z0], [[1, C + Z0 - 16]], 16, 0)
     g_c = iota(T.c4[:], [[0, 32], [1, 4]], 0, 0)
+    g_two = iota(T.two[:], [[0, W1 + TW]], -1, 0)
     g_r = iota(T.raw[:], [[16, 34]], DUMP, 0)
     g_sm = iota(T.smr[:], [[0, 17], [1, 2], [0, 16]], 0, 0)
+    g_one = iota(T.one[:], [[0, W0 + TW]], 1, 0)
+    k_xs = [iota(V("xs", 0, 0, 256), [[0, 256]], NONE, 0)]
     g_r1 = iota(T.rin[:, C + Z0:PW], [[1, PW - C - Z0]], C + Z0, 0)
-    g_g = iota(T.gro[:], [[1, 8], [0, 64]], 0, 0)
     g_e = iota(T.eb[:], [[0, 516]], 1, 0)
     wait("g", [g_e])
     g_e = done(g.affine_select(T.eb[:], T.eb[:], [[1, 516]], OP.is_equal, 0.0, -3, -4), "cg", 1)
+    g_g = iota(T.gro[:], [[1, 8], [0, 64]], 0, 0)
+    k_xs += [iota(V("xs", t, 0, 256), [[0, 256]], NONE, 0) for t in (1, 2)]
 
-    k_two = ms(T.two[:], -1.0)
+    s_n0 = act(T.nam[:, 0:16], T.i16[:], AF.Exp, [g_i], scale=-1.0 / LAM, bias=TOP)
     ts(T.ci[:, 0:1], T.pcol[:], 15, None, OP.bitwise_and, None, [g_p])
     ts(T.ci[:, 1:2], T.pcol[:], 4, 1, OP.arith_shift_right, OP.bitwise_and, [])
     ts(T.ci[:, 2:3], T.pcol[:], 4, None, OP.arith_shift_right, None, [])
     k = ts(T.ci[:, 3:4], T.pcol[:], 2, 3, OP.arith_shift_right, OP.bitwise_and, [])
-    k_c = ms(T.c64[:], STEP)
     k_cf = cp(T.cf[:], T.ci[:], [k])
     fi, fh, fg, fq = (T.cf[:, j:j + 1] for j in range(4))
-    w0, vp, w1, hb, q1, q2, c2 = (T.cx[:, j:j + 1] for j in range(7))
-    scan(T.r64[:, 0:64], T.c64[:], T.c64[:], 456.0, OP.add, OP.max, [k_c])
+    w0, vp, w1, hb, q1 = (T.cx[:, j:j + 1] for j in range(5))
     k = ts(T.lt[:], T.i16[:, 0:8], fi, 1.0, OP.is_lt, OP.add, [k_cf, g_i])
     k_vp = ts(vp, fi, 7.0, None, OP.is_equal, None, [])
     k_gm = ts(T.gm[:], T.i16[:], fg, None, OP.is_equal, None, [])
@@ -179,20 +196,16 @@ def rank_program(g, core, T, topo):
     k_l = ts(T.pat[:, 64:128], T.d64[:], 0.0, vp, OP.is_gt, OP.mult, [g_d, k_vp])
     k_16 = ts(T.sg16[:], T.i16[:], fi, 2.0, OP.not_equal, OP.mult, [])
     k = ts(w0, fi, 7.0, T.pw2[:, 7:8], OP.is_lt, OP.mult, [k])
-    k_r = scan(T.r64[:, 64:128], T.c64[:], T.c64[:], 64 * STEP + 200.0, OP.add, OP.max, [])
     k_hb = ts(hb, fh, -1.0, BIG, OP.add, OP.mult, [])
+    k_q = ts(q1, fi, 128 * AW, PICK - DUMP * 128 * AW, OP.mult, OP.add, [])
     k = ts(w1, vp, -128.0, w0, OP.mult, OP.add, [k])
-    ts(T.two[:, W1 + 3:W1 + 35:2], T.sg16[:], -3.0, None, OP.add, None, [k_16, k_two])
-    k_two = ts(T.two[:, W1 + 35:W1 + 67:2], T.sg16[:], -1.0, 1.0, OP.mult, OP.add, [])
+    fills = [ms(T.gb[:, 0:2], 0.0), ms(T.vv[:, 0:16], 0.0)]
     k = ts(T.pat[:, 0:64], T.d64[:], 0.0, w1, OP.is_equal, OP.mult, [k])
-    ts(q1, fq, STEP, STEP - AW - DUMP * STEP / 4, OP.mult, OP.add, [])
-    k_q = ts(q2, fq, -32.0, -32.504, OP.mult, OP.add, [])
+    fills += [ms(T.vv[:, 16 + C // 2:32 + C // 2], 0.0), ms(T.vv[:, 16 + C:32 + C], 0.0)]
     k_pat = tt(T.pat[:, 128:192], T.pat[:, 0:64], T.pat[:, 64:128], OP.subtract, [k, k_l])
-    k_c2 = ts(c2, fi, 8.0, q2, OP.mult, OP.add, [k_q])
-    s_n0 = act(T.nam[:, 0:C + Z0], T.rin[:, 0:C + Z0], AF.Exp, [g_r0], scale=-1.0 / LAM, bias=TOP)
-    kb = [ts(T.cb[:, 64 * j:64 * j + 64], T.pat[:, 128:192], T.gm[:, j:j + 1], None, OP.mult, None, [k_pat, k_gm])
+    s_n0 = act(T.nam[:, 16:C + Z0], T.rin[:, 16:C + Z0], AF.Exp, [g_r0], scale=-1.0 / LAM, bias=TOP)
+    kb = [act(T.cb[:, 64 * j:64 * j + 64], T.pat[:, 128:192], AF.Copy, [k_pat, k_gm], scale=T.gm[:, j:j + 1])
           for j in range(8)]
-    k_qu = qz(T.qu[:], T.su[:], T.uin[:], [du])
 
     def sg(t, pos, n, m):
         return V("sig", t, 8 * pos + m * n, 8 * pos + (m + 1) * n)
@@ -204,97 +217,119 @@ def rank_program(g, core, T, topo):
     def scans_by_twos(t, n, offs, deps, init, ideps):
         def win(q):
             return T.two[:, W1 - 64 * q:W1 - 64 * q + TW].indirect(offs)
-        e = [act(V("ee", t, 256 * q, 256 * q + n), win(q), AF.Copy, deps + [k_two]) for q in range(3 if t else 4)]
+        e = [act(V("ee", t, 256 * q, 256 * q + n), win(q), AF.Copy, deps + [k_two]) for q in range(3)]
+        e.append(cp(V("ee", t, 768, 768 + n), win(3), deps + [k_two]))
         for q in range(4):
-            if q == 0 and t:
-                e.append(cp(V("ee", t, 768, 768 + n), win(3), deps + [k_two]))
             ka = ts(sg(t, 0, n, 2 * q), V("ee", t, 256 * q, 256 * q + n), -1.0, 2.0, OP.min, OP.add, [e[q]])
             kc = ts(sg(t, 0, n, 2 * q + 1), V("ee", t, 256 * q, 256 * q + n), -1.0, -1.0, OP.max, OP.mult, [])
             follow(t, 0, n, 2 * q, init, [ka] + ideps)
             k = follow(t, 0, n, 2 * q + 1, init, [kc])
         return k
 
-    def scans_by_ones(t, pos, n, offs, deps, ideps):
+    def scans_by_ones(t, pos, n, offs, deps, ideps, out):
         tok = [act(sg(t, pos, n, m), T.one[:, W0 - 32 * m:W0 - 32 * m + TW].indirect(offs), AF.Copy, deps)
                for m in range(8)]
 
         def job(m):
-            return lambda: follow(t, pos, n, m, lambda j: V("st", t, 8 * (pos - 1) + j, 8 * (pos - 1) + j + 1),
-                                  [tok[m]] + ideps)
+            return lambda: out.append(follow(t, pos, n, m, lambda j: V("st", t, 8 * (pos - 1) + j, 8 * (pos - 1) + j + 1),
+                                             [tok[m]] + ideps))
         return [job(m) for m in range(8)]
 
     def turn(src, tr, n, deps):
         trp(tr(0, n), src(16, 16 + n), deps)
         return trp(tr(n, 2 * n + 32), src(0, n + 32), [])
 
-    def number(t, pos, n, offs, deps, before, jobs, gaps):
-        def gap(j):
-            run(jobs, gaps[j])
+    def number(t, pos, n, offs, deps, cuts, k):
         z = V("zz", t, pos, pos + n)
-        kz = tt(z, V("st", t, 8 * pos if t else 0, 8 * (pos + n)).indirect(offs), names(t, pos, n), OP.max, deps)
-        init = 1.0 / 16
-        gap(0)
-        if pos:
-            init = V("vk", t, 40, 41)
-            cp(init, T.vv[:, 15 + pos:16 + pos], [before])
-        k = tt(V("ga", t, pos, pos + n), z, names(t, pos, n), OP.is_gt, [kz])
-        gap(1)
-        k = ts(T.gb[:, pos + 1:pos + n + 1], V("ga", t, pos, pos + n), 1025.0 / 1024.0, None, OP.mult, None, [k] + fills)
-        gap(2)
-        k = scan(T.vv[:, 16 + pos:16 + pos + n], T.gb[:, pos:pos + n], V("ga", t, pos, pos + n), init, OP.add, OP.subtract, [k])
-        gap(3)
         o, c = (544 if pos else 0), pos // 16
         d = c + n // 16
-        k = turn(lambda a, b: T.vv[:, pos + a:pos + b], lambda a, b: V("tr", t, o + a, o + b), n, [k])
-        gap(4)
-        k = scan(V("ss", t, o, o + 2 * n + 32), V("tr", t, o, o + 2 * n + 32), T.cap[:, 0:2 * n + 32], 0.0, OP.add, OP.min,
-                 [k] + k_cap)
-        gap(5)
-        k = tt(V("vk", t, c, d), V("ss", t, o + 15, o + n, 16), V("ss", t, o + n + 31, o + 2 * n + 16, 16), OP.add, [k])
-        gap(6)
-        k = ts(V("de", t, c, d), V("vk", t, c, d), 1024.0, None, OP.mult, None, [k])
-        gap(7)
-        return cp(V("xs", t, 16, 896).indirect(V("de", t, c, d)), z, [k, k_xs[t]])
+        init = V("vk", t, 40, 41) if pos else 1.0 / 16
 
-    qz(T.qx[:, 0:C // 2], T.sx[:, 0:C // 2], T.xin[:, 0:2 * C], [dxa])
-    k = qz(T.qx[:, C // 2:C], T.sx[:, C // 2:C], T.xin[:, 2 * C:4 * C], [dxb])
-    s_sm = act(T.sm[:], T.smr[:], AF.Abs, [g_sm, k_hb], bias=hb, scale=BIG)
-    s_x = [act(plane(e, Z0, Z0 + C), T.xin[:, e:4 * C:4], AF.Copy, [dxa, dxb], scale=0.5) for e in range(2)]
-    p = mm(T.ps[:, 0:C], T.qu[:], T.su[:], T.qx[:], T.sx[:], [k, k_qu])
-    k_qb = qz(T.qc[:, 0:128], T.sc[:, 0:128], T.cb[:], kb)
-    k_m = ts(T.msk[:], T.c4[:], fq, 2.0 ** 26, OP.is_equal, OP.mult, [g_c])
-    k_tw = ts(T.tw0[:], T.raw[:, 0:32], STEP / 4, q1, OP.mult, OP.add, [g_r, k_q])
-    k_bits = ts(V("bt", 0, 0, C), T.ps[:, 0:C], 0.0, None, OP.is_gt, None, [p])
-    k_du = ts(T.dmp[:], T.raw[:], fi, 1.0 / 1024, OP.add, OP.mult, [])
-    k = qz(V("qb", 0, 0, 128), V("sb", 0, 0, 128), V("bt", 0, 0, 512), [k_bits])
-    p = mm(T.pb[:, 0:128], T.qc[:, 0:128], T.sc[:, 0:128], V("qb", 0, 0, 128), V("sb", 0, 0, 128), [k, k_qb])
-    k_one = ms(T.one[:], 1.0)
-    k_pb = tt(V("vl", 0, 0, 128), T.pb[:, 0:128], T.r64[:], OP.add, [p, k_r])
-    k_pa = None
-    k_one = ts(T.one[:, W0 + 2:W0 + 34:2], T.sg16[:], -1.0, None, OP.add, None, [k_one])
-    k = scan(V("sl", 0, 0, 128), T.msk[:], V("vl", 0, 0, 128), 0.0, OP.max, OP.min, [k_pb, k_m])
-    fills = [ms(T.gb[:, 0:2], 0.0), ms(T.vv[:, 0:16], 0.0)]
-    k1 = tt(V("pk", 0, 0, 32), V("sl", 0, 3, 128, 4), T.tw0[:], OP.subtract, [k, k_tw])
-    k2 = ts(T.au[:, 32:64], V("sl", 0, 3, 128, 4), 1.0 / (16 * AW), c2, OP.mult, OP.add, [k_c2])
-    k1 = ts(T.au[:, 0:32], V("pk", 0, 0, 32), 1.0 / 256, -0.498, OP.mult, OP.add, [k1])
+        def larger():
+            k[pos] = tt(z, V("st", t, 8 * pos if t else 0, 8 * (pos + n)).indirect(offs), names(t, pos, n), OP.max, deps)
+            if pos:
+                cp(init, T.vv[:, 15 + pos:16 + pos], [k[0]])
+
+        def second():
+            k[pos] = tt(V("ga", t, pos, pos + n), z, names(t, pos, n), OP.is_gt, [k[pos]])
+
+        def back():
+            k[pos] = ts(T.gb[:, pos + 1:pos + n + 1], V("ga", t, pos, pos + n), 1025.0 / 1024.0, None, OP.mult, None,
+                        [k[pos]] + fills)
+
+        def count():
+            k[pos] = scan(T.vv[:, 16 + pos:16 + pos + n], T.gb[:, pos:pos + n], V("ga", t, pos, pos + n), init,
+                          OP.add, OP.subtract, [k[pos]])
+
+        def turned():
+            k[pos] = turn(lambda a, b: T.vv[:, pos + a:pos + b], lambda a, b: V("tr", t, o + a, o + b), n, [k[pos]])
+
+        def summed():
+            k[pos] = scan(V("ss", t, o, o + 2 * n + 32), V("tr", t, o, o + 2 * n + 32), T.cap[:, 0:2 * n + 32], 0.0,
+                          OP.add, OP.min, [k[pos]] + k_cap)
+
+        def joined():
+            k[pos] = tt(V("vk", t, c, d), V("ss", t, o + 15, o + n, 16), V("ss", t, o + n + 31, o + 2 * n + 16, 16),
+                        OP.add, [k[pos]])
+
+        def places():
+            k[pos] = ts(V("de", t, c, d), V("vk", t, c, d), 1024.0, None, OP.mult, None, [k[pos]])
+
+        def piece(a, b):
+            def put():
+                k["put"] = cp(V("xs", t, 16, 896).indirect(V("de", t, c + a, c + b)),
+                              V("zz", t, pos + 16 * a, pos + 16 * b), [k[pos], k_xs[t], k.get("put")])
+            return put
+        return ([larger, second, back, count, turned, summed, joined, places],
+                [piece(a, b) for a, b in zip(cuts, cuts[1:])])
+
+    WEAVE = "abababababababab" + "cdcdcdcdcdcdfdfdfe"
+
     hc = C // 2
-    fills += [ms(T.vv[:, 16 + hc:32 + hc], 0.0), ms(T.vv[:, 16 + C:32 + C], 0.0)]
     k_cap = [ms(T.cap[:], 60000.0)]
+    k_qu = qz(T.qu[:], T.su[:], T.uin[:], [du])
+    ka = qz(T.qx[:, 0:hc], T.sx[:, 0:hc], T.xin[:, 0:2 * C], [dxa])
+    pa = mm(4, T.qu[:], T.su[:], T.qx[:, 0:hc], T.sx[:, 0:hc], hc, [ka, k_qu])
+    kc = qz(T.qx[:, hc:C], T.sx[:, hc:C], T.xin[:, 2 * C:4 * C], [dxb])
+    pb = mm(5, T.qu[:], T.su[:], T.qx[:, hc:C], T.sx[:, hc:C], hc, [kc])
+    s_x = [act(plane(0, Z0, Z0 + C), T.xin[:, 0:4 * C:4], AF.Copy, [dxa, dxb], scale=0.5)]
+    s_sm = act(T.sm[:], T.smr[:], AF.Abs, [g_sm, k_hb], bias=hb, scale=BIG)
+    ka = used(4, ts(V("bt", 0, 0, hc), bank(4, hc), 0.0, None, OP.is_gt, None, [pa]))
+    k_qb = qz(T.qc[:, 0:128], T.sc[:, 0:128], T.cb[:], kb)
+    kc = used(5, ts(V("bt", 0, hc, C), bank(5, hc), 0.0, None, OP.is_gt, None, [pb]))
+    k_pik = ts(T.pik[:, 1:129], T.c4[:], fq, -PICK, OP.is_equal, OP.mult, [g_c])
+    k = qz(V("qb", 0, 0, 128), V("sb", 0, 0, 128), V("bt", 0, 0, 512), [ka, kc])
+    p = mm(6, T.qc[:, 0:128], T.sc[:, 0:128], V("qb", 0, 0, 128), V("sb", 0, 0, 128), 128, [k, k_qb])
+    ts(T.two[:, W1 + 3:W1 + 35:2], T.sg16[:], -3.0, None, OP.add, None, [k_16, g_two])
+    k_two = ts(T.two[:, W1 + 35:W1 + 67:2], T.sg16[:], -1.0, 1.0, OP.mult, OP.add, [])
+    k_m = ts(T.m01[:], T.c4[:], 0.0, None, OP.is_gt, None, [])
+    k_tab = ts(T.tab[:], T.raw[:, 0:32], 128 * AW, q1, OP.mult, OP.add, [g_r, k_q])
+    k = used(6, tt(V("vl", 0, 0, 128), bank(6, 128), T.pik[:, 1:129], OP.add, [p, k_pik]))
+    k_du = ts(T.dmp[:], T.raw[:], fi, 1.0 / 1024, OP.add, OP.mult, [])
+    k = scan(V("sl", 0, 0, 128), T.m01[:], V("vl", 0, 0, 128), 0.0, OP.mult, OP.min, [k, k_m])
+    k_p0 = ms(T.pik[:, 0:1], 0.0)
+    k1 = ts(T.au[:, 0:16], V("sl", 0, 3, 64, 4), PICK + 456 + AW - 127.5, 1.0 / 256, OP.add, OP.mult, [k])
+    k1b = ts(T.au[:, 16:32], V("sl", 0, 67, 128, 4), PICK + 200 + AW - 127.5, 1.0 / 256, OP.add, OP.mult, [])
+    k2 = tt(V("pk", 0, 0, 32), V("sl", 0, 3, 128, 4), T.tab[:], OP.add, [k_tab])
+    k_one = ts(T.one[:, W0 + 2:W0 + 34:2], T.sg16[:], -1.0, None, OP.add, None, [g_one])
     k_sc = scans_by_twos(0, hc, T.au[:, 0:16], [k1], lambda m: BIG, [s_n0])
+    k2 = ts(T.au[:, 32:64], V("pk", 0, 0, 32), 1.0 / (16 * AW), -0.47, OP.mult, OP.add, [k2])
     k_cap = [tt(T.cap[:, 15:544:16], T.dmp[:], T.sm[:, 15:544:16], OP.min, k_cap + [k_du, s_sm])]
-    k_xs = [act(V("xs", 0, 0, 256), T.rin[:, 0:256], AF.Identity, [s_n0], scale=0.0, bias=T.nam[:, 0:1])]
-    jobs = scans_by_ones(0, hc, hc, T.au[:, 16:32], [k1, k_one], [k_sc])
-    k_num = number(0, 0, hc, T.au[:, 32:48], [k_sc, k2], None, jobs, [1, 1, 1, 1, 1, 1, 0, 1])
-    k_sc = run(jobs) or k_num
+    last = []
+    scans = scans_by_ones(0, hc, hc, T.au[:, 16:32], [k1b, k_one], [k_sc], last)
     s_n1 = act(T.nam[:, C + Z0:PW], T.rin[:, C + Z0:PW], AF.Exp, [g_r1], scale=-1.0 / LAM, bias=TOP)
     s_ln = act(T.ln0[:], T.nam[:, 0:1], AF.Ln, [])
-    s_x += [act(plane(e, Z0, Z0 + C), T.xin[:, e:4 * C:4], AF.Copy, [], scale=0.5) for e in range(2, 4)]
-    k_z, k_bz = [], []
-    jobs = [lambda: k_z.append(ms(T.pool[:, 0:4 * PW:PW], 0.0)), lambda: k_z.append(ms(T.pool[:, ZE:4 * PW:PW], 0.0)),
-            lambda: k_bz.append(ms(V("bt", 1, P, 512), 0.0)), lambda: k_bz.append(ms(V("bt", 2, P, 512), 0.0))]
-    k_num = number(0, hc, hc, T.au[:, 48:64], [k_sc, k_num], k_num, jobs, [0, 1, 1, 1, 1, 0, 0, 0])
+    s_x += [act(plane(e, Z0, Z0 + C), T.xin[:, e:4 * C:4], AF.Copy, [], scale=0.5) for e in range(1, 4)]
+    k_z, k_pad = [], []
+    kn = {}
+    a, c = number(0, 0, hc, T.au[:, 32:48], [k_sc, k2], [0, 4, 8, 10, 12, 14, 16], kn)
+    d, e = number(0, hc, hc, T.au[:, 48:64], last, [0, 16], kn)
+    weave(WEAVE, {"a": a, "b": scans, "c": c, "d": d, "e": e,
+                  "f": [lambda: k_z.append(ms(T.pool[:, 0:4 * PW:PW], 0.0)),
+                        lambda: k_z.append(ms(T.pool[:, ZE:4 * PW:PW], 0.0)),
+                        lambda: k_pad.append(ms(T.bb[:, 4 * P:1024], 0.0))]})
+    k_sc = last[-1]
     pool_deps = k_z + s_x
-    pw_free = []
     k_qe = []
 
     def qe_job(b):
@@ -302,129 +337,172 @@ def rank_program(g, core, T, topo):
                                       T.eb[:, 3 - b:515 - b], [g_e]))
     qe_jobs = [qe_job(b) for b in range(4)]
     nsent = 0
+    k_qbb = None
 
     for t in range(R):
         n = NT[t]
+        u = t + 1
         end = Z0 + Q0[t] + n
-        k = turn(lambda a, b: V("xs", t, a, b), lambda a, b: V("tx", t, a, b), P, [k_num])
+        k = turn(lambda a, b: V("xs", t, a, b), lambda a, b: V("tx", t, a, b), P, [kn["put"]])
         w = 2 * P + 32
-        k_lo = scan(V("lo", t, 0, w), V("tx", t, 0, w), T.sm[:, 16:16 + w], BIG, OP.min, OP.max, [k, s_sm])
+        if t < R - 1:
+            k_inc = tt(V("inc", u, 0, 56), T.pik[:, 1:57], T.pik[:, 0:56], OP.subtract, [k_p0])
+        k_lo = scan(V("lo", t, 0, w // 8), V("tx", t, 7, w, 8), T.sm[:, 23:16 + w:8], BIG, OP.min, OP.max, [k, s_sm])
         k_hi = scan(V("hi", t, 0, w), V("tx", t, 0, w), T.sm[:, 0:w], 0.0, OP.max, OP.min, [])
-        k_lo = tt(V("fv", t, 0, 14), V("lo", t, 15, P, 16), V("lo", t, P + 31, w - 16, 16), OP.min, [k_lo])
-        k_hi = tt(V("fv", t, 16, 30), V("hi", t, 15, P, 16), V("hi", t, P + 31, w - 16, 16), OP.max, [k_hi])
+        k_lo = tt(V("fv", t, 0, 14), V("lo", t, 1, P // 8, 2), V("lo", t, P // 8 + 3, w // 8 - 2, 2), OP.min, [k_lo])
         s_lo = act(V("lg", t, 0, 14), V("fv", t, 0, 14), AF.Ln, [k_lo])
+        if t < R - 1:
+            k3 = ms(V("tw", t, 0, 1), 0.0)
+        k_hi = tt(V("fv", t, 16, 30), V("hi", t, 15, P, 16), V("hi", t, P + 31, w - 16, 16), OP.max, [k_hi])
         s_hi = act(V("lg", t, 16, 30), V("fv", t, 16, 30), AF.Ln, [k_hi])
         if t < R - 1:
-            k3 = ts(V("tw", t, 0, 14), V("fv", t, 0, 14), T.nam[:, 0:1], 2.0 ** 22, OP.is_ge, OP.mult, [k_lo])
+            k3 = ts(V("tw", t, 1, 15), V("fv", t, 0, 14), T.nam[:, 0:1], GONE, OP.is_ge, OP.mult, [k_lo])
         else:
             k3 = ts(T.hf[:, 0:14], V("fv", t, 0, 14), T.nam[:, 0:1], None, OP.is_lt, None, [k_lo])
         ko = ts(V("ofs", t, 0, 14), V("lg", t, 0, 14), T.ln0[:], -LAM, OP.subtract, OP.mult, [s_lo, s_ln])
-        kj = ts(V("ofs", t, 14, 28), V("lg", t, 16, 30), T.ln0[:], -LAM, OP.subtract, OP.mult, [s_hi])
-        s1 = [act(V("tmp", t, P * e, P * e + P), plane(e, 0, end).indirect(V("ofs", t, 0, 14)), AF.Copy,
-                  [ko] + pool_deps) for e in range(4)]
         if t < R - 1:
-            k_w = tt(V("tw", t, 16, 30), T.tw0[:, 0:14], V("tw", t, 0, 14), OP.add, [k3, k_tw])
-            k_xs.append(act(V("xs", t + 1, 0, 256), T.rin[:, 0:256], AF.Identity, [], scale=0.0, bias=T.nam[:, 0:1]))
+            k4 = tt(V("tw", t, 16, 30), V("tw", t, 0, 14), V("tw", t, 1, 15), OP.subtract, [k3])
+        kj = ts(V("ofs", t, 14, 28), V("lg", t, 16, 30), T.ln0[:], -LAM, OP.subtract, OP.mult, [s_hi])
+        s1 = [[act(V("tmp", t, P * e + a, P * e + b), plane(e, 0, end).indirect(V("ofs", t, a // 16, b // 16)), AF.Copy,
+                   [ko] + pool_deps) for e in range(4)] for a, b in RUNS]
+        if t < R - 1:
+            k_w = tt(V("tw", t, 32, 46), T.tab[:, 0:14], V("tw", t, 1, 15), OP.add, [])
+            k_inc = tt(V("inc", u, 0, 56, 4), V("inc", u, 0, 56, 4), V("tw", t, 16, 30), OP.add, [k4, k_inc])
+            hh, qh, sh = T["hh%d" % t], T["qh%d" % t], T["sh%d" % t]
+            k_bz = [ms(V("bt", u, P, 512), 0.0), ms(hh[:, 4 * P:1024], 0.0)]
         else:
             s_have = act(T.ocb[:, A:A + P], T.t01[:].indirect(T.hf[:, 0:14]), AF.Copy, [k3, k_01])
             dma("y", T.occ[:], T.ocb[0:128:16, :], "do", [s_have, s_occ])
             k = qz(T.qt[:, 0:A], T.sct[:, 0:A], T.tt[:, 0:4 * A], s_t)
             dma("y", T.oc[:, 0:4 * A], T.qt[:, 0:A].bitcast(dt.uint8), "do", [k])
-            p_y = mm(T.py[:, 0:A], T.qv[:], T.sv[:], T.qt[:, 0:A], T.sct[:, 0:A], [k, k_qv])
-        run(qe_jobs, 2)
-        for e in range(4):
-            k = tt(V("bb", t, e, 4 * P, 4), plane(e, 0, end).indirect(V("ofs", t, 14, 28)),
-                   V("tmp", t, P * e, P * e + P), OP.add, [s1[e], kj] + pool_deps)
-        k = qz(V("qbb", t, 0, P), V("sbb", t, 0, P), V("bb", t, 0, 4 * P), [k])
-        pw = [mm(T.pw[:, 512 * b:512 * b + P], T.qw[:, 128 * b:128 * b + 128], T.sw[:, 128 * b:128 * b + 128],
-                 V("qbb", t, 0, P), V("sbb", t, 0, P), [k, dw] + pw_free) for b in range(4)]
+            p_y = mm(7, T.qv[:], T.sv[:], T.qt[:, 0:A], T.sct[:, 0:A], A, [k, k_qv])
+            s_y = used(7, act(T.ysb[:, 0:A], bank(7, A), AF.Copy, [p_y]))
+            dma("y", T.y[:, 0:A], T.ysb[:, 0:A], "do", [s_y])
+            k_bz = [ms(T.tt[:, 4 * (A + P):4 * (A + 256)], 0.0)]
+        pw = []
+        for h, (a, b) in enumerate(RUNS):
+            for e in range(4):
+                k = tt(T.bb[:, 4 * a + e:4 * b:4], plane(e, 0, end).indirect(V("ofs", t, 14 + a // 16, 14 + b // 16)),
+                       V("tmp", t, P * e + a, P * e + b), OP.add, [s1[h][e], kj, k_qbb] + pool_deps)
+            k = qz(V("qbb", t, a, a + 128), V("sbb", t, a, a + 128), T.bb[:, 4 * a:4 * a + 512], [k] + k_pad)
+            pw.append([mm(4 * h + j, T.qw[:, 128 * j:128 * j + 128], T.sw[:, 128 * j:128 * j + 128],
+                          V("qbb", t, a, a + 128), V("sbb", t, a, a + 128), 128, [k, dw]) for j in range(4)])
+        k_qbb = k
         if t == R - 1:
             break
-        if t == 0:
-            k = ts(T.ca[:], T.gro[:], fg, vp, OP.is_equal, OP.mult, [g_g])
-        else:
-            k_qv = qz(T.qv[:], T.sv[:], T.vin[:], [dv])
-            ms(T.t01[:, 0:1], 0.0)
-            k_01 = ms(T.t01[:, 1:16], 1.0)
-        hh, qh, sh = T["hh%d" % t], T["qh%d" % t], T["sh%d" % t]
-        ev = []
-        for b in range(4):
-            if b % 2:
-                ev.append(ts(hh[:, b:4 * P:4], T.pw[:, 512 * b:512 * b + P], 0.0, 0.03125, OP.max, OP.mult, [pw[b]]))
+        ev = [used(j, act(hh[:, j:512:4], bank(j, 128), AF.Relu, [pw[0][j]], scale=0.03125)) for j in range(4)]
+        ka = qz(qh[:, 0:128], sh[:, 0:128], hh[:, 0:512], ev)
+        pa = mm(0, T.qu[:], T.su[:], qh[:, 0:128], sh[:, 0:128], 128, [ka])
+        for j in range(4):
+            if j % 2:
+                ev.append(used(4 + j, ts(hh[:, 512 + j:4 * P:4], bank(4 + j, P - 128), 0.0, 0.03125, OP.max, OP.mult,
+                                         [pw[1][j]])))
             else:
-                ev.append(act(hh[:, b:4 * P:4], T.pw[:, 512 * b:512 * b + P], AF.Relu, [pw[b]], scale=0.03125))
-        k_qh = qz(qh[:], sh[:], hh[:], ev)
+                ev.append(used(4 + j, act(hh[:, 512 + j:4 * P:4], bank(4 + j, P - 128), AF.Relu, [pw[1][j]], scale=0.03125)))
+        k_qh = qz(qh[:, 128:256], sh[:, 128:256], hh[:, 512:1024], ev + k_bz)
+        pb = mm(1, T.qu[:], T.su[:], qh[:, 128:256], sh[:, 128:256], 128, [k_qh])
         s_h = [act(plane(e, end, end + P), hh[:, e:4 * P:4], AF.Copy, ev, scale=0.5) for e in range(4)]
         mate = T.cores[rank ^ (1 << t)]
         rid, pid, _ = topo.addr(mate)
         em, ne = topo.mask(core, mate), len(topo.engines(core, mate))
         wait("g", [k_qh])
-        g.remote_dma(T["ls%d" % t][:], sh[:], T.sem["ac%d" % t], T.sem.sent, pid, rid, em)
-        u = t + 1
-        p = mm(T.ps[:, 0:P], T.qu[:], T.su[:], qh[:], sh[:], [k_qh, k_bits])
+        g.remote_dma(T["ls%d" % t][:], sh[:, 0:P], T.sem["ac%d" % t], T.sem.sent, pid, rid, em)
+        ka = used(0, ts(V("bt", u, 0, 128), bank(0, 128), 0.0, None, OP.is_gt, None, [pa]))
         if t == 0:
-            k_qa = qz(T.qc[:, 128:256], T.sc[:, 128:256], T.ca[:], [k])
-        k_bits = ts(V("bt", u, 0, P), T.ps[:, 0:P], 0.0, None, OP.is_gt, None, [p])
-        k = qz(V("qb", u, 0, 128), V("sb", u, 0, 128), V("bt", u, 0, 512), [k_bits] + k_bz)
-        pa = mm(T.pa[:, 0:128], T.qc[:, 128:256], T.sc[:, 128:256], V("qb", u, 0, 128), V("sb", u, 0, 128), [k, k_qa, k_pa])
-        pb = mm(T.pb[:, 0:128], T.qc[:, 0:128], T.sc[:, 0:128], V("qb", u, 0, 128), V("sb", u, 0, 128), [k, k_pb])
+            k_ca = ts(T.ca[:], T.gro[:], fg, vp, OP.is_equal, OP.mult, [g_g])
+        else:
+            k_qv = qz(T.qv[:], T.sv[:], T.vin[:], [dv])
+        kc = used(1, ts(V("bt", u, 128, P), bank(1, P - 128), 0.0, None, OP.is_gt, None, [pb]))
+        if t == 0:
+            k_qa = qz(T.qc[:, 128:256], T.sc[:, 128:256], T.ca[:], [k_ca])
+        k = qz(V("qb", u, 0, 128), V("sb", u, 0, 128), V("bt", u, 0, 512), [ka, kc])
+        pa = mm(2, T.qc[:, 128:256], T.sc[:, 128:256], V("qb", u, 0, 128), V("sb", u, 0, 128), 128, [k, k_qa])
+        pb = mm(3, T.qc[:, 0:128], T.sc[:, 0:128], V("qb", u, 0, 128), V("sb", u, 0, 128), 128, [k])
+        if t == 0:
+            run(qe_jobs, 2)
+        else:
+            ms(T.t01[:, 0:1], 0.0)
+            k_01 = ms(T.t01[:, 1:16], 1.0)
+        k = used(2, scan(V("ii", u, 0, 56), bank(2, 56), V("inc", u, 0, 56), 384.0 - L - 1, OP.add, OP.add, [pa, k_inc]))
         run(qe_jobs, 1)
-        k_pa = scan(V("ii", u, 0, 56), T.pa[:, 0:56], T.c64[:, 0:56], 384.0 - L - 1, OP.add, OP.add, [pa])
-        k_pb = tt(V("vl", u, 0, 56), T.pb[:, 0:56], V("ii", u, 0, 56), OP.add, [pb, k_pa])
-        k = scan(V("sl", u, 0, 56), T.msk[:, 0:56], V("vl", u, 0, 56), 0.0, OP.max, OP.min, [k_pb])
+        k = used(3, tt(V("vl", u, 0, 56), bank(3, 56), V("ii", u, 0, 56), OP.add, [pb, k]))
+        run(qe_jobs, 1)
+        k = scan(V("sl", u, 0, 56), T.m01[:, 0:56], V("vl", u, 0, 56), 0.0, OP.mult, OP.min, [k])
         msg, ll = T["msg%d" % t], T["ll%d" % t]
-        k1 = tt(V("pk", u, 0, 14), V("sl", u, 3, 56, 4), V("tw", t, 16, 30), OP.subtract, [k, k_w])
-        k2 = ts(msg[:, 14:28], V("sl", u, 3, 56, 4), 1.0 / (16 * AW), c2, OP.mult, OP.add, [])
-        k1 = ts(msg[:, 0:14], V("pk", u, 0, 14), 1.0 / 256, -0.498, OP.mult, OP.add, [k1])
-        wait("g", [k1])
+        k1 = ts(msg[:, 0:14], V("sl", u, 3, 56, 4), PICK + AW - 127.5, 1.0 / 256, OP.add, OP.mult, [k])
+        k2 = tt(V("pk", u, 0, 14), V("sl", u, 3, 56, 4), V("tw", t, 32, 46), OP.add, [k_w])
+        k2 = ts(msg[:, 14:28], V("pk", u, 0, 14), 1.0 / (16 * AW), -0.504, OP.mult, OP.add, [k2])
+        wait("g", [k2])
         g.remote_dma(ll[:], msg[:], T.sem["al%d" % t], T.sem.sent, pid, rid, em)
-        g.remote_dma(T["lq%d" % t][:].bitcast(dt.uint8), qh[:].bitcast(dt.uint8), T.sem["ac%d" % t], T.sem.sent, pid, rid, em)
+        g.remote_dma(T["lq%d" % t][:].bitcast(dt.uint8), qh[:, 0:P].bitcast(dt.uint8), T.sem["ac%d" % t], T.sem.sent,
+                     pid, rid, em)
         nsent += 3 * ne
-        run(qe_jobs, 1)
         k_sc = scans_by_twos(u, P, msg[:, 0:14], [k1], lambda m: V("st", t, 8 * (n - 1) + m, 8 * (n - 1) + m + 1),
                              [k_sc, s_n1])
         al, ac = ("al%d" % t, ne), ("ac%d" % t, 2 * ne)
-        jobs = scans_by_ones(u, P, P, ll[:, 0:14], [al], [k_sc])
-        k_own = number(u, 0, P, msg[:, 14:28], [k_sc], None, jobs, [1, 1, 1, 1, 1, 1, 0, 1])
-        k_sc = run(jobs) or k_own
-        pd = [mm(T.pw[:, 512 * b:512 * b + P], T.qe[:, 128 * b:128 * b + 128], T.se[:, 128 * b:128 * b + 128],
-                 T["lq%d" % t][:], T["ls%d" % t][:], [ac] + k_qe + ev) for b in range(4)]
-        pw_free = [act(plane(b, end + P, end + 2 * P), T.pw[:, 512 * b:512 * b + P], AF.Copy,
-                       [pd[b]], scale=0.5) for b in range(4)]
-        pool_deps = pw_free + s_h
+        last = []
+        scans = scans_by_ones(u, P, P, ll[:, 0:14], [al], [k_sc], last)
+        pd = [mm(4 + b, T.qe[:, 128 * b:128 * b + 128], T.se[:, 128 * b:128 * b + 128],
+                 T["lq%d" % t][:], T["ls%d" % t][:], P, [ac] + k_qe) for b in range(4)]
+        s_d = [used(4 + b, act(plane(b, end + P, end + 2 * P), bank(4 + b, P), AF.Copy, [pd[b]], scale=0.5))
+               for b in range(4)]
+        pool_deps = s_d + s_h
         jobs = []
         if u == R - 1:
             fin = V("st", u, 8 * (2 * P - 1), 16 * P)
             tok = {}
 
             def fin_a():
-                k = ts(T.wa[:], fin, -1.0, T.nam[:, ZE:ZE + 1], OP.mult, OP.max, [k_sc])
+                k = ts(T.wa[:], fin, -1.0, T.nam[:, ZE:ZE + 1], OP.mult, OP.max, last)
                 tok["l"] = act(T.wl[:], T.wa[:], AF.Ln, [k])
-                tok["f"] = ts(T.wo[:, 8:16], fin, 0.0, None, OP.is_lt, None, [])
 
             def fin_b():
+                tok["f"] = ts(T.wo[:, 8:16], fin, 0.0, None, OP.is_lt, None, [])
+
+            def fin_c():
                 tok["w"] = ts(T.wo[:, 0:8], T.wl[:], T.ln0[:], -LAM, OP.subtract, OP.mult, [tok["l"]])
-            jobs = [fin_a, fin_b]
-        k_num = number(u, P, P, ll[:, 14:28], [k_sc, k_own, al], k_own, jobs, [1, 0, 0, 0, 1, 0, 0, 0])
+            jobs = [fin_a, fin_b, fin_c]
+        kn = {}
+        last.append(al)
+        a, c = number(u, 0, P, msg[:, 14:28], [k_sc, k2], [0, 4, 6, 8, 10, 12, 14], kn)
+        d, e = number(u, P, P, ll[:, 14:28], last, [0, 14], kn)
+        weave(WEAVE, {"a": a, "b": scans, "c": c, "d": d, "e": e, "f": jobs})
+        k_sc = last[-1]
         if u == R - 1:
             s_t = [act(T.tt[:, e:4 * A:4], plane(e, 0, ZE + 1).indirect(T.wo[:, 0:8]), AF.Copy,
                        [tok["w"]] + pool_deps, scale=2.0) for e in range(4)]
             s_occ = act(T.ocb[:, 0:A], T.t01[:].indirect(T.wo[:, 8:16]), AF.Copy, [tok["f"], k_01])
 
-    s_y = act(T.ysb[:, 0:A], T.py[:, 0:A], AF.Copy, [p_y])
-    dma("y", T.y[:, 0:A], T.ysb[:, 0:A], "do", [s_y])
-    ev = []
-    for b in range(4):
-        k = tt(T.hm[:, P * b:P * b + P], T.pw[:, 512 * b:512 * b + P], T.ocb[:, A:A + P], OP.mult, [pw[b], s_have])
-        if b < 3:
-            ev.append(act(T.tt[:, 4 * A + b:4 * (A + P):4], T.hm[:, P * b:P * b + P], AF.Relu, [k], scale=0.03125))
+    for h, (a, b) in enumerate(RUNS):
+        ev = []
+        for j in range(4):
+            m = T.hm[:, P * j + a:P * j + b]
+            o = T.tt[:, 4 * (A + a) + j:4 * (A + b):4]
+            k = used(4 * h + j, tt(m, bank(4 * h + j, b - a), T.ocb[:, A + a:A + b], OP.mult, [pw[h][j], s_have]))
+            if j < 3 or not h:
+                ev.append(act(o, m, AF.Relu, [k], scale=0.03125))
+            else:
+                if h:
+                    first()
+                ev.append(ts(o, m, 0.0, 0.03125, OP.max, OP.mult, [k]))
+
+        def out(h=h, a=a, b=b, ev=ev):
+            k = qz(T.qt[:, A + a:A + a + 128], T.sct[:, A + a:A + a + 128], T.tt[:, 4 * (A + a):4 * (A + a) + 512], ev + k_bz)
+            p = mm(h, T.qv[:], T.sv[:], T.qt[:, A + a:A + a + 128], T.sct[:, A + a:A + a + 128], 128, [k])
+            dma("y", T.oc[:, 4 * (A + a):4 * (A + b)], T.qt[:, A + a:A + b].bitcast(dt.uint8), "do", [k])
+            return k, p
+        if not h:
+            res = []
+
+            def first(out=out):
+                res.append(out())
         else:
-            ev.append(ts(T.tt[:, 4 * A + b:4 * (A + P):4], T.hm[:, P * b:P * b + P], 0.0, 0.03125, OP.max, OP.mult, [k]))
-    k = qz(T.qt[:, A:A + P], T.sct[:, A:A + P], T.tt[:, 4 * A:4 * (A + P)], ev)
-    p = mm(T.ps[:, 0:P], T.qv[:], T.sv[:], T.qt[:, A:A + P], T.sct[:, A:A + P], [k, k_bits])
-    dma("y", T.oc[:, 4 * A:4 * (A + P)], T.qt[:, A:A + P].bitcast(dt.uint8), "do", [k])
+            res.append(out())
+    (ka, pa), (kc, pb) = res
+    k = act(T.ysb[:, A:A + 128], bank(0, 128), AF.Copy, [pa])
+    dma("s", T.y[:, A:A + 128], T.ysb[:, A:A + 128], "do", [k])
     for j in range(4):
-        dma("s" if j < 2 else "y", T.osc[4 * j:4 * j + 4, :], T.sct[32 * j:32 * j + 4, :], "do", [k])
-    k = cp(T.ysb[:, A:A + P], T.ps[:, 0:P], [p])
-    dma("s", T.y[:, A:A + P], T.ysb[:, A:A + P], "do", [k])
+        dma("s" if j < 2 else "y", T.osc[4 * j:4 * j + 4, :], T.sct[32 * j:32 * j + 4, 0:A + P], "do", [kc])
+    k = cp(T.ysb[:, A + 128:A + P], bank(1, P - 128), [pb])
+    dma("s", T.y[:, A + 128:A + P], T.ysb[:, A + 128:A + P], "do", [k])
     wait("g", [(s, c) for s, c in cnt.items()] + [("sent", nsent)])

@@ -16,6 +16,14 @@ AW = 512.0
 W0, W1, TW = 224, 192, 272
 DUMP = P + L
 RUNS = [(0, 128), (128, P)]
+WEAVE0 = "ayabababababbabb" + "cdzdzdcdcdfdfdfe"
+WEAVE = "mmammmmmmmmyaya" + "sasbasabsabbabbbb" + "cdfdzdzdcdfdcdfe"
+CUTS0 = [[0, 16], [0, 8, 12, 16], [0, 8, 16]]
+CUTS = [[0, 8, 14], [0, 6, 10, 14], [0, 8, 14]]
+TWOS0, TWOS = 0, 2
+MID = 2
+LAST = RUNS
+WEAVE1 = "opoopqoopqpopqpjqqjqjqqjqjjjjjjjjj"
 H16 = "float16"
 CD, U8, BF, F32, I32, U16 = "float8_e4m3fn_x4", "uint8", "bfloat16", "float32", "int32", "uint16"
 
@@ -31,23 +39,23 @@ for _n, _c, _d in [
     ("vin", 512, BF), ("qv", 128, CD), ("sv", 128, U8), ("qw", 512, CD), ("sw", 512, U8),
     ("pool", 4 * PW, BF), ("gb", C + 16, H16), ("vv", C + 32, H16),
     ("pcol", 1, I32), ("ci", 4, I32), ("cf", 4, F32), ("cx", 12, F32), ("lt", 8, F32), ("pw2", 8, F32),
-    ("d64", 64, BF), ("pat", 192, BF), ("i16", 16, F32), ("gm", 16, F32), ("c4", 128, BF), ("raw", 34, F32),
+    ("d64", 64, BF), ("pat", 192, BF), ("i16", 16, F32), ("gm", 16, F32), ("c4", 64, BF), ("raw", 34, F32),
     ("cb", 512, BF), ("ca", 512, BF), ("gro", 512, BF), ("qc", 256, CD), ("sc", 256, U8),
     ("eb", 516, BF), ("qe", 512, CD), ("se", 512, U8),
-    ("m01", 128, BF), ("pik", 130, F32), ("st", 8 * NQ, BF), ("sg16", 16, BF),
-    ("one", W0 + TW, BF), ("two", W1 + TW, BF), ("tab", 32, F32), ("smr", 544, BF), ("sm", 544, BF),
+    ("m01", 64, BF), ("pik", 66, F32), ("bt", 512, BF), ("bu", 512, BF), ("st", 8 * NQ, BF), ("sg16", 16, BF),
+    ("one", W0 + TW, BF), ("odd", W0 + TW, BF), ("twe", W1 + TW, BF), ("two", W1 + TW, BF), ("tab", 32, F32), ("smr", 544, BF), ("sm", 544, BF),
     ("cap", 544, H16), ("dmp", 34, F32), ("rin", PW, F32), ("nam", PW, BF), ("t01", 16, F32), ("ln0", 1, F32),
-    ("tt", 4 * (A + 256), BF), ("qt", A + 256, CD), ("sct", A + 256, U8), ("ysb", A + P, F32), ("ocb", A + P, F32),
+    ("tt", 4 * (A + 288), BF), ("qt", A + 288, CD), ("sct", A + 288, U8), ("ysb", A + P, F32), ("ocb", A + P, F32),
     ("hm", 4 * P, F32), ("wa", 8, F32), ("wl", 8, F32), ("wo", 16, U16), ("hf", 16, U16),
-    ("bb", 1024, BF), ("au", 64, U16),
+    ("bb", 4 * 288, BF), ("au", 64, U16),
 ]:
     _sb(_n, _c, _d)
-WID = {"bt": (512, BF), "qb": (128, CD), "sb": (128, U8), "ii": (64, F32), "vl": (128, F32), "sl": (128, F32),
-       "pk": (32, F32), "ee": (4 * 256, BF), "sig": (8 * C, BF), "zz": (C, BF), "inc": (64, BF),
+WID = {"qb": (256, CD), "sb": (256, U8), "ii": (128, F32), "vl": (128, F32), "sl": (128, F32),
+       "pk": (32, F32), "ee": (4 * 256, BF), "ef": (4 * 256, BF), "sig": (8 * C, BF), "zz": (C, BF), "gg": (256, BF), "inc": (64, F32),
        "ga": (C, H16), "tr": (1088, H16), "ss": (1088, H16),
-       "vk": (48, F32), "de": (32, U16), "xs": (896, BF), "tx": (480, BF), "lo": (64, BF), "hi": (480, BF),
-       "fv": (32, F32), "lg": (32, F32), "ofs": (28, U16), "tmp": (4 * P, BF), "qbb": (256, CD),
-       "sbb": (256, U8), "tw": (48, F32)}
+       "vk": (48, F32), "de": (32, U16), "xs": (896, BF), "tx": (512, BF), "lo": (64, BF), "hi": (512, BF),
+       "fv": (32, F32), "lg": (32, F32), "ofs": (28, U16), "tmp": (4 * P, BF), "qbb": (288, CD),
+       "sbb": (288, U8), "tw": (48, F32)}
 for _n, (_c, _d) in WID.items():
     _sb(_n, R * _c, _d)
 for _t in range(2):
@@ -158,7 +166,7 @@ def rank_program(g, core, T, topo):
             run(lists[c], 1)
 
     du = dma("y", T.uin[:], T.u[:], "du", [])
-    dxa = dma("s", T.xin[:, 0:2 * C], T.x[:, 0:2 * C], "dxa", [])
+    dxa = dma("y", T.xin[:, 0:2 * C], T.x[:, 0:2 * C], "dxa", [])
     dxb = dma("y", T.xin[:, 2 * C:4 * C], T.x[:, 2 * C:4 * C], "dxb", [])
     dma("y", T.qw[:].bitcast(dt.uint8), T.wc[:], "dw", [dxa, dxb])
     dw = dma("y", T.sw[:], T.ws[:], "dw", [])
@@ -168,27 +176,38 @@ def rank_program(g, core, T, topo):
     g_i = iota(T.i16[:], [[1, 16]], 0, 0)
     g_d = iota(T.d64[:], [[0, 4], [-1, 4], [1, 4]], 0, 0)
     g_r0 = iota(T.rin[:, 16:C + Z0], [[1, C + Z0 - 16]], 16, 0)
-    g_c = iota(T.c4[:], [[0, 32], [1, 4]], 0, 0)
-    g_two = iota(T.two[:], [[0, W1 + TW]], -1, 0)
+    g_c = iota(T.c4[:], [[0, 16], [1, 4]], 0, 0)
     g_r = iota(T.raw[:], [[16, 34]], DUMP, 0)
     g_sm = iota(T.smr[:], [[0, 17], [1, 2], [0, 16]], 0, 0)
-    g_one = iota(T.one[:], [[0, W0 + TW]], 1, 0)
+    g_odd = iota(T.odd[:], [[0, W0 + TW]], 1, 0)
     k_xs = [iota(V("xs", 0, 0, 256), [[0, 256]], NONE, 0)]
     g_r1 = iota(T.rin[:, C + Z0:PW], [[1, PW - C - Z0]], C + Z0, 0)
     g_e = iota(T.eb[:], [[0, 516]], 1, 0)
     wait("g", [g_e])
     g_e = done(g.affine_select(T.eb[:], T.eb[:], [[1, 516]], OP.is_equal, 0.0, -3, -4), "cg", 1)
     g_g = iota(T.gro[:], [[1, 8], [0, 64]], 0, 0)
+    iota(T.tw[:, 0:96:48], [[0, 2]], 0, 0)
+    k_z = [iota(T.pool[:, 0:4 * PW:PW], [[0, 4]], 0, 0), iota(T.pool[:, ZE:4 * PW:PW], [[0, 4]], 0, 0)]
+    k_pad = [iota(b[:, b.shape[1] - w:b.shape[1]], [[0, w]], 0, 0)
+             for b, w in ((T.bb, 256), (T.hh0, 128), (T.hh1, 128), (T.tt, 256))]
+    g_one = iota(T.one[:], [[0, W0 + TW]], 1, 0)
+    g_twe = iota(T.twe[:], [[0, W1 + TW]], -1, 0)
+    g_bu = iota(T.bu[:], [[0, 512]], 0, 0)
     k_xs += [iota(V("xs", t, 0, 256), [[0, 256]], NONE, 0) for t in (1, 2)]
 
     s_n0 = act(T.nam[:, 0:16], T.i16[:], AF.Exp, [g_i], scale=-1.0 / LAM, bias=TOP)
+    g_two = ms(T.two[:], -1.0)
     ts(T.ci[:, 0:1], T.pcol[:], 15, None, OP.bitwise_and, None, [g_p])
     ts(T.ci[:, 1:2], T.pcol[:], 4, 1, OP.arith_shift_right, OP.bitwise_and, [])
     ts(T.ci[:, 2:3], T.pcol[:], 4, None, OP.arith_shift_right, None, [])
     k = ts(T.ci[:, 3:4], T.pcol[:], 2, 3, OP.arith_shift_right, OP.bitwise_and, [])
+    k_bt = ms(T.bt[:, C // 2:C], 0.0)
     k_cf = cp(T.cf[:], T.ci[:], [k])
     fi, fh, fg, fq = (T.cf[:, j:j + 1] for j in range(4))
     w0, vp, w1, hb, q1 = (T.cx[:, j:j + 1] for j in range(5))
+
+    def signs_of(i, a, b, dep):
+        return used(i, ts(T.bt[:, a:b], bank(i, b - a), 0.0, None, OP.is_gt, None, [dep]))
     k = ts(T.lt[:], T.i16[:, 0:8], fi, 1.0, OP.is_lt, OP.add, [k_cf, g_i])
     k_vp = ts(vp, fi, 7.0, None, OP.is_equal, None, [])
     k_gm = ts(T.gm[:], T.i16[:], fg, None, OP.is_equal, None, [])
@@ -207,51 +226,85 @@ def rank_program(g, core, T, topo):
     kb = [act(T.cb[:, 64 * j:64 * j + 64], T.pat[:, 128:192], AF.Copy, [k_pat, k_gm], scale=T.gm[:, j:j + 1])
           for j in range(8)]
 
-    def sg(t, pos, n, m):
-        return V("sig", t, 8 * pos + m * n, 8 * pos + (m + 1) * n)
+    def sg(t, pos, n, m, w=1):
+        return V("sig", t, 8 * pos + m * n, 8 * pos + (m + w) * n)
 
-    def follow(t, pos, n, m, init, deps):
-        return scan(V("st", t, 8 * pos + m, 8 * (pos + n), 8), names(t, pos, n), sg(t, pos, n, m), init(m),
-                    OP.min, OP.mult, deps)
+    def follow(t, pos, n, m, init, deps, slot=None):
+        return scan(V("st", t, 8 * pos + m, 8 * (pos + n), 8), names(t, pos, n), sg(t, pos, n, m if slot is None else slot),
+                    init(m), OP.min, OP.mult, deps)
 
-    def scans_by_twos(t, n, offs, deps, init, ideps):
+    def scans_by_twos(t, pos, n, offs, deps, init, ideps, out, ones=None):
         def win(q):
             return T.two[:, W1 - 64 * q:W1 - 64 * q + TW].indirect(offs)
-        e = [act(V("ee", t, 256 * q, 256 * q + n), win(q), AF.Copy, deps + [k_two]) for q in range(3)]
-        e.append(cp(V("ee", t, 768, 768 + n), win(3), deps + [k_two]))
-        for q in range(4):
-            ka = ts(sg(t, 0, n, 2 * q), V("ee", t, 256 * q, 256 * q + n), -1.0, 2.0, OP.min, OP.add, [e[q]])
-            kc = ts(sg(t, 0, n, 2 * q + 1), V("ee", t, 256 * q, 256 * q + n), -1.0, -1.0, OP.max, OP.mult, [])
-            follow(t, 0, n, 2 * q, init, [ka] + ideps)
-            k = follow(t, 0, n, 2 * q + 1, init, [kc])
-        return k
 
-    def scans_by_ones(t, pos, n, offs, deps, ideps, out):
-        tok = [act(sg(t, pos, n, m), T.one[:, W0 - 32 * m:W0 - 32 * m + TW].indirect(offs), AF.Copy, deps)
-               for m in range(8)]
+        order = [0, 1, 2, 3] if ones else [0, 3, 1, 2]
+        slot = {2 * q + b: 4 * (j // 2) + 2 * b + j % 2 for j, q in enumerate(order) for b in (0, 1)}
+
+        def ee(j, w=1):
+            return V("ee", t, 4 * pos + j * n, 4 * pos + (j + w) * n)
+        k = {q: act(ee(order.index(q)), win(q), AF.Copy, deps + [k_two]) for q in range(2 if ones else 3)}
+        s = {m: act(sg(t, pos, n, slot[m]), T.odd[:, W0 - 32 * m:W0 - 32 * m + TW].indirect(offs), AF.Copy, deps + k_odd)
+             for m in range(4 if ones else 8, 8)}
+
+        def signs(j):
+            a, b = order[j:j + 2]
+
+            def first():
+                s[2 * a] = s[2 * b] = ts(sg(t, pos, n, 2 * j, 2), ee(j, 2), -1.0, 2.0, OP.min, OP.add, [k[a], k[b]])
+
+            def second():
+                s[2 * a + 1] = s[2 * b + 1] = ts(sg(t, pos, n, 2 * j + 2, 2), ee(j, 2), -1.0, -1.0, OP.max, OP.mult, [])
+            return [first, second]
+
+        def some(ms):
+            return [lambda m=m: out.append(follow(t, pos, n, m, init, [s[m]] + ideps, slot[m])) for m in ms]
+        if ones:
+            return signs(0) + some([0, 2, 1, 3, 4, 5, 6, 7])
+        return ([lambda: k.update({3: cp(ee(1), win(3), deps + [k_two])})] + signs(0) + some([0, 6]) + signs(2)
+                + some([1, 7, 2, 4, 3, 5]))
+
+    def before(t, pos):
+        return lambda m: V("st", t, 8 * (pos - 1) + m, 8 * (pos - 1) + m + 1)
+
+    def scans_by_ones(t, pos, n, offs, deps, ideps, out, twos):
+        one, two = (T.one, T.twe) if t else (T.odd, T.two)
+        got = [act(V("ef", t, 256 * q, 256 * q + n), two[:, W1 - 64 * q:W1 - 64 * q + TW].indirect(offs), AF.Copy, deps)
+               for q in range(twos)]
+        tok = {m: act(sg(t, pos, n, m), one[:, W0 - 32 * m:W0 - 32 * m + TW].indirect(offs), AF.Copy, deps)
+               for m in range(2 * twos, 8)}
 
         def job(m):
-            return lambda: out.append(follow(t, pos, n, m, lambda j: V("st", t, 8 * (pos - 1) + j, 8 * (pos - 1) + j + 1),
-                                             [tok[m]] + ideps))
-        return [job(m) for m in range(8)]
+            return lambda: out.append(follow(t, pos, n, m, before(t, pos), [tok[m]] + ideps))
+
+        def signs(q):
+            e = V("ef", t, 256 * q, 256 * q + n)
+            return [lambda: tok.update({2 * q: ts(sg(t, pos, n, 2 * q), e, -1.0, 2.0, OP.min, OP.add, [got[q]])}),
+                    lambda: tok.update({2 * q + 1: ts(sg(t, pos, n, 2 * q + 1), e, -1.0, -1.0, OP.max, OP.mult, [])})]
+        return [job(m) for m in range(8)], [j for q in range(twos) for j in signs(q)]
 
     def turn(src, tr, n, deps):
         trp(tr(0, n), src(16, 16 + n), deps)
         return trp(tr(n, 2 * n + 32), src(0, n + 32), [])
 
-    def number(t, pos, n, offs, deps, cuts, k):
-        z = V("zz", t, pos, pos + n)
+    def number(t, pos, n, offs, parts, zcuts, cuts, k):
         o, c = (544 if pos else 0), pos // 16
         d = c + n // 16
         init = V("vk", t, 40, 41) if pos else 1.0 / 16
 
-        def larger():
-            k[pos] = tt(z, V("st", t, 8 * pos if t else 0, 8 * (pos + n)).indirect(offs), names(t, pos, n), OP.max, deps)
-            if pos:
-                cp(init, T.vv[:, 15 + pos:16 + pos], [k[0]])
+        def own(a, b):
+            return V("st", t, 8 * pos if t else 0, 8 * (pos + b)).indirect(offs(a // 16, b // 16))
 
-        def second():
-            k[pos] = tt(V("ga", t, pos, pos + n), z, names(t, pos, n), OP.is_gt, [k[pos]])
+        def second(a, b, deps):
+            def job():
+                k[pos] = tt(V("ga", t, pos + a, pos + b), own(a, b), names(t, pos + a, b - a), OP.is_gt, deps)
+                if pos:
+                    cp(init, T.vv[:, 15 + pos:16 + pos], [k[0]])
+            return job
+
+        def larger(a, b):
+            def job():
+                k["z", pos] = tt(V("zz", t, pos + a, pos + b), own(a, b), names(t, pos + a, b - a), OP.max, [])
+            return job
 
         def back():
             k[pos] = ts(T.gb[:, pos + 1:pos + n + 1], V("ga", t, pos, pos + n), 1025.0 / 1024.0, None, OP.mult, None,
@@ -278,175 +331,255 @@ def rank_program(g, core, T, topo):
         def piece(a, b):
             def put():
                 k["put"] = cp(V("xs", t, 16, 896).indirect(V("de", t, c + a, c + b)),
-                              V("zz", t, pos + 16 * a, pos + 16 * b), [k[pos], k_xs[t], k.get("put")])
+                              V("zz", t, pos + 16 * a, pos + 16 * b), [k[pos], k["z", pos], k_xs[t], k.get("put")])
             return put
-        return ([larger, second, back, count, turned, summed, joined, places],
-                [piece(a, b) for a, b in zip(cuts, cuts[1:])])
+        return ([second(*p) for p in parts] + [back, count, turned, summed, joined, places],
+                [larger(16 * a, 16 * b) for a, b in zip(zcuts, zcuts[1:])], [piece(a, b) for a, b in zip(cuts, cuts[1:])])
 
-    WEAVE = "abababababababab" + "cdcdcdcdcdcdfdfdfe"
 
     hc = C // 2
     k_cap = [ms(T.cap[:], 60000.0)]
     k_qu = qz(T.qu[:], T.su[:], T.uin[:], [du])
-    ka = qz(T.qx[:, 0:hc], T.sx[:, 0:hc], T.xin[:, 0:2 * C], [dxa])
-    pa = mm(4, T.qu[:], T.su[:], T.qx[:, 0:hc], T.sx[:, 0:hc], hc, [ka, k_qu])
-    kc = qz(T.qx[:, hc:C], T.sx[:, hc:C], T.xin[:, 2 * C:4 * C], [dxb])
-    pb = mm(5, T.qu[:], T.su[:], T.qx[:, hc:C], T.sx[:, hc:C], hc, [kc])
-    s_x = [act(plane(0, Z0, Z0 + C), T.xin[:, 0:4 * C:4], AF.Copy, [dxa, dxb], scale=0.5)]
-    s_sm = act(T.sm[:], T.smr[:], AF.Abs, [g_sm, k_hb], bias=hb, scale=BIG)
-    ka = used(4, ts(V("bt", 0, 0, hc), bank(4, hc), 0.0, None, OP.is_gt, None, [pa]))
-    k_qb = qz(T.qc[:, 0:128], T.sc[:, 0:128], T.cb[:], kb)
-    kc = used(5, ts(V("bt", 0, hc, C), bank(5, hc), 0.0, None, OP.is_gt, None, [pb]))
-    k_pik = ts(T.pik[:, 1:129], T.c4[:], fq, -PICK, OP.is_equal, OP.mult, [g_c])
-    k = qz(V("qb", 0, 0, 128), V("sb", 0, 0, 128), V("bt", 0, 0, 512), [ka, kc])
-    p = mm(6, T.qc[:, 0:128], T.sc[:, 0:128], V("qb", 0, 0, 128), V("sb", 0, 0, 128), 128, [k, k_qb])
-    ts(T.two[:, W1 + 3:W1 + 35:2], T.sg16[:], -3.0, None, OP.add, None, [k_16, g_two])
-    k_two = ts(T.two[:, W1 + 35:W1 + 67:2], T.sg16[:], -1.0, 1.0, OP.mult, OP.add, [])
+    k = qz(T.qx[:, 0:hc], T.sx[:, 0:hc], T.xin[:, 0:2 * C], [dxa])
+    p = mm(4, T.qu[:], T.su[:], T.qx[:, 0:hc], T.sx[:, 0:hc], hc, [k, k_qu])
+    k_pik = ts(T.pik[:, 1:65], T.c4[:], fq, -PICK, OP.is_equal, OP.mult, [g_c])
     k_m = ts(T.m01[:], T.c4[:], 0.0, None, OP.is_gt, None, [])
-    k_tab = ts(T.tab[:], T.raw[:, 0:32], 128 * AW, q1, OP.mult, OP.add, [g_r, k_q])
-    k = used(6, tt(V("vl", 0, 0, 128), bank(6, 128), T.pik[:, 1:129], OP.add, [p, k_pik]))
-    k_du = ts(T.dmp[:], T.raw[:], fi, 1.0 / 1024, OP.add, OP.mult, [])
-    k = scan(V("sl", 0, 0, 128), T.m01[:], V("vl", 0, 0, 128), 0.0, OP.mult, OP.min, [k, k_m])
+    k_qb = qz(T.qc[:, 0:128], T.sc[:, 0:128], T.cb[:], kb)
     k_p0 = ms(T.pik[:, 0:1], 0.0)
+    ts(T.two[:, W1 + 3:W1 + 35:2], T.sg16[:], -3.0, None, OP.add, None, [k_16, g_two])
+    k = signs_of(4, 0, hc, p)
+    k_two = ts(T.two[:, W1 + 35:W1 + 67:2], T.sg16[:], -1.0, 1.0, OP.mult, OP.add, [])
+    k = qz(V("qb", 0, 0, 128), V("sb", 0, 0, 128), T.bt[:], [k, k_bt])
+    p = mm(6, T.qc[:, 0:128], T.sc[:, 0:128], V("qb", 0, 0, 128), V("sb", 0, 0, 128), 128, [k, k_qb])
+    k = qz(T.qx[:, hc:C], T.sx[:, hc:C], T.xin[:, 2 * C:4 * C], [dxb])
+    pb = mm(5, T.qu[:], T.su[:], T.qx[:, hc:C], T.sx[:, hc:C], hc, [k])
+    s_sm = act(T.sm[:], T.smr[:], AF.Abs, [g_sm, k_hb], bias=hb, scale=BIG)
+    s_x = []
+    k = used(6, tt(V("vl", 0, 0, 64), bank(6, 64), T.pik[:, 1:65], OP.add, [p, k_pik]))
+    k_tab = ts(T.tab[:], T.raw[:, 0:32], 128 * AW, q1, OP.mult, OP.add, [g_r, k_q])
+    k = scan(V("sl", 0, 0, 64), T.m01[:], V("vl", 0, 0, 64), 0.0, OP.mult, OP.min, [k, k_m])
+    k_du = ts(T.dmp[:], T.raw[:], fi, 1.0 / 1024, OP.add, OP.mult, [])
     k1 = ts(T.au[:, 0:16], V("sl", 0, 3, 64, 4), PICK + 456 + AW - 127.5, 1.0 / 256, OP.add, OP.mult, [k])
-    k1b = ts(T.au[:, 16:32], V("sl", 0, 67, 128, 4), PICK + 200 + AW - 127.5, 1.0 / 256, OP.add, OP.mult, [])
-    k2 = tt(V("pk", 0, 0, 32), V("sl", 0, 3, 128, 4), T.tab[:], OP.add, [k_tab])
-    k_one = ts(T.one[:, W0 + 2:W0 + 34:2], T.sg16[:], -1.0, None, OP.add, None, [g_one])
-    k_sc = scans_by_twos(0, hc, T.au[:, 0:16], [k1], lambda m: BIG, [s_n0])
-    k2 = ts(T.au[:, 32:64], V("pk", 0, 0, 32), 1.0 / (16 * AW), -0.47, OP.mult, OP.add, [k2])
+    k_sb = signs_of(5, hc, C, pb)
+    mine, last, k_odd = [], [], []
+    jobs = scans_by_twos(0, 0, hc, T.au[:, 0:16], [k1], lambda m: BIG, [s_n0], mine)
     k_cap = [tt(T.cap[:, 15:544:16], T.dmp[:], T.sm[:, 15:544:16], OP.min, k_cap + [k_du, s_sm])]
-    last = []
-    scans = scans_by_ones(0, hc, hc, T.au[:, 16:32], [k1b, k_one], [k_sc], last)
+    k = qz(V("qb", 0, 128, 256), V("sb", 0, 128, 256), T.bt[:], [k_sb])
+    p = mm(7, T.qc[:, 0:128], T.sc[:, 0:128], V("qb", 0, 128, 256), V("sb", 0, 128, 256), 128, [k])
+    run(jobs, 1)
+    k = used(7, tt(V("vl", 0, 64, 128), T.pm[:, 512 * 7 + 64:512 * 7 + 128], T.pik[:, 1:65], OP.add, [p]))
+    run(jobs, 1)
+    k = scan(V("sl", 0, 64, 128), T.m01[:], V("vl", 0, 64, 128), 0.0, OP.mult, OP.min, [k])
+    run(jobs, 1)
+    k1b = ts(T.au[:, 16:32], V("sl", 0, 67, 128, 4), PICK + 456 + AW - 127.5, 1.0 / 256, OP.add, OP.mult, [k])
+    k_odd.append(ts(T.odd[:, W0 + 3:W0 + 35:2], T.sg16[:], -1.0, None, OP.add, None, [g_odd]))
+    scans, signs = scans_by_ones(0, hc, hc, T.au[:, 16:32], [k1b] + k_odd, mine, last, TWOS0)
+    run(jobs, 2)
+    k2 = tt(V("pk", 0, 0, 32), V("sl", 0, 3, 128, 4), T.tab[:], OP.add, [k_tab])
+    run(jobs, 6)
+    k2 = ts(T.au[:, 32:64], V("pk", 0, 0, 32), 1.0 / (16 * AW), -0.47, OP.mult, OP.add, [k2])
+    run(jobs)
+    k_sc = mine[-1]
     s_n1 = act(T.nam[:, C + Z0:PW], T.rin[:, C + Z0:PW], AF.Exp, [g_r1], scale=-1.0 / LAM, bias=TOP)
-    s_ln = act(T.ln0[:], T.nam[:, 0:1], AF.Ln, [])
-    s_x += [act(plane(e, Z0, Z0 + C), T.xin[:, e:4 * C:4], AF.Copy, [], scale=0.5) for e in range(1, 4)]
-    k_z, k_pad = [], []
-    kn = {}
-    a, c = number(0, 0, hc, T.au[:, 32:48], [k_sc, k2], [0, 4, 8, 10, 12, 14, 16], kn)
-    d, e = number(0, hc, hc, T.au[:, 48:64], last, [0, 16], kn)
-    weave(WEAVE, {"a": a, "b": scans, "c": c, "d": d, "e": e,
-                  "f": [lambda: k_z.append(ms(T.pool[:, 0:4 * PW:PW], 0.0)),
-                        lambda: k_z.append(ms(T.pool[:, ZE:4 * PW:PW], 0.0)),
-                        lambda: k_pad.append(ms(T.bb[:, 4 * P:1024], 0.0))]})
-    k_sc = last[-1]
-    pool_deps = k_z + s_x
+
+    def halved_x():
+        s_x.append(act(T.ln0[:], T.nam[:, 0:1], AF.Ln, []))
+        s_x.extend(act(plane(e, Z0, Z0 + C), T.xin[:, e:4 * C:4], AF.Copy, [dxa, dxb], scale=0.5) for e in range(4))
     k_qe = []
 
     def qe_job(b):
         return lambda: k_qe.append(qz(T.qe[:, 128 * b:128 * b + 128], T.se[:, 128 * b:128 * b + 128],
                                       T.eb[:, 3 - b:515 - b], [g_e]))
     qe_jobs = [qe_job(b) for b in range(4)]
+    kn = {}
+    a, y, c = number(0, 0, hc, lambda a, b: T.au[:, 32 + a:32 + b], [(0, hc, [k_sc, k2])], CUTS0[0], CUTS0[1], kn)
+    d, z, e = number(0, hc, hc, lambda a, b: T.au[:, 48 + a:48 + b], [(0, hc, last)], CUTS0[2], [0, 16], kn)
+    k_qa = []
+    jobs = [lambda: k_qa.append(ts(T.ca[:], T.gro[:], fg, vp, OP.is_equal, OP.mult, [g_g])), qe_jobs.pop(),
+            lambda: k_qa.append(qz(T.qc[:, 128:256], T.sc[:, 128:256], T.ca[:], k_qa))]
+    halved_x()
+    weave(WEAVE0, {"a": a, "b": scans, "c": c, "d": d, "e": e, "f": jobs, "y": y, "z": z, "s": signs})
+    s_ln = s_x[0]
+    k_sc = last[-1]
+    pool_deps = k_z + s_x
     nsent = 0
     k_qbb = None
+    k_01, k_qv, k_twe = [], [], []
 
     for t in range(R):
         n = NT[t]
         u = t + 1
         end = Z0 + Q0[t] + n
-        k = turn(lambda a, b: V("xs", t, a, b), lambda a, b: V("tx", t, a, b), P, [kn["put"]])
-        w = 2 * P + 32
+        runs = RUNS if t < R - 1 else LAST
+        na = runs[0][1]
+        ca, ob = na // 16, 2 * na + 32
         if t < R - 1:
             k_inc = tt(V("inc", u, 0, 56), T.pik[:, 1:57], T.pik[:, 0:56], OP.subtract, [k_p0])
-        k_lo = scan(V("lo", t, 0, w // 8), V("tx", t, 7, w, 8), T.sm[:, 23:16 + w:8], BIG, OP.min, OP.max, [k, s_sm])
-        k_hi = scan(V("hi", t, 0, w), V("tx", t, 0, w), T.sm[:, 0:w], 0.0, OP.max, OP.min, [])
-        k_lo = tt(V("fv", t, 0, 14), V("lo", t, 1, P // 8, 2), V("lo", t, P // 8 + 3, w // 8 - 2, 2), OP.min, [k_lo])
-        s_lo = act(V("lg", t, 0, 14), V("fv", t, 0, 14), AF.Ln, [k_lo])
+        kt = [turn(lambda c, d: V("xs", t, a + c, a + d), lambda c, d: V("tx", t, o + c, o + d), b - a, [kn["put"]])
+              for (a, b), o in zip(runs, (0, ob))]
+
+        def lo(o, n, dep):
+            return scan(V("lo", t, o // 8, (o + 2 * n + 32) // 8), V("tx", t, o + 7, o + 2 * n + 32, 8),
+                        T.sm[:, 23:48 + 2 * n:8], BIG, OP.min, OP.max, [dep, s_sm])
+
+        def hi(o, n):
+            return scan(V("hi", t, o, o + 2 * n + 32), V("tx", t, o, o + 2 * n + 32), T.sm[:, 0:2 * n + 32], 0.0,
+                        OP.max, OP.min, [])
+
+        def lo2(c, o, n, dep):
+            return tt(V("fv", t, c, c + n // 16), V("lo", t, o // 8 + 1, (o + n) // 8, 2),
+                      V("lo", t, (o + n) // 8 + 3, (o + 2 * n + 16) // 8, 2), OP.min, [dep])
+
+        def hi2(c, o, n, dep):
+            return tt(V("fv", t, c, c + n // 16), V("hi", t, o + 15, o + n, 16),
+                      V("hi", t, o + n + 31, o + 2 * n + 16, 16), OP.max, [dep])
+
+        def logs(a, b, dep):
+            return act(V("lg", t, a, b), V("fv", t, a, b), AF.Ln, [dep])
+
+        def column(a, b, dep):
+            return ts(V("ofs", t, a, b), V("lg", t, a, b), T.ln0[:], -LAM, OP.subtract, OP.mult, [dep, s_ln])
+
+        def seconds(a, b, c, e, dep):
+            return act(V("tmp", t, P * e + a, P * e + b), plane(e, 0, end).indirect(V("ofs", t, c, c + (b - a) // 16)),
+                       AF.Copy, [dep] + pool_deps)
+
+        def paired(c, a, b, dep):
+            if t < R - 1:
+                return ts(V("tw", t, 1 + a, 1 + b), V("fv", t, c, c + b - a), T.nam[:, 0:1], GONE, OP.is_ge, OP.mult, [dep])
+            return ts(T.hf[:, a:b], V("fv", t, c, c + b - a), T.nam[:, 0:1], None, OP.is_lt, None, [dep])
+        k1 = lo(0, na, kt[0])
+        k2 = hi(0, na)
+        s_lo = logs(0, ca, lo2(0, 0, na, k1))
+        k1 = lo(ob, P - na, kt[1])
+        s_hi = logs(ca, 2 * ca, hi2(ca, 0, na, k2))
+        k2 = hi(ob, P - na)
+        k_lo = lo2(2 * ca, ob, P - na, k1)
+        ko = column(0, ca, s_lo)
+        k_hi = hi2(14 + ca, ob, P - na, k2)
+        kj = [column(ca, 2 * ca, s_hi)]
+        cols = [(ca, 2 * ca), (14 + ca, 28)]
+        s1 = [[None, seconds(0, na, 0, 1, ko)]]
+        s_lo = logs(2 * ca, 28, k_hi)
+        s1[0] += [seconds(0, na, 0, e, ko) for e in (2, 3)]
+        s1[0][0] = cp(V("tmp", t, 0, na), plane(0, 0, end).indirect(V("ofs", t, 0, ca)), [ko] + pool_deps)
+        paired(0, 0, ca, None)
+        k3 = paired(2 * ca, ca, 14, k_lo)
         if t < R - 1:
-            k3 = ms(V("tw", t, 0, 1), 0.0)
-        k_hi = tt(V("fv", t, 16, 30), V("hi", t, 15, P, 16), V("hi", t, P + 31, w - 16, 16), OP.max, [k_hi])
-        s_hi = act(V("lg", t, 16, 30), V("fv", t, 16, 30), AF.Ln, [k_hi])
-        if t < R - 1:
-            k3 = ts(V("tw", t, 1, 15), V("fv", t, 0, 14), T.nam[:, 0:1], GONE, OP.is_ge, OP.mult, [k_lo])
-        else:
-            k3 = ts(T.hf[:, 0:14], V("fv", t, 0, 14), T.nam[:, 0:1], None, OP.is_lt, None, [k_lo])
-        ko = ts(V("ofs", t, 0, 14), V("lg", t, 0, 14), T.ln0[:], -LAM, OP.subtract, OP.mult, [s_lo, s_ln])
-        if t < R - 1:
-            k4 = tt(V("tw", t, 16, 30), V("tw", t, 0, 14), V("tw", t, 1, 15), OP.subtract, [k3])
-        kj = ts(V("ofs", t, 14, 28), V("lg", t, 16, 30), T.ln0[:], -LAM, OP.subtract, OP.mult, [s_hi])
-        s1 = [[act(V("tmp", t, P * e + a, P * e + b), plane(e, 0, end).indirect(V("ofs", t, a // 16, b // 16)), AF.Copy,
-                   [ko] + pool_deps) for e in range(4)] for a, b in RUNS]
-        if t < R - 1:
-            k_w = tt(V("tw", t, 32, 46), T.tab[:, 0:14], V("tw", t, 1, 15), OP.add, [])
-            k_inc = tt(V("inc", u, 0, 56, 4), V("inc", u, 0, 56, 4), V("tw", t, 16, 30), OP.add, [k4, k_inc])
             hh, qh, sh = T["hh%d" % t], T["qh%d" % t], T["sh%d" % t]
-            k_bz = [ms(V("bt", u, P, 512), 0.0), ms(hh[:, 4 * P:1024], 0.0)]
-        else:
-            s_have = act(T.ocb[:, A:A + P], T.t01[:].indirect(T.hf[:, 0:14]), AF.Copy, [k3, k_01])
-            dma("y", T.occ[:], T.ocb[0:128:16, :], "do", [s_have, s_occ])
-            k = qz(T.qt[:, 0:A], T.sct[:, 0:A], T.tt[:, 0:4 * A], s_t)
-            dma("y", T.oc[:, 0:4 * A], T.qt[:, 0:A].bitcast(dt.uint8), "do", [k])
-            p_y = mm(7, T.qv[:], T.sv[:], T.qt[:, 0:A], T.sct[:, 0:A], A, [k, k_qv])
-            s_y = used(7, act(T.ysb[:, 0:A], bank(7, A), AF.Copy, [p_y]))
-            dma("y", T.y[:, 0:A], T.ysb[:, 0:A], "do", [s_y])
-            k_bz = [ms(T.tt[:, 4 * (A + P):4 * (A + 256)], 0.0)]
         pw = []
-        for h, (a, b) in enumerate(RUNS):
+        for h, (a, b) in enumerate(runs):
+            w = max(b - a, 128)
             for e in range(4):
-                k = tt(T.bb[:, 4 * a + e:4 * b:4], plane(e, 0, end).indirect(V("ofs", t, 14 + a // 16, 14 + b // 16)),
-                       V("tmp", t, P * e + a, P * e + b), OP.add, [s1[h][e], kj, k_qbb] + pool_deps)
-            k = qz(V("qbb", t, a, a + 128), V("sbb", t, a, a + 128), T.bb[:, 4 * a:4 * a + 512], [k] + k_pad)
-            pw.append([mm(4 * h + j, T.qw[:, 128 * j:128 * j + 128], T.sw[:, 128 * j:128 * j + 128],
-                          V("qbb", t, a, a + 128), V("sbb", t, a, a + 128), 128, [k, dw]) for j in range(4)])
+                k = tt(T.bb[:, 4 * a + e:4 * b:4], plane(e, 0, end).indirect(V("ofs", t, *cols[h])),
+                       V("tmp", t, P * e + a, P * e + b), OP.add, [s1[h][e], kj[h], k_qbb] + pool_deps)
+                if h + e == 0:
+                    kj.append(column(2 * ca, 28, s_lo))
+                    s1.append([seconds(na, P, 2 * ca, j, kj[1]) for j in range(4)])
+                    if t == R - 1:
+                        s_have = act(T.ocb[:, A:A + P], T.t01[:].indirect(T.hf[:, 0:14]), AF.Copy, [k3] + k_01)
+                        dma("y", T.occ[:], T.ocb[0:128:16, :], "do", [s_have, s_occ])
+            if t == R - 1 and not h:
+                k5 = qz(T.qt[:, 0:A], T.sct[:, 0:A], T.tt[:, 0:4 * A], s_t)
+                dma("y", T.oc[:, 0:4 * A], T.qt[:, 0:A].bitcast(dt.uint8), "do", [k5])
+                p_y = mm(7, T.qv[:], T.sv[:], T.qt[:, 0:A], T.sct[:, 0:A], A, [k5] + k_qv)
+                s_y = used(7, act(T.ysb[:, 0:A], bank(7, A), AF.Copy, [p_y]))
+                dma("y", T.y[:, 0:A], T.ysb[:, 0:A], "do", [s_y])
+            if h and t < R - 1:
+                k_inc = tt(V("inc", u, 0, 56, 4), V("inc", u, 0, 56, 4), V("tw", t, 16, 30), OP.add, [k4, k_inc])
+            elif t < R - 1:
+                k4 = tt(V("tw", t, 16, 30), V("tw", t, 0, 14), V("tw", t, 1, 15), OP.subtract, [k3])
+                k_w = tt(V("tw", t, 32, 46), T.tab[:, 0:14], V("tw", t, 1, 15), OP.add, [])
+            k = qz(V("qbb", t, a, a + w), V("sbb", t, a, a + w), T.bb[:, 4 * a:4 * (a + w)], [k] + k_pad)
+            pw.append([])
+            for j in range(5):
+                if h and t < R - 1 and j == MID:
+                    ka = qz(qh[:, 0:128], sh[:, 0:128], hh[:, 0:512], ev)
+                    pa = mm(0, T.qu[:], T.su[:], qh[:, 0:128], sh[:, 0:128], 128, [ka])
+                if j < 4:
+                    pw[h].append(mm(4 * h + j, T.qw[:, 128 * j:128 * j + 128], T.sw[:, 128 * j:128 * j + 128],
+                                    V("qbb", t, a, a + w), V("sbb", t, a, a + w), w, [k, dw]))
+            if t < R - 1:
+                ev = [used(4 * h + j, act(hh[:, 4 * a + j:4 * b:4], bank(4 * h + j, b - a), AF.Relu, [pw[h][j]],
+                                          scale=0.03125)) for j in range(4)]
         k_qbb = k
         if t == R - 1:
             break
-        ev = [used(j, act(hh[:, j:512:4], bank(j, 128), AF.Relu, [pw[0][j]], scale=0.03125)) for j in range(4)]
-        ka = qz(qh[:, 0:128], sh[:, 0:128], hh[:, 0:512], ev)
-        pa = mm(0, T.qu[:], T.su[:], qh[:, 0:128], sh[:, 0:128], 128, [ka])
-        for j in range(4):
-            if j % 2:
-                ev.append(used(4 + j, ts(hh[:, 512 + j:4 * P:4], bank(4 + j, P - 128), 0.0, 0.03125, OP.max, OP.mult,
-                                         [pw[1][j]])))
-            else:
-                ev.append(used(4 + j, act(hh[:, 512 + j:4 * P:4], bank(4 + j, P - 128), AF.Relu, [pw[1][j]], scale=0.03125)))
-        k_qh = qz(qh[:, 128:256], sh[:, 128:256], hh[:, 512:1024], ev + k_bz)
-        pb = mm(1, T.qu[:], T.su[:], qh[:, 128:256], sh[:, 128:256], 128, [k_qh])
         s_h = [act(plane(e, end, end + P), hh[:, e:4 * P:4], AF.Copy, ev, scale=0.5) for e in range(4)]
         mate = T.cores[rank ^ (1 << t)]
         rid, pid, _ = topo.addr(mate)
         em, ne = topo.mask(core, mate), len(topo.engines(core, mate))
-        wait("g", [k_qh])
-        g.remote_dma(T["ls%d" % t][:], sh[:, 0:P], T.sem["ac%d" % t], T.sem.sent, pid, rid, em)
-        ka = used(0, ts(V("bt", u, 0, 128), bank(0, 128), 0.0, None, OP.is_gt, None, [pa]))
+        msg, ll, lq = T["msg%d" % t], T["ll%d" % t], T["lq%d" % t]
+        al, ac = ("al%d" % t, ne), ("ac%d" % t, 3 * ne)
+        wait("g", [ka])
+        g.remote_dma(lq[:, 0:128].bitcast(dt.uint8), qh[:, 0:128].bitcast(dt.uint8), T.sem[ac[0]], T.sem.sent, pid, rid, em)
+        kl = {}
+
+        def listing(h):
+            a, b = RUNS[h][0] // 4, RUNS[h][1] // 4
+            w, x, y = b - a, 2 + 2 * h, 3 + 2 * h
+            q, s, bt = V("qb", u, 128 * h, 128 * h + 128), V("sb", u, 128 * h, 128 * h + 128), (T.bt, T.bu)[h]
+
+            def signs():
+                kl[h] = used(h, ts(bt[:, 0:4 * w], bank(h, 4 * w), 0.0, None, OP.is_gt, None, [kl[h]]))
+
+            def products():
+                k = qz(q, s, bt[:], [kl[h], g_bu])
+                kl[h] = mm(x, T.qc[:, 128:256], T.sc[:, 128:256], q, s, 128, [k] + k_qa)
+                kl[h, "b"] = mm(y, T.qc[:, 0:128], T.sc[:, 0:128], q, s, 128, [k])
+
+            def counted():
+                init = V("ii", u, a - 1, a) if h else 384.0 - L - 1
+                kl[h] = kl[h, "c"] = used(x, scan(V("ii", u, a, b), bank(x, w), V("inc", u, a, b), init, OP.add, OP.add,
+                                                  [kl[h], k_inc, kl.get((0, "c"))]))
+
+            def packed():
+                kl[h] = used(y, tt(V("vl", u, a, b), bank(y, w), V("ii", u, a, b), OP.add, [kl[h, "b"], kl[h]]))
+
+            def picked():
+                kl[h] = scan(V("sl", u, a, b), T.m01[:, 0:w], V("vl", u, a, b), 0.0, OP.mult, OP.min, [kl[h]])
+
+            def listed():
+                k = ts(msg[:, a // 4:b // 4], V("sl", u, a + 3, b, 4), PICK + AW - 127.5, 1.0 / 256, OP.add, OP.mult, [kl[h]])
+                if h:
+                    more.extend(scans_by_twos(u, 128, P - 128, msg[:, 8:14], [k], before(u, 128), mine, rest, True))
+                else:
+                    jobs.extend(scans_by_twos(u, 0, 128, msg[:, 0:8], [k], before(t, n), [k_sc, s_n1], mine))
+            return [signs, products, counted, packed, picked, listed]
+
+        def scores():
+            k = qz(qh[:, 128:256], sh[:, 128:256], hh[:, 512:1024], ev + k_pad)
+            kl[1] = mm(1, T.qu[:], T.su[:], qh[:, 128:256], sh[:, 128:256], 128, [k])
+
+        def placed():
+            kl["p"] = tt(V("pk", u, 0, 14), V("sl", u, 3, 56, 4), V("tw", t, 32, 46), OP.add, [k_w, kl[0], kl[1]])
+
+        def send():
+            wait("g", [ts(msg[:, 14:28], V("pk", u, 0, 14), 1.0 / (16 * AW), -0.504, OP.mult, OP.add, [kl["p"]])])
+            g.remote_dma(ll[:], msg[:], T.sem[al[0]], T.sem.sent, pid, rid, em)
+            g.remote_dma(lq[:, 128:P].bitcast(dt.uint8), qh[:, 128:P].bitcast(dt.uint8), T.sem[ac[0]], T.sem.sent, pid, rid, em)
+            g.remote_dma(T["ls%d" % t][:], sh[:, 0:P], T.sem[ac[0]], T.sem.sent, pid, rid, em)
         if t == 0:
-            k_ca = ts(T.ca[:], T.gro[:], fg, vp, OP.is_equal, OP.mult, [g_g])
+            other = [lambda: ts(T.twe[:, W1 + 2:W1 + 34:2], T.sg16[:], -3.0, None, OP.add, None, [g_twe]),
+                     lambda: k_twe.append(ts(T.twe[:, W1 + 34:W1 + 66:2], T.sg16[:], -1.0, 1.0, OP.mult, OP.add, [])),
+                     lambda: k_twe.append(ts(T.one[:, W0 + 2:W0 + 34:2], T.sg16[:], -1.0, None, OP.add, None, [g_one]))]
+            other += qe_jobs
         else:
-            k_qv = qz(T.qv[:], T.sv[:], T.vin[:], [dv])
-        kc = used(1, ts(V("bt", u, 128, P), bank(1, P - 128), 0.0, None, OP.is_gt, None, [pb]))
-        if t == 0:
-            k_qa = qz(T.qc[:, 128:256], T.sc[:, 128:256], T.ca[:], [k_ca])
-        k = qz(V("qb", u, 0, 128), V("sb", u, 0, 128), V("bt", u, 0, 512), [ka, kc])
-        pa = mm(2, T.qc[:, 128:256], T.sc[:, 128:256], V("qb", u, 0, 128), V("sb", u, 0, 128), 128, [k, k_qa])
-        pb = mm(3, T.qc[:, 0:128], T.sc[:, 0:128], V("qb", u, 0, 128), V("sb", u, 0, 128), 128, [k])
-        if t == 0:
-            run(qe_jobs, 2)
-        else:
-            ms(T.t01[:, 0:1], 0.0)
-            k_01 = ms(T.t01[:, 1:16], 1.0)
-        k = used(2, scan(V("ii", u, 0, 56), bank(2, 56), V("inc", u, 0, 56), 384.0 - L - 1, OP.add, OP.add, [pa, k_inc]))
-        run(qe_jobs, 1)
-        k = used(3, tt(V("vl", u, 0, 56), bank(3, 56), V("ii", u, 0, 56), OP.add, [pb, k]))
-        run(qe_jobs, 1)
-        k = scan(V("sl", u, 0, 56), T.m01[:, 0:56], V("vl", u, 0, 56), 0.0, OP.mult, OP.min, [k])
-        msg, ll = T["msg%d" % t], T["ll%d" % t]
-        k1 = ts(msg[:, 0:14], V("sl", u, 3, 56, 4), PICK + AW - 127.5, 1.0 / 256, OP.add, OP.mult, [k])
-        k2 = tt(V("pk", u, 0, 14), V("sl", u, 3, 56, 4), V("tw", t, 32, 46), OP.add, [k_w])
-        k2 = ts(msg[:, 14:28], V("pk", u, 0, 14), 1.0 / (16 * AW), -0.504, OP.mult, OP.add, [k2])
-        wait("g", [k2])
-        g.remote_dma(ll[:], msg[:], T.sem["al%d" % t], T.sem.sent, pid, rid, em)
-        g.remote_dma(T["lq%d" % t][:].bitcast(dt.uint8), qh[:, 0:P].bitcast(dt.uint8), T.sem["ac%d" % t], T.sem.sent,
-                     pid, rid, em)
-        nsent += 3 * ne
-        k_sc = scans_by_twos(u, P, msg[:, 0:14], [k1], lambda m: V("st", t, 8 * (n - 1) + m, 8 * (n - 1) + m + 1),
-                             [k_sc, s_n1])
-        al, ac = ("al%d" % t, ne), ("ac%d" % t, 2 * ne)
-        last = []
-        scans = scans_by_ones(u, P, P, ll[:, 0:14], [al], [k_sc], last)
+            other = [lambda: ms(T.t01[:, 0:1], 0.0), lambda: k_01.append(ms(T.t01[:, 1:16], 1.0)), lambda: None,
+                     lambda: k_qv.append(qz(T.qv[:], T.sv[:], T.vin[:], [dv]))]
+        mine, rest, last, jobs, more = [], [], [], [], []
+        kl[0] = pa
+        later = listing(1)
+        weave(WEAVE1, {"p": listing(0), "q": [scores] + later[:5] + [placed, later[5], send], "o": other, "j": jobs})
+        nsent += 4 * ne
+        scans, signs = scans_by_ones(u, P, P, ll[:, 0:14], [al] + k_twe, rest, last, TWOS)
         pd = [mm(4 + b, T.qe[:, 128 * b:128 * b + 128], T.se[:, 128 * b:128 * b + 128],
-                 T["lq%d" % t][:], T["ls%d" % t][:], P, [ac] + k_qe) for b in range(4)]
-        s_d = [used(4 + b, act(plane(b, end + P, end + 2 * P), bank(4 + b, P), AF.Copy, [pd[b]], scale=0.5))
-               for b in range(4)]
-        pool_deps = s_d + s_h
+                 lq[:], T["ls%d" % t][:], P, [ac] + k_qe) for b in range(4)]
+        pool_deps = list(s_h)
+
+        def unpacked():
+            pool_deps.extend(used(4 + b, act(plane(b, end + P, end + 2 * P), bank(4 + b, P), AF.Copy, [pd[b]], scale=0.5))
+                             for b in range(4))
         jobs = []
         if u == R - 1:
             fin = V("st", u, 8 * (2 * P - 1), 16 * P)
@@ -464,16 +597,17 @@ def rank_program(g, core, T, topo):
             jobs = [fin_a, fin_b, fin_c]
         kn = {}
         last.append(al)
-        a, c = number(u, 0, P, msg[:, 14:28], [k_sc, k2], [0, 4, 6, 8, 10, 12, 14], kn)
-        d, e = number(u, P, P, ll[:, 14:28], last, [0, 14], kn)
-        weave(WEAVE, {"a": a, "b": scans, "c": c, "d": d, "e": e, "f": jobs})
+        a, y, c = number(u, 0, P, lambda a, b: msg[:, 14 + a:14 + b], [(0, 128, mine), (128, P, rest)], CUTS[0], CUTS[1], kn)
+        d, z, e = number(u, P, P, lambda a, b: ll[:, 14 + a:14 + b], [(0, P, last)], CUTS[2], [0, 14], kn)
+        unpacked()
+        weave(WEAVE, {"a": a, "b": scans, "c": c, "d": d, "e": e, "f": jobs, "m": more, "s": signs, "y": y, "z": z})
         k_sc = last[-1]
         if u == R - 1:
             s_t = [act(T.tt[:, e:4 * A:4], plane(e, 0, ZE + 1).indirect(T.wo[:, 0:8]), AF.Copy,
                        [tok["w"]] + pool_deps, scale=2.0) for e in range(4)]
-            s_occ = act(T.ocb[:, 0:A], T.t01[:].indirect(T.wo[:, 8:16]), AF.Copy, [tok["f"], k_01])
+            s_occ = act(T.ocb[:, 0:A], T.t01[:].indirect(T.wo[:, 8:16]), AF.Copy, [tok["f"]] + k_01)
 
-    for h, (a, b) in enumerate(RUNS):
+    for h, (a, b) in enumerate(LAST):
         ev = []
         for j in range(4):
             m = T.hm[:, P * j + a:P * j + b]
@@ -487,8 +621,9 @@ def rank_program(g, core, T, topo):
                 ev.append(ts(o, m, 0.0, 0.03125, OP.max, OP.mult, [k]))
 
         def out(h=h, a=a, b=b, ev=ev):
-            k = qz(T.qt[:, A + a:A + a + 128], T.sct[:, A + a:A + a + 128], T.tt[:, 4 * (A + a):4 * (A + a) + 512], ev + k_bz)
-            p = mm(h, T.qv[:], T.sv[:], T.qt[:, A + a:A + a + 128], T.sct[:, A + a:A + a + 128], 128, [k])
+            w = max(b - a, 128)
+            k = qz(T.qt[:, A + a:A + a + w], T.sct[:, A + a:A + a + w], T.tt[:, 4 * (A + a):4 * (A + a + w)], ev + k_pad)
+            p = mm(h, T.qv[:], T.sv[:], T.qt[:, A + a:A + a + w], T.sct[:, A + a:A + a + w], w, [k])
             dma("y", T.oc[:, 4 * (A + a):4 * (A + b)], T.qt[:, A + a:A + b].bitcast(dt.uint8), "do", [k])
             return k, p
         if not h:
@@ -499,10 +634,10 @@ def rank_program(g, core, T, topo):
         else:
             res.append(out())
     (ka, pa), (kc, pb) = res
-    k = act(T.ysb[:, A:A + 128], bank(0, 128), AF.Copy, [pa])
-    dma("s", T.y[:, A:A + 128], T.ysb[:, A:A + 128], "do", [k])
+    k = act(T.ysb[:, A:A + na], bank(0, na), AF.Copy, [pa])
+    dma("s", T.y[:, A:A + na], T.ysb[:, A:A + na], "do", [k])
     for j in range(4):
         dma("s" if j < 2 else "y", T.osc[4 * j:4 * j + 4, :], T.sct[32 * j:32 * j + 4, 0:A + P], "do", [kc])
-    k = cp(T.ysb[:, A + 128:A + P], bank(1, P - 128), [pb])
-    dma("s", T.y[:, A + 128:A + P], T.ysb[:, A + 128:A + P], "do", [k])
+    k = cp(T.ysb[:, A + na:A + P], bank(1, P - na), [pb])
+    dma("s", T.y[:, A + na:A + P], T.ysb[:, A + na:A + P], "do", [k])
     wait("g", [(s, c) for s, c in cnt.items()] + [("sent", nsent)])

from concourse.mybir import dt, AluOpType as OP, ActivationFunctionType as AF

C, A, P, L, R = 512, 128, 224, 96, 3
NT = [C, 2 * P, 2 * P]
Q0 = [0, C, C + 2 * P]
Z0 = 1
NQ = C + 4 * P
ZE = Z0 + NQ
PW = ZE + 15
LAM, TOP = 48.0, 14.7
BIG = 2.0 ** 30
NONE = 2 ** 22
PICK = 2.0 ** 18
GONE = 2.0 ** 20
AW = 512.0
W0, W1, TW = 224, 192, 272
DUMP = P + L
RUNS = [(0, 128), (128, P)]
WEAVE0 = "ayabababababbabb" + "cdzdzdcdcdfdfdfe"
WEAVE = "mmammmmmmmmyaya" + "sasbasabsabbabbbb" + "cdfdzdzdcdfdcdfe"
CUTS0 = [[0, 16], [0, 8, 12, 16], [0, 8, 16]]
CUTS = [[0, 8, 14], [0, 6, 10, 14], [0, 8, 14]]
TWOS0, TWOS = 0, 2
MID = 2
LAST = RUNS
WEAVE1 = "opoopqoopqpopqpjqqjqjqqjqjjjjjjjjj"
H16 = "float16"
CD, U8, BF, F32, I32, U16 = "float8_e4m3fn_x4", "uint8", "bfloat16", "float32", "int32", "uint16"

SCRATCH = {}


def _sb(name, cols, dtype):
    SCRATCH[name] = ("sbuf", [128, cols], dtype)


for _n, _c, _d in [
    ("xin", 4 * C, BF), ("qx", C, CD), ("sx", C, U8), ("uin", 512, BF), ("qu", 128, CD), ("su", 128, U8),
    ("vin", 512, BF), ("qv", 128, CD), ("sv", 128, U8), ("qw", 512, CD), ("sw", 512, U8),
    ("pool", 4 * PW, BF), ("gb", C + 16, H16), ("vv", C + 32, H16),
    ("pcol", 1, I32), ("ci", 4, I32), ("cf", 4, F32), ("cx", 12, F32), ("lt", 8, F32), ("pw2", 8, F32),
    ("d64", 64, BF), ("pat", 192, BF), ("i16", 16, F32), ("gm", 16, F32), ("c4", 64, BF), ("raw", 34, F32),
    ("cb", 512, BF), ("ca", 512, BF), ("gro", 512, BF), ("qc", 256, CD), ("sc", 256, U8),
    ("eb", 516, BF), ("qe", 512, CD), ("se", 512, U8),
    ("m01", 64, BF), ("pik", 66, F32), ("bt", 512, BF), ("bu", 512, BF), ("st", 8 * NQ, BF), ("sg16", 16, BF),
    ("one", W0 + TW, BF), ("odd", W0 + TW, BF), ("twe", W1 + TW, BF), ("two", W1 + TW, BF), ("tab", 32, F32), ("smr", 544, BF), ("sm", 544, BF),
    ("cap", 544, H16), ("dmp", 34, F32), ("rin", PW, F32), ("nam", PW, BF), ("t01", 16, F32), ("ln0", 1, F32),
    ("tt", 4 * (A + 288), BF), ("qt", A + 288, CD), ("sct", A + 288, U8), ("ysb", A + P, F32), ("ocb", A + P, F32),
    ("hm", 4 * P, F32), ("wa", 8, F32), ("wl", 8, F32), ("wo", 16, U16), ("hf", 16, U16),
    ("bb", 4 * 288, BF), ("au", 64, U16),
]:
    _sb(_n, _c, _d)
WID = {"qb": (256, CD), "sb": (256, U8), "ii": (128, F32), "vl": (128, F32), "sl": (128, F32),
       "pk": (32, F32), "ee": (4 * 256, BF), "ef": (4 * 256, BF), "sig": (8 * C, BF), "zz": (C, BF), "gg": (256, BF), "inc": (64, F32),
       "ga": (C, H16), "tr": (1088, H16), "ss": (1088, H16),
       "vk": (48, F32), "de": (32, U16), "xs": (896, BF), "tx": (512, BF), "lo": (64, BF), "hi": (512, BF),
       "fv": (32, F32), "lg": (32, F32), "ofs": (28, U16), "tmp": (4 * P, BF), "qbb": (288, CD),
       "sbb": (288, U8), "tw": (48, F32)}
for _n, (_c, _d) in WID.items():
    _sb(_n, R * _c, _d)
for _t in range(2):
    for _n, _c, _d in [("hh", 1024, BF), ("qh", 256, CD), ("sh", 256, U8), ("lq", P, CD), ("ls", P, U8),
                       ("msg", 28, U16), ("ll", 28, U16)]:
        _sb("%s%d" % (_n, _t), _c, _d)
SCRATCH["pm"] = ("psum", [128, 4096], F32)

SEMAPHORES = ["cv", "cs", "cp", "cg", "du", "dxa", "dxb", "dw", "dv", "do", "sent", "ac0", "ac1", "al0", "al1"]


def rank_program(g, core, T, topo):
    rank = T.rank_of(core)
    if rank is None:
        return
    que = {"v": g.vector, "s": g.scalar, "p": g.tensor, "g": g, "y": g.sync}
    cnt = {}
    seen = {}
    users = [[] for _ in range(8)]

    def wait(q, deps):
        need = {}
        for d in deps:
            if d is not None and d[1] > need.get(d[0], 0):
                need[d[0]] = d[1]
        for s, n in need.items():
            if n > seen.get((q, s), 0):
                que[q].wait_ge(T.sem[s], n)
                seen[(q, s)] = n

    def done(ins, s, n):
        ins.then_inc(T.sem[s], n)
        cnt[s] = cnt.get(s, 0) + n
        return (s, cnt[s])

    def ts(out, in0, s1, s2, o0, o1, deps):
        wait("v", deps)
        if o1 is None:
            return done(g.vector.tensor_scalar(out, in0, s1, None, o0), "cv", 1)
        return done(g.vector.tensor_scalar(out, in0, s1, s2, o0, o1), "cv", 1)

    def tt(out, a, b, o, deps):
        wait("v", deps)
        return done(g.vector.tensor_tensor(out, a, b, o), "cv", 1)

    def cp(out, a, deps):
        wait("v", deps)
        return done(g.vector.tensor_copy(out, a), "cv", 1)

    def ms(out, c):
        return done(g.vector.memset(out, c), "cv", 1)

    def scan(out, d0, d1, init, o0, o1, deps):
        wait("v", deps)
        return done(g.vector.tensor_tensor_scan(out, d0, d1, init, o0, o1), "cv", 1)

    def trp(out, a, deps):
        wait("v", deps)
        return done(g.vector.transpose(out, a), "cv", 1)

    def qz(q, s, a, deps):
        wait("v", deps)
        return done(g.vector.quantize_mx(q, s, a), "cv", 1)

    def act(out, a, f, deps, **kw):
        wait("s", deps)
        return done(g.scalar.activation(out, a, f, **kw), "cs", 1)

    def bank(i, n):
        return T.pm[:, 512 * i:512 * i + n]

    def mm(i, q1, s1, q2, s2, n, deps):
        wait("p", deps + users[i])
        users[i] = []
        return done(g.tensor.matmul_mx(bank(i, n), q1, s1, q2, s2, True, True), "cp", 1)

    def used(i, k):
        users[i].append(k)
        return k

    def iota(out, pat, base, ch, flag=True):
        if flag:
            return done(g.iota(out, pat, base, ch, allow_small_or_imprecise_dtypes=True), "cg", 1)
        return done(g.iota(out, pat, base, ch), "cg", 1)

    def dma(q, out, a, s, deps):
        wait(q, deps)
        return done(que[q].dma_start(out, a), s, 16)

    def V(name, t, a, b, step=1):
        w = 8 * Q0[t] if name == "st" else WID[name][0] * t
        return T[name][:, w + a:w + b:step] if step != 1 else T[name][:, w + a:w + b]

    def plane(e, a, b):
        return T.pool[:, PW * e + a:PW * e + b]

    def names(t, pos, n):
        return T.nam[:, Z0 + Q0[t] + pos:Z0 + Q0[t] + pos + n]

    def run(jobs, k=99):
        last = None
        for _ in range(min(k, len(jobs))):
            last = jobs.pop(0)()
        return last

    def weave(order, lists):
        for c in order:
            run(lists[c], 1)

    du = dma("y", T.uin[:], T.u[:], "du", [])
    dxa = dma("y", T.xin[:, 0:2 * C], T.x[:, 0:2 * C], "dxa", [])
    dxb = dma("y", T.xin[:, 2 * C:4 * C], T.x[:, 2 * C:4 * C], "dxb", [])
    dma("y", T.qw[:].bitcast(dt.uint8), T.wc[:], "dw", [dxa, dxb])
    dw = dma("y", T.sw[:], T.ws[:], "dw", [])
    dv = dma("y", T.vin[:], T.v[:], "dv", [])

    g_p = iota(T.pcol[:], [[0, 1]], 0, 1, False)
    g_i = iota(T.i16[:], [[1, 16]], 0, 0)
    g_d = iota(T.d64[:], [[0, 4], [-1, 4], [1, 4]], 0, 0)
    g_r0 = iota(T.rin[:, 16:C + Z0], [[1, C + Z0 - 16]], 16, 0)
    g_c = iota(T.c4[:], [[0, 16], [1, 4]], 0, 0)
    g_r = iota(T.raw[:], [[16, 34]], DUMP, 0)
    g_sm = iota(T.smr[:], [[0, 17], [1, 2], [0, 16]], 0, 0)
    g_odd = iota(T.odd[:], [[0, W0 + TW]], 1, 0)
    k_xs = [iota(V("xs", 0, 0, 256), [[0, 256]], NONE, 0)]
    g_r1 = iota(T.rin[:, C + Z0:PW], [[1, PW - C - Z0]], C + Z0, 0)
    g_e = iota(T.eb[:], [[0, 516]], 1, 0)
    wait("g", [g_e])
    g_e = done(g.affine_select(T.eb[:], T.eb[:], [[1, 516]], OP.is_equal, 0.0, -3, -4), "cg", 1)
    g_g = iota(T.gro[:], [[1, 8], [0, 64]], 0, 0)
    iota(T.tw[:, 0:96:48], [[0, 2]], 0, 0)
    k_z = [iota(T.pool[:, 0:4 * PW:PW], [[0, 4]], 0, 0), iota(T.pool[:, ZE:4 * PW:PW], [[0, 4]], 0, 0)]
    k_pad = [iota(b[:, b.shape[1] - w:b.shape[1]], [[0, w]], 0, 0)
             for b, w in ((T.bb, 256), (T.hh0, 128), (T.hh1, 128), (T.tt, 256))]
    g_one = iota(T.one[:], [[0, W0 + TW]], 1, 0)
    g_twe = iota(T.twe[:], [[0, W1 + TW]], -1, 0)
    g_bu = iota(T.bu[:], [[0, 512]], 0, 0)
    k_xs += [iota(V("xs", t, 0, 256), [[0, 256]], NONE, 0) for t in (1, 2)]

    s_n0 = act(T.nam[:, 0:16], T.i16[:], AF.Exp, [g_i], scale=-1.0 / LAM, bias=TOP)
    g_two = ms(T.two[:], -1.0)
    ts(T.ci[:, 0:1], T.pcol[:], 15, None, OP.bitwise_and, None, [g_p])
    ts(T.ci[:, 1:2], T.pcol[:], 4, 1, OP.arith_shift_right, OP.bitwise_and, [])
    ts(T.ci[:, 2:3], T.pcol[:], 4, None, OP.arith_shift_right, None, [])
    k = ts(T.ci[:, 3:4], T.pcol[:], 2, 3, OP.arith_shift_right, OP.bitwise_and, [])
    k_bt = ms(T.bt[:, C // 2:C], 0.0)
    k_cf = cp(T.cf[:], T.ci[:], [k])
    fi, fh, fg, fq = (T.cf[:, j:j + 1] for j in range(4))
    w0, vp, w1, hb, q1 = (T.cx[:, j:j + 1] for j in range(5))

    def signs_of(i, a, b, dep):
        return used(i, ts(T.bt[:, a:b], bank(i, b - a), 0.0, None, OP.is_gt, None, [dep]))
    k = ts(T.lt[:], T.i16[:, 0:8], fi, 1.0, OP.is_lt, OP.add, [k_cf, g_i])
    k_vp = ts(vp, fi, 7.0, None, OP.is_equal, None, [])
    k_gm = ts(T.gm[:], T.i16[:], fg, None, OP.is_equal, None, [])
    k = scan(T.pw2[:], T.lt[:], T.lt[:], AW, OP.mult, OP.max, [k])
    k_l = ts(T.pat[:, 64:128], T.d64[:], 0.0, vp, OP.is_gt, OP.mult, [g_d, k_vp])
    k_16 = ts(T.sg16[:], T.i16[:], fi, 2.0, OP.not_equal, OP.mult, [])
    k = ts(w0, fi, 7.0, T.pw2[:, 7:8], OP.is_lt, OP.mult, [k])
    k_hb = ts(hb, fh, -1.0, BIG, OP.add, OP.mult, [])
    k_q = ts(q1, fi, 128 * AW, PICK - DUMP * 128 * AW, OP.mult, OP.add, [])
    k = ts(w1, vp, -128.0, w0, OP.mult, OP.add, [k])
    fills = [ms(T.gb[:, 0:2], 0.0), ms(T.vv[:, 0:16], 0.0)]
    k = ts(T.pat[:, 0:64], T.d64[:], 0.0, w1, OP.is_equal, OP.mult, [k])
    fills += [ms(T.vv[:, 16 + C // 2:32 + C // 2], 0.0), ms(T.vv[:, 16 + C:32 + C], 0.0)]
    k_pat = tt(T.pat[:, 128:192], T.pat[:, 0:64], T.pat[:, 64:128], OP.subtract, [k, k_l])
    s_n0 = act(T.nam[:, 16:C + Z0], T.rin[:, 16:C + Z0], AF.Exp, [g_r0], scale=-1.0 / LAM, bias=TOP)
    kb = [act(T.cb[:, 64 * j:64 * j + 64], T.pat[:, 128:192], AF.Copy, [k_pat, k_gm], scale=T.gm[:, j:j + 1])
          for j in range(8)]

    def sg(t, pos, n, m, w=1):
        return V("sig", t, 8 * pos + m * n, 8 * pos + (m + w) * n)

    def follow(t, pos, n, m, init, deps, slot=None):
        return scan(V("st", t, 8 * pos + m, 8 * (pos + n), 8), names(t, pos, n), sg(t, pos, n, m if slot is None else slot),
                    init(m), OP.min, OP.mult, deps)

    def scans_by_twos(t, pos, n, offs, deps, init, ideps, out, ones=None):
        def win(q):
            return T.two[:, W1 - 64 * q:W1 - 64 * q + TW].indirect(offs)

        order = [0, 1, 2, 3] if ones else [0, 3, 1, 2]
        slot = {2 * q + b: 4 * (j // 2) + 2 * b + j % 2 for j, q in enumerate(order) for b in (0, 1)}

        def ee(j, w=1):
            return V("ee", t, 4 * pos + j * n, 4 * pos + (j + w) * n)
        k = {q: act(ee(order.index(q)), win(q), AF.Copy, deps + [k_two]) for q in range(2 if ones else 3)}
        s = {m: act(sg(t, pos, n, slot[m]), T.odd[:, W0 - 32 * m:W0 - 32 * m + TW].indirect(offs), AF.Copy, deps + k_odd)
             for m in range(4 if ones else 8, 8)}

        def signs(j):
            a, b = order[j:j + 2]

            def first():
                s[2 * a] = s[2 * b] = ts(sg(t, pos, n, 2 * j, 2), ee(j, 2), -1.0, 2.0, OP.min, OP.add, [k[a], k[b]])

            def second():
                s[2 * a + 1] = s[2 * b + 1] = ts(sg(t, pos, n, 2 * j + 2, 2), ee(j, 2), -1.0, -1.0, OP.max, OP.mult, [])
            return [first, second]

        def some(ms):
            return [lambda m=m: out.append(follow(t, pos, n, m, init, [s[m]] + ideps, slot[m])) for m in ms]
        if ones:
            return signs(0) + some([0, 2, 1, 3, 4, 5, 6, 7])
        return ([lambda: k.update({3: cp(ee(1), win(3), deps + [k_two])})] + signs(0) + some([0, 6]) + signs(2)
                + some([1, 7, 2, 4, 3, 5]))

    def before(t, pos):
        return lambda m: V("st", t, 8 * (pos - 1) + m, 8 * (pos - 1) + m + 1)

    def scans_by_ones(t, pos, n, offs, deps, ideps, out, twos):
        one, two = (T.one, T.twe) if t else (T.odd, T.two)
        got = [act(V("ef", t, 256 * q, 256 * q + n), two[:, W1 - 64 * q:W1 - 64 * q + TW].indirect(offs), AF.Copy, deps)
               for q in range(twos)]
        tok = {m: act(sg(t, pos, n, m), one[:, W0 - 32 * m:W0 - 32 * m + TW].indirect(offs), AF.Copy, deps)
               for m in range(2 * twos, 8)}

        def job(m):
            return lambda: out.append(follow(t, pos, n, m, before(t, pos), [tok[m]] + ideps))

        def signs(q):
            e = V("ef", t, 256 * q, 256 * q + n)
            return [lambda: tok.update({2 * q: ts(sg(t, pos, n, 2 * q), e, -1.0, 2.0, OP.min, OP.add, [got[q]])}),
                    lambda: tok.update({2 * q + 1: ts(sg(t, pos, n, 2 * q + 1), e, -1.0, -1.0, OP.max, OP.mult, [])})]
        return [job(m) for m in range(8)], [j for q in range(twos) for j in signs(q)]

    def turn(src, tr, n, deps):
        trp(tr(0, n), src(16, 16 + n), deps)
        return trp(tr(n, 2 * n + 32), src(0, n + 32), [])

    def number(t, pos, n, offs, parts, zcuts, cuts, k):
        o, c = (544 if pos else 0), pos // 16
        d = c + n // 16
        init = V("vk", t, 40, 41) if pos else 1.0 / 16

        def own(a, b):
            return V("st", t, 8 * pos if t else 0, 8 * (pos + b)).indirect(offs(a // 16, b // 16))

        def second(a, b, deps):
            def job():
                k[pos] = tt(V("ga", t, pos + a, pos + b), own(a, b), names(t, pos + a, b - a), OP.is_gt, deps)
                if pos:
                    cp(init, T.vv[:, 15 + pos:16 + pos], [k[0]])
            return job

        def larger(a, b):
            def job():
                k["z", pos] = tt(V("zz", t, pos + a, pos + b), own(a, b), names(t, pos + a, b - a), OP.max, [])
            return job

        def back():
            k[pos] = ts(T.gb[:, pos + 1:pos + n + 1], V("ga", t, pos, pos + n), 1025.0 / 1024.0, None, OP.mult, None,
                        [k[pos]] + fills)

        def count():
            k[pos] = scan(T.vv[:, 16 + pos:16 + pos + n], T.gb[:, pos:pos + n], V("ga", t, pos, pos + n), init,
                          OP.add, OP.subtract, [k[pos]])

        def turned():
            k[pos] = turn(lambda a, b: T.vv[:, pos + a:pos + b], lambda a, b: V("tr", t, o + a, o + b), n, [k[pos]])

        def summed():
            k[pos] = scan(V("ss", t, o, o + 2 * n + 32), V("tr", t, o, o + 2 * n + 32), T.cap[:, 0:2 * n + 32], 0.0,
                          OP.add, OP.min, [k[pos]] + k_cap)

        def joined():
            k[pos] = tt(V("vk", t, c, d), V("ss", t, o + 15, o + n, 16), V("ss", t, o + n + 31, o + 2 * n + 16, 16),
                        OP.add, [k[pos]])

        def places():
            k[pos] = ts(V("de", t, c, d), V("vk", t, c, d), 1024.0, None, OP.mult, None, [k[pos]])

        def piece(a, b):
            def put():
                k["put"] = cp(V("xs", t, 16, 896).indirect(V("de", t, c + a, c + b)),
                              V("zz", t, pos + 16 * a, pos + 16 * b), [k[pos], k["z", pos], k_xs[t], k.get("put")])
            return put
        return ([second(*p) for p in parts] + [back, count, turned, summed, joined, places],
                [larger(16 * a, 16 * b) for a, b in zip(zcuts, zcuts[1:])], [piece(a, b) for a, b in zip(cuts, cuts[1:])])


    hc = C // 2
    k_cap = [ms(T.cap[:], 60000.0)]
    k_qu = qz(T.qu[:], T.su[:], T.uin[:], [du])
    k = qz(T.qx[:, 0:hc], T.sx[:, 0:hc], T.xin[:, 0:2 * C], [dxa])
    p = mm(4, T.qu[:], T.su[:], T.qx[:, 0:hc], T.sx[:, 0:hc], hc, [k, k_qu])
    k_pik = ts(T.pik[:, 1:65], T.c4[:], fq, -PICK, OP.is_equal, OP.mult, [g_c])
    k_m = ts(T.m01[:], T.c4[:], 0.0, None, OP.is_gt, None, [])
    k_qb = qz(T.qc[:, 0:128], T.sc[:, 0:128], T.cb[:], kb)
    k_p0 = ms(T.pik[:, 0:1], 0.0)
    ts(T.two[:, W1 + 3:W1 + 35:2], T.sg16[:], -3.0, None, OP.add, None, [k_16, g_two])
    k = signs_of(4, 0, hc, p)
    k_two = ts(T.two[:, W1 + 35:W1 + 67:2], T.sg16[:], -1.0, 1.0, OP.mult, OP.add, [])
    k = qz(V("qb", 0, 0, 128), V("sb", 0, 0, 128), T.bt[:], [k, k_bt])
    p = mm(6, T.qc[:, 0:128], T.sc[:, 0:128], V("qb", 0, 0, 128), V("sb", 0, 0, 128), 128, [k, k_qb])
    k = qz(T.qx[:, hc:C], T.sx[:, hc:C], T.xin[:, 2 * C:4 * C], [dxb])
    pb = mm(5, T.qu[:], T.su[:], T.qx[:, hc:C], T.sx[:, hc:C], hc, [k])
    s_sm = act(T.sm[:], T.smr[:], AF.Abs, [g_sm, k_hb], bias=hb, scale=BIG)
    s_x = []
    k = used(6, tt(V("vl", 0, 0, 64), bank(6, 64), T.pik[:, 1:65], OP.add, [p, k_pik]))
    k_tab = ts(T.tab[:], T.raw[:, 0:32], 128 * AW, q1, OP.mult, OP.add, [g_r, k_q])
    k = scan(V("sl", 0, 0, 64), T.m01[:], V("vl", 0, 0, 64), 0.0, OP.mult, OP.min, [k, k_m])
    k_du = ts(T.dmp[:], T.raw[:], fi, 1.0 / 1024, OP.add, OP.mult, [])
    k1 = ts(T.au[:, 0:16], V("sl", 0, 3, 64, 4), PICK + 456 + AW - 127.5, 1.0 / 256, OP.add, OP.mult, [k])
    k_sb = signs_of(5, hc, C, pb)
    mine, last, k_odd = [], [], []
    jobs = scans_by_twos(0, 0, hc, T.au[:, 0:16], [k1], lambda m: BIG, [s_n0], mine)
    k_cap = [tt(T.cap[:, 15:544:16], T.dmp[:], T.sm[:, 15:544:16], OP.min, k_cap + [k_du, s_sm])]
    k = qz(V("qb", 0, 128, 256), V("sb", 0, 128, 256), T.bt[:], [k_sb])
    p = mm(7, T.qc[:, 0:128], T.sc[:, 0:128], V("qb", 0, 128, 256), V("sb", 0, 128, 256), 128, [k])
    run(jobs, 1)
    k = used(7, tt(V("vl", 0, 64, 128), T.pm[:, 512 * 7 + 64:512 * 7 + 128], T.pik[:, 1:65], OP.add, [p]))
    run(jobs, 1)
    k = scan(V("sl", 0, 64, 128), T.m01[:], V("vl", 0, 64, 128), 0.0, OP.mult, OP.min, [k])
    run(jobs, 1)
    k1b = ts(T.au[:, 16:32], V("sl", 0, 67, 128, 4), PICK + 456 + AW - 127.5, 1.0 / 256, OP.add, OP.mult, [k])
    k_odd.append(ts(T.odd[:, W0 + 3:W0 + 35:2], T.sg16[:], -1.0, None, OP.add, None, [g_odd]))
    scans, signs = scans_by_ones(0, hc, hc, T.au[:, 16:32], [k1b] + k_odd, mine, last, TWOS0)
    run(jobs, 2)
    k2 = tt(V("pk", 0, 0, 32), V("sl", 0, 3, 128, 4), T.tab[:], OP.add, [k_tab])
    run(jobs, 6)
    k2 = ts(T.au[:, 32:64], V("pk", 0, 0, 32), 1.0 / (16 * AW), -0.47, OP.mult, OP.add, [k2])
    run(jobs)
    k_sc = mine[-1]
    s_n1 = act(T.nam[:, C + Z0:PW], T.rin[:, C + Z0:PW], AF.Exp, [g_r1], scale=-1.0 / LAM, bias=TOP)

    def halved_x():
        s_x.append(act(T.ln0[:], T.nam[:, 0:1], AF.Ln, []))
        s_x.extend(act(plane(e, Z0, Z0 + C), T.xin[:, e:4 * C:4], AF.Copy, [dxa, dxb], scale=0.5) for e in range(4))
    k_qe = []

    def qe_job(b):
        return lambda: k_qe.append(qz(T.qe[:, 128 * b:128 * b + 128], T.se[:, 128 * b:128 * b + 128],
                                      T.eb[:, 3 - b:515 - b], [g_e]))
    qe_jobs = [qe_job(b) for b in range(4)]
    kn = {}
    a, y, c = number(0, 0, hc, lambda a, b: T.au[:, 32 + a:32 + b], [(0, hc, [k_sc, k2])], CUTS0[0], CUTS0[1], kn)
    d, z, e = number(0, hc, hc, lambda a, b: T.au[:, 48 + a:48 + b], [(0, hc, last)], CUTS0[2], [0, 16], kn)
    k_qa = []
    jobs = [lambda: k_qa.append(ts(T.ca[:], T.gro[:], fg, vp, OP.is_equal, OP.mult, [g_g])), qe_jobs.pop(),
            lambda: k_qa.append(qz(T.qc[:, 128:256], T.sc[:, 128:256], T.ca[:], k_qa))]
    halved_x()
    weave(WEAVE0, {"a": a, "b": scans, "c": c, "d": d, "e": e, "f": jobs, "y": y, "z": z, "s": signs})
    s_ln = s_x[0]
    k_sc = last[-1]
    pool_deps = k_z + s_x
    nsent = 0
    k_qbb = None
    k_01, k_qv, k_twe = [], [], []

    for t in range(R):
        n = NT[t]
        u = t + 1
        end = Z0 + Q0[t] + n
        runs = RUNS if t < R - 1 else LAST
        na = runs[0][1]
        ca, ob = na // 16, 2 * na + 32
        if t < R - 1:
            k_inc = tt(V("inc", u, 0, 56), T.pik[:, 1:57], T.pik[:, 0:56], OP.subtract, [k_p0])
        kt = [turn(lambda c, d: V("xs", t, a + c, a + d), lambda c, d: V("tx", t, o + c, o + d), b - a, [kn["put"]])
              for (a, b), o in zip(runs, (0, ob))]

        def lo(o, n, dep):
            return scan(V("lo", t, o // 8, (o + 2 * n + 32) // 8), V("tx", t, o + 7, o + 2 * n + 32, 8),
                        T.sm[:, 23:48 + 2 * n:8], BIG, OP.min, OP.max, [dep, s_sm])

        def hi(o, n):
            return scan(V("hi", t, o, o + 2 * n + 32), V("tx", t, o, o + 2 * n + 32), T.sm[:, 0:2 * n + 32], 0.0,
                        OP.max, OP.min, [])

        def lo2(c, o, n, dep):
            return tt(V("fv", t, c, c + n // 16), V("lo", t, o // 8 + 1, (o + n) // 8, 2),
                      V("lo", t, (o + n) // 8 + 3, (o + 2 * n + 16) // 8, 2), OP.min, [dep])

        def hi2(c, o, n, dep):
            return tt(V("fv", t, c, c + n // 16), V("hi", t, o + 15, o + n, 16),
                      V("hi", t, o + n + 31, o + 2 * n + 16, 16), OP.max, [dep])

        def logs(a, b, dep):
            return act(V("lg", t, a, b), V("fv", t, a, b), AF.Ln, [dep])

        def column(a, b, dep):
            return ts(V("ofs", t, a, b), V("lg", t, a, b), T.ln0[:], -LAM, OP.subtract, OP.mult, [dep, s_ln])

        def seconds(a, b, c, e, dep):
            return act(V("tmp", t, P * e + a, P * e + b), plane(e, 0, end).indirect(V("ofs", t, c, c + (b - a) // 16)),
                       AF.Copy, [dep] + pool_deps)

        def paired(c, a, b, dep):
            if t < R - 1:
                return ts(V("tw", t, 1 + a, 1 + b), V("fv", t, c, c + b - a), T.nam[:, 0:1], GONE, OP.is_ge, OP.mult, [dep])
            return ts(T.hf[:, a:b], V("fv", t, c, c + b - a), T.nam[:, 0:1], None, OP.is_lt, None, [dep])
        k1 = lo(0, na, kt[0])
        k2 = hi(0, na)
        s_lo = logs(0, ca, lo2(0, 0, na, k1))
        k1 = lo(ob, P - na, kt[1])
        s_hi = logs(ca, 2 * ca, hi2(ca, 0, na, k2))
        k2 = hi(ob, P - na)
        k_lo = lo2(2 * ca, ob, P - na, k1)
        ko = column(0, ca, s_lo)
        k_hi = hi2(14 + ca, ob, P - na, k2)
        kj = [column(ca, 2 * ca, s_hi)]
        cols = [(ca, 2 * ca), (14 + ca, 28)]
        s1 = [[None, seconds(0, na, 0, 1, ko)]]
        s_lo = logs(2 * ca, 28, k_hi)
        s1[0] += [seconds(0, na, 0, e, ko) for e in (2, 3)]
        s1[0][0] = cp(V("tmp", t, 0, na), plane(0, 0, end).indirect(V("ofs", t, 0, ca)), [ko] + pool_deps)
        paired(0, 0, ca, None)
        k3 = paired(2 * ca, ca, 14, k_lo)
        if t < R - 1:
            hh, qh, sh = T["hh%d" % t], T["qh%d" % t], T["sh%d" % t]
        pw = []
        for h, (a, b) in enumerate(runs):
            w = max(b - a, 128)
            for e in range(4):
                k = tt(T.bb[:, 4 * a + e:4 * b:4], plane(e, 0, end).indirect(V("ofs", t, *cols[h])),
                       V("tmp", t, P * e + a, P * e + b), OP.add, [s1[h][e], kj[h], k_qbb] + pool_deps)
                if h + e == 0:
                    kj.append(column(2 * ca, 28, s_lo))
                    s1.append([seconds(na, P, 2 * ca, j, kj[1]) for j in range(4)])
                    if t == R - 1:
                        s_have = act(T.ocb[:, A:A + P], T.t01[:].indirect(T.hf[:, 0:14]), AF.Copy, [k3] + k_01)
                        dma("y", T.occ[:], T.ocb[0:128:16, :], "do", [s_have, s_occ])
            if t == R - 1 and not h:
                k5 = qz(T.qt[:, 0:A], T.sct[:, 0:A], T.tt[:, 0:4 * A], s_t)
                dma("y", T.oc[:, 0:4 * A], T.qt[:, 0:A].bitcast(dt.uint8), "do", [k5])
                p_y = mm(7, T.qv[:], T.sv[:], T.qt[:, 0:A], T.sct[:, 0:A], A, [k5] + k_qv)
                s_y = used(7, act(T.ysb[:, 0:A], bank(7, A), AF.Copy, [p_y]))
                dma("y", T.y[:, 0:A], T.ysb[:, 0:A], "do", [s_y])
            if h and t < R - 1:
                k_inc = tt(V("inc", u, 0, 56, 4), V("inc", u, 0, 56, 4), V("tw", t, 16, 30), OP.add, [k4, k_inc])
            elif t < R - 1:
                k4 = tt(V("tw", t, 16, 30), V("tw", t, 0, 14), V("tw", t, 1, 15), OP.subtract, [k3])
                k_w = tt(V("tw", t, 32, 46), T.tab[:, 0:14], V("tw", t, 1, 15), OP.add, [])
            k = qz(V("qbb", t, a, a + w), V("sbb", t, a, a + w), T.bb[:, 4 * a:4 * (a + w)], [k] + k_pad)
            pw.append([])
            for j in range(5):
                if h and t < R - 1 and j == MID:
                    ka = qz(qh[:, 0:128], sh[:, 0:128], hh[:, 0:512], ev)
                    pa = mm(0, T.qu[:], T.su[:], qh[:, 0:128], sh[:, 0:128], 128, [ka])
                if j < 4:
                    pw[h].append(mm(4 * h + j, T.qw[:, 128 * j:128 * j + 128], T.sw[:, 128 * j:128 * j + 128],
                                    V("qbb", t, a, a + w), V("sbb", t, a, a + w), w, [k, dw]))
            if t < R - 1:
                ev = [used(4 * h + j, act(hh[:, 4 * a + j:4 * b:4], bank(4 * h + j, b - a), AF.Relu, [pw[h][j]],
                                          scale=0.03125)) for j in range(4)]
        k_qbb = k
        if t == R - 1:
            break
        s_h = [act(plane(e, end, end + P), hh[:, e:4 * P:4], AF.Copy, ev, scale=0.5) for e in range(4)]
        mate = T.cores[rank ^ (1 << t)]
        rid, pid, _ = topo.addr(mate)
        em, ne = topo.mask(core, mate), len(topo.engines(core, mate))
        msg, ll, lq = T["msg%d" % t], T["ll%d" % t], T["lq%d" % t]
        al, ac = ("al%d" % t, ne), ("ac%d" % t, 3 * ne)
        wait("g", [ka])
        g.remote_dma(lq[:, 0:128].bitcast(dt.uint8), qh[:, 0:128].bitcast(dt.uint8), T.sem[ac[0]], T.sem.sent, pid, rid, em)
        kl = {}

        def listing(h):
            a, b = RUNS[h][0] // 4, RUNS[h][1] // 4
            w, x, y = b - a, 2 + 2 * h, 3 + 2 * h
            q, s, bt = V("qb", u, 128 * h, 128 * h + 128), V("sb", u, 128 * h, 128 * h + 128), (T.bt, T.bu)[h]

            def signs():
                kl[h] = used(h, ts(bt[:, 0:4 * w], bank(h, 4 * w), 0.0, None, OP.is_gt, None, [kl[h]]))

            def products():
                k = qz(q, s, bt[:], [kl[h], g_bu])
                kl[h] = mm(x, T.qc[:, 128:256], T.sc[:, 128:256], q, s, 128, [k] + k_qa)
                kl[h, "b"] = mm(y, T.qc[:, 0:128], T.sc[:, 0:128], q, s, 128, [k])

            def counted():
                init = V("ii", u, a - 1, a) if h else 384.0 - L - 1
                kl[h] = kl[h, "c"] = used(x, scan(V("ii", u, a, b), bank(x, w), V("inc", u, a, b), init, OP.add, OP.add,
                                                  [kl[h], k_inc, kl.get((0, "c"))]))

            def packed():
                kl[h] = used(y, tt(V("vl", u, a, b), bank(y, w), V("ii", u, a, b), OP.add, [kl[h, "b"], kl[h]]))

            def picked():
                kl[h] = scan(V("sl", u, a, b), T.m01[:, 0:w], V("vl", u, a, b), 0.0, OP.mult, OP.min, [kl[h]])

            def listed():
                k = ts(msg[:, a // 4:b // 4], V("sl", u, a + 3, b, 4), PICK + AW - 127.5, 1.0 / 256, OP.add, OP.mult, [kl[h]])
                if h:
                    more.extend(scans_by_twos(u, 128, P - 128, msg[:, 8:14], [k], before(u, 128), mine, rest, True))
                else:
                    jobs.extend(scans_by_twos(u, 0, 128, msg[:, 0:8], [k], before(t, n), [k_sc, s_n1], mine))
            return [signs, products, counted, packed, picked, listed]

        def scores():
            k = qz(qh[:, 128:256], sh[:, 128:256], hh[:, 512:1024], ev + k_pad)
            kl[1] = mm(1, T.qu[:], T.su[:], qh[:, 128:256], sh[:, 128:256], 128, [k])

        def placed():
            kl["p"] = tt(V("pk", u, 0, 14), V("sl", u, 3, 56, 4), V("tw", t, 32, 46), OP.add, [k_w, kl[0], kl[1]])

        def send():
            wait("g", [ts(msg[:, 14:28], V("pk", u, 0, 14), 1.0 / (16 * AW), -0.504, OP.mult, OP.add, [kl["p"]])])
            g.remote_dma(ll[:], msg[:], T.sem[al[0]], T.sem.sent, pid, rid, em)
            g.remote_dma(lq[:, 128:P].bitcast(dt.uint8), qh[:, 128:P].bitcast(dt.uint8), T.sem[ac[0]], T.sem.sent, pid, rid, em)
            g.remote_dma(T["ls%d" % t][:], sh[:, 0:P], T.sem[ac[0]], T.sem.sent, pid, rid, em)
        if t == 0:
            other = [lambda: ts(T.twe[:, W1 + 2:W1 + 34:2], T.sg16[:], -3.0, None, OP.add, None, [g_twe]),
                     lambda: k_twe.append(ts(T.twe[:, W1 + 34:W1 + 66:2], T.sg16[:], -1.0, 1.0, OP.mult, OP.add, [])),
                     lambda: k_twe.append(ts(T.one[:, W0 + 2:W0 + 34:2], T.sg16[:], -1.0, None, OP.add, None, [g_one]))]
            other += qe_jobs
        else:
            other = [lambda: ms(T.t01[:, 0:1], 0.0), lambda: k_01.append(ms(T.t01[:, 1:16], 1.0)), lambda: None,
                     lambda: k_qv.append(qz(T.qv[:], T.sv[:], T.vin[:], [dv]))]
        mine, rest, last, jobs, more = [], [], [], [], []
        kl[0] = pa
        later = listing(1)
        weave(WEAVE1, {"p": listing(0), "q": [scores] + later[:5] + [placed, later[5], send], "o": other, "j": jobs})
        nsent += 4 * ne
        scans, signs = scans_by_ones(u, P, P, ll[:, 0:14], [al] + k_twe, rest, last, TWOS)
        pd = [mm(4 + b, T.qe[:, 128 * b:128 * b + 128], T.se[:, 128 * b:128 * b + 128],
                 lq[:], T["ls%d" % t][:], P, [ac] + k_qe) for b in range(4)]
        pool_deps = list(s_h)

        def unpacked():
            pool_deps.extend(used(4 + b, act(plane(b, end + P, end + 2 * P), bank(4 + b, P), AF.Copy, [pd[b]], scale=0.5))
                             for b in range(4))
        jobs = []
        if u == R - 1:
            fin = V("st", u, 8 * (2 * P - 1), 16 * P)
            tok = {}

            def fin_a():
                k = ts(T.wa[:], fin, -1.0, T.nam[:, ZE:ZE + 1], OP.mult, OP.max, last)
                tok["l"] = act(T.wl[:], T.wa[:], AF.Ln, [k])

            def fin_b():
                tok["f"] = ts(T.wo[:, 8:16], fin, 0.0, None, OP.is_lt, None, [])

            def fin_c():
                tok["w"] = ts(T.wo[:, 0:8], T.wl[:], T.ln0[:], -LAM, OP.subtract, OP.mult, [tok["l"]])
            jobs = [fin_a, fin_b, fin_c]
        kn = {}
        last.append(al)
        a, y, c = number(u, 0, P, lambda a, b: msg[:, 14 + a:14 + b], [(0, 128, mine), (128, P, rest)], CUTS[0], CUTS[1], kn)
        d, z, e = number(u, P, P, lambda a, b: ll[:, 14 + a:14 + b], [(0, P, last)], CUTS[2], [0, 14], kn)
        unpacked()
        weave(WEAVE, {"a": a, "b": scans, "c": c, "d": d, "e": e, "f": jobs, "m": more, "s": signs, "y": y, "z": z})
        k_sc = last[-1]
        if u == R - 1:
            s_t = [act(T.tt[:, e:4 * A:4], plane(e, 0, ZE + 1).indirect(T.wo[:, 0:8]), AF.Copy,
                       [tok["w"]] + pool_deps, scale=2.0) for e in range(4)]
            s_occ = act(T.ocb[:, 0:A], T.t01[:].indirect(T.wo[:, 8:16]), AF.Copy, [tok["f"]] + k_01)

    for h, (a, b) in enumerate(LAST):
        ev = []
        for j in range(4):
            m = T.hm[:, P * j + a:P * j + b]
            o = T.tt[:, 4 * (A + a) + j:4 * (A + b):4]
            k = used(4 * h + j, tt(m, bank(4 * h + j, b - a), T.ocb[:, A + a:A + b], OP.mult, [pw[h][j], s_have]))
            if j < 3 or not h:
                ev.append(act(o, m, AF.Relu, [k], scale=0.03125))
            else:
                if h:
                    first()
                ev.append(ts(o, m, 0.0, 0.03125, OP.max, OP.mult, [k]))

        def out(h=h, a=a, b=b, ev=ev):
            w = max(b - a, 128)
            k = qz(T.qt[:, A + a:A + a + w], T.sct[:, A + a:A + a + w], T.tt[:, 4 * (A + a):4 * (A + a + w)], ev + k_pad)
            p = mm(h, T.qv[:], T.sv[:], T.qt[:, A + a:A + a + w], T.sct[:, A + a:A + a + w], w, [k])
            dma("y", T.oc[:, 4 * (A + a):4 * (A + b)], T.qt[:, A + a:A + b].bitcast(dt.uint8), "do", [k])
            return k, p
        if not h:
            res = []

            def first(out=out):
                res.append(out())
        else:
            res.append(out())
    (ka, pa), (kc, pb) = res
    k = act(T.ysb[:, A:A + na], bank(0, na), AF.Copy, [pa])
    dma("s", T.y[:, A:A + na], T.ysb[:, A:A + na], "do", [k])
    for j in range(4):
        dma("s" if j < 2 else "y", T.osc[4 * j:4 * j + 4, :], T.sct[32 * j:32 * j + 4, 0:A + P], "do", [kc])
    k = cp(T.ysb[:, A + na:A + P], bank(1, P - na), [pb])
    dma("s", T.y[:, A + na:A + P], T.ysb[:, A + na:A + P], "do", [k])
    wait("g", [(s, c) for s, c in cnt.items()] + [("sent", nsent)])
